import numpy as np, ml_dtypes
CORES = [25,29,65,69,153,157,193,197]
N = 8
import mx_ref
BF = ml_dtypes.bfloat16
def cols(t, e):
    v = np.concatenate([t.reshape(128, -1, 4), np.zeros((128, 1, 4), BF)], axis=1)
    return np.ascontiguousarray(v[:, e]).reshape(128, -1)
def cut(t, i, w=512):
    return t[:, w * i:w * i + w]
def pick(q, e):
    c = np.concatenate([q[0].reshape(128, -1, 4), np.zeros((128, 1, 4), np.uint8)], axis=1); s = np.concatenate([q[1], np.ones((16, 1), np.uint8)], axis=1)
    return (np.ascontiguousarray(c[:, e].reshape(128, -1)), np.ascontiguousarray(s[:, e]))
def join(*qs):
    return (np.concatenate([q[0] for q in qs], axis=1), np.concatenate([q[1] for q in qs], axis=1))
def put(q, e, v):
    c, s = q[0].reshape(128, -1, 4).copy(), q[1].copy(); c[:, e] = v[0].reshape(128, -1, 4); s[:, e] = v[1]
    return (c.reshape(128, -1), s)
def pk(c, s):
    return (np.ascontiguousarray(c), mx_ref.live(s))
def emit(q):
    return q[0], q[1]
def decode(q):
    o = []
    for b in range(4):
        e = np.zeros((128, 128, 4), np.float32); e[np.arange(128), np.arange(128), b] = 1
        o.append(mx_ref.matmul(mx_ref.quantize(e.reshape(128, 512).astype(BF)), q))
    return np.stack(o, axis=2).reshape(128, -1)
def f(rng, *shape):
    return mx_ref.flush((rng.standard_normal(shape, dtype=np.float32) * np.exp2(rng.integers(-2, 3, shape[:-1] + (1,)))).astype(BF))
def wide(rng, *shape, cols=0):
    v = rng.standard_normal(shape, dtype=np.float32) * np.exp2(rng.integers(-12, 13, shape)).astype(np.float32)
    if cols: v *= np.repeat(np.exp2(rng.integers(-cols, cols + 1, shape[:-2] + (1, shape[-1] // 4))) * (rng.random(shape[:-2] + (1, shape[-1] // 4)) > 0.0625), 4, axis=-1).astype(np.float32)
    return mx_ref.flush(v.astype(BF))
M, A, E, R, O = 128, 16, 32, 2, 1
def big(v):
    v = v.astype(np.float32)
    v[np.abs(v) < np.float32(2.0 ** -14)] = 0
    return v.astype(BF)
def plain(rng):
    return {"me": big(f(rng, N, 128, 4 * M)), "x": big(f(rng, N, 128, 4 * A)), "w": f(rng, N, 128, 512 * O)}
def signs(rng, n):
    h = np.ones((1, 1))
    while len(h) < n: h = np.block([[h, h], [h, -h]])
    return h[rng.permutation(n)[:128]][:, rng.permutation(n)] * rng.choice([-1.0, 1.0], n)
def tiles(v):
    return v.reshape(-1, 128, 4).transpose(1, 0, 2).reshape(128, -1)
def store(rng, m, q):
    return {"me": big(np.stack([tiles(v) for v in m.reshape(N, M, 512)])), "x": big(np.stack([tiles(v) for v in q.reshape(N, A, 512)])), "w": f(rng, N, 128, 512 * O)}
def low(rng):
    return rng.standard_normal((N * M, 512), dtype=np.float32) * np.float32(2.0 ** -6)
def rough(rng, v):
    return v * (1 + 0.0625 * rng.uniform(-1, 1, v.shape)) * np.exp2(rng.integers(0, 2, (len(v), 1)))
def places(rng, s):
    at = np.zeros(len(s), int)
    for r in range(N):
        j = np.flatnonzero(s == r)
        at[j] = r * M + rng.permutation(M)[:len(j)]
    return at
def spare(rng, r, at):
    return rng.permutation(np.setdiff1d(np.arange(r * M, r * M + M), at))
def planted(rng, at, o):
    k, i = np.unique(at, return_inverse=True)
    v, m = signs(rng, 512), low(rng)
    m[k] = rough(rng, v[:len(k)])
    m[at[o[0]]] *= 8
    q = rough(rng, v[i])
    q[o[0]] = 4 * v[i[o[0]]] + 8 * v[i[o[-1]]]
    q[o[2]] = q[o[1]]
    return store(rng, m, q)
def setup_inputs(rng):
    return plain(rng)
def setup_inputs_hot(rng):
    h = int(rng.integers(0, N))
    g = (h + int(rng.integers(1, N))) % N
    at = (h + rng.integers(1, N, 128)) % N * M + rng.integers(0, M, 128)
    o = np.flatnonzero(np.arange(128) // A != h)
    p, u = h * M + rng.permutation(M)[:7], g * M + rng.permutation(M)[:6]
    at[o] = u[rng.integers(0, 6, len(o))]
    k = np.concatenate([o[:A], rng.permutation(o[A:-1])[:len(o) // 2 - A - 1]])
    at[k] = p[rng.integers(0, 6, len(k))]
    at[o[2]] = at[o[1]]
    at[o[-1]] = p[6]
    return planted(rng, at, o)
def setup_inputs_ties(rng):
    d, b = plain(rng), int(rng.integers(2, N))
    g = np.full((N, 4), 4.0)
    g[b] = 1
    g[(b + int(rng.integers(1, N))) % N] = 16
    p = big(np.abs(f(rng, 128, 16 * N).astype(np.float32)) * np.repeat(g.reshape(-1), 4))
    k = f(rng, 128, 120).astype(np.float32)
    k[:, :96] = np.abs(k[:, :96])
    k[:, :48] = -k[:, :48]
    k[:, :16] = k[:, :16] * np.float32(2.0 ** 24)
    k = big(k)
    e = rng.permutation(np.concatenate([np.arange(30), rng.integers(12, 24, 58), rng.integers(0, 30, 40)]))
    m = []
    for r in range(N):
        own = np.concatenate([4 * r + np.arange(4), 4 * ((r + 1) % N) + np.arange(4)])
        m.append(cols(p, rng.permutation(np.concatenate([own, own, own[rng.integers(0, 8, M - 16)]]))))
    d["me"] = np.stack(m)
    d["x"] = np.stack([cols(k, e[r * A:r * A + A]) for r in range(N)])
    return d
def setup_inputs_second(rng):
    a, b = signs(rng, 256), signs(rng, 256)
    s = rng.permutation(np.arange(128) % N)
    p = places(rng, np.concatenate([s, (s + rng.integers(1, N, 128)) % N]))
    e = rng.permutation(512)
    e, g = e[:256], e[256:]
    m, q = low(rng), rng.uniform(-1, 1, (128, 512)) * 2.0 ** -6
    q[:, e] = a
    m[p[:128, None], e] = a
    m[p[:128, None], g] = 4 * b
    m[p[128:, None], g] = 16 * b
    return store(rng, m, q)
def setup_inputs_idle(rng):
    o = rng.permutation(N)
    s = o[rng.integers(2, N, 128)]
    s[rng.permutation(128)[:E]] = o[1]
    at = places(rng, s)
    j = int(np.argmin(s))
    z = np.sort(spare(rng, int(s[j]), at)[:2])
    at[j] = z[0]
    far = spare(rng, int(s.max()), at)[0]
    v, m = signs(rng, 512), low(rng)
    v = v * v[j]
    m[at] = rough(rng, v)
    m = m - np.float32(0.25)
    m[[z[0], z[1], far]] = 0
    q = rough(rng, v)
    q[j] = 2 * q[j]
    d = store(rng, m * np.float32(2.0 ** 27), q * 2.0 ** 27)
    c = 4 * int(z[0] % M)
    d["me"][int(s[j]), :, c:c + 4] = BF(-0.0)
    return d
def setup_inputs_spread(rng):
    return {**plain(rng), "me": big(wide(rng, N, 128, 4 * M, cols=3)), "x": big(wide(rng, N, 128, 4 * A, cols=3))}
def check_inputs(d):
    b = []
    for k, least in (("me", 2.0 ** -14), ("x", 2.0 ** -14), ("w", 2.0 ** -30)):
        v = np.abs(d[k].astype(np.float32))
        if not (np.isfinite(v).all() and ((v == 0) | (v >= least) & (v <= 2.0 ** 30)).all()): b.append("a value of " + k)
    return b
def reference(me, x, w):
    mem = [mx_ref.quantize(np.ascontiguousarray(me[r])) for r in range(N)]
    q = join(*[mx_ref.quantize(np.ascontiguousarray(x[r])) for r in range(N)])
    wi = np.zeros((N, R, 128), np.float32)
    for t in range(R):
        s = np.concatenate([mx_ref.matmul(q, mem[r]) for r in range(N)], axis=1) + np.float32(0)
        win = np.argmax(s, axis=1)
        answered = np.zeros(128, bool)
        for r in range(N): answered[np.flatnonzero(win // M == r)[:E]] = True
        wi[:, t] = np.where(answered, win, -1 - win)
        half = decode(pick(join(*mem), win)) * np.float32(0.5)
        new = mx_ref.quantize((half + decode(q) * np.float32(0.5)).astype(BF))
        a = np.flatnonzero(answered)
        q = put(q, a, pick(new, a))
        for r in range(N):
            j = a[win[a] // M == r]
            if j.size:
                c, i = np.unique(win[j] - r * M, return_index=True)
                mem[r] = put(mem[r], c, pick(new, j[i]))
    oc, osc, y = np.zeros((N, 128, 4 * M), np.uint8), np.zeros((N, 16, M), np.uint8), np.zeros((N, 128, 128 * O), np.float32)
    for r in range(N):
        oc[r], osc[r] = emit(mem[r])
        for o in range(O): y[r, :, 128 * o:128 * o + 128] = mx_ref.matmul(mx_ref.quantize(np.ascontiguousarray(cut(w[r], o))), q)
    return {"oc": oc, "osc": osc, "wi": wi, "y": y}

@@ -1,0 +1,564 @@
+from concourse.bass import DstId, RemoteDMATransfer
+from concourse.mybir import dt, AluOpType, AxisListType, ActivationFunctionType
+
+F8 = "float8_e4m3fn_x4"
+SCRATCH = {"ps": ("psum", [128, 4096], "float32")}
+for _n, _w in (("xq", 128), ("wq", 128), ("rx", 32), ("rm", 128), ("ld0", 384), ("ld1", 384), ("qf", 128), ("mc0", 416),
+               ("mc1", 416), ("fm", 128), ("mp0", 128), ("mp1", 128), ("wc", 896), ("ec", 512), ("hac", 128), ("hfc", 128),
+               ("hcc", 136), ("hlc", 128), ("hmc", 128)):
+    SCRATCH[_n] = ("sbuf", [128, _w], F8)
+    SCRATCH[_n + "s"] = ("sbuf", [128, _w], "uint8")
+for _n, _w in (("xt", 512), ("mt", 512), ("wt", 512), ("ha", 512), ("hf", 512), ("hc", 520), ("hl", 512), ("hm", 512), ("ht", 520),
+               ("wtile", 3584), ("et", 2048), ("zz", 512), ("wina", 512), ("d1", 512), ("d2", 512), ("winc", 256), ("tc1", 256),
+               ("tc2", 256), ("tc3", 256), ("tri", 128), ("m1", 96), ("hold", 96), ("jm", 128), ("jt", 512), ("jw", 96),
+               ("idn", 128), ("jk", 5120), ("fra", 128), ("clo", 128), ("chi", 128), ("le", 128), ("eqt", 128), ("tg", 128),
+               ("ep", 256), ("co", 256)):
+    SCRATCH[_n] = ("sbuf", [128, _w], "bfloat16")
+for _n, _w in (("jf", 128), ("b8", 8), ("pf", 4), ("rmk", 8), ("dg", 8), ("kb", 8), ("cc", 8), ("vd", 8), ("wd", 8), ("lm0", 16),
+               ("lm1", 16), ("nl", 16), ("cm", 256), ("aa", 4), ("lw", 2), ("vv", 2), ("an", 2), ("w1", 128), ("w2", 128),
+               ("mx", 1), ("eq", 8), ("sc", 8), ("acc", 4), ("acv", 1), ("pv", 8), ("triv", 128), ("kk", 4),
+               ("ta", 2), ("jg", 2), ("jd", 2), ("l3", 2), ("un", 2), ("nm", 2), ("wv", 8), ("oh", 16), ("og", 16), ("wo", 2),
+               ("ysb", 128)):
+    SCRATCH[_n] = ("sbuf", [128, _w], "float32")
+for _n, _w in (("ox", 2), ("oaw", 8), ("oc8", 8), ("oslot", 4), ("o2", 8), ("o3", 16), ("ol", 24), ("om", 8)):
+    SCRATCH[_n] = ("sbuf", [128, _w], "uint16")
+for _n, _w in (("pint", 4), ("bi", 2)):
+    SCRATCH[_n] = ("sbuf", [128, _w], "int32")
+SEMAPHORES = ["V", "S", "P", "G", "ls", "xa", "ma", "mr", "ms", "m0", "m1", "nn", "c0", "c1",
+              "dx", "dm", "dw", "t0", "t1", "t2", "t3", "t4", "u0", "u1", "u2", "u3", "u4", "u5", "u6", "u7"]
+A = 16
+E = 32
+QO = 256
+WAKE = 0.2
+DMA, CALL = 1.8, 0.5
+HOP = {"xa": 6.0, "ma": 7.0, "m0": 1.6, "m1": 1.6, "nn": 1.6, "c0": 2.4, "c1": 2.4}
+
+
+def plan(T, topo):
+    cores = T.cores
+    n = len(cores)
+    near = [[q for q in range(n) if q == r or topo.may_write(cores[r], cores[q])] for r in range(n)]
+    far = [[q for q in range(n) if q not in near[r]] for r in range(n)]
+    chip = [[q for q in range(n) if cores[q] in topo.cores_of(cores[r])] for r in range(n)]
+    partner = [[q for q in far[r] if topo.host(cores[q]) == topo.host(cores[r]) and topo.die(cores[q]) == topo.die(cores[r])][0]
+               for r in range(n)]
+    port = [[c for c in topo.cores_of(cores[r]) if c not in cores and topo.die(c) == topo.die(cores[r])
+             and topo.may_write(c, cores[far[r][0]])] for r in range(n)]
+    xrel = [(port[chip[r][0]][0], port[chip[r][1]][0]) for r in range(n)]
+    mrel = [(port[r][1], port[r][0]) for r in range(n)]
+    return near, far, chip, partner, xrel, mrel
+
+
+def bits(engines):
+    return sum(1 << e for e in engines)
+
+
+def make_send(g, core, T, topo, count):
+    def send(sem, parts):
+        tr = []
+        for src, dst, eng in parts:
+            ids = []
+            for c, _ in dst:
+                rid, pid = topo.addr(c, core)
+                ids.append(DstId(rid=rid, pnc=pid))
+            tr.append(RemoteDMATransfer(dst_ids=ids, dma_engine_mask=bits(eng), remote_sem=T.sem[sem],
+                                        srcs=[src], dsts=[d for _, d in dst], alu_op=0))
+            count[0] += len(eng)
+        g.remote_dma_fused(tr, local_sem=T.sem.ls)
+    return send
+
+
+def relay(g, core, T, topo, pl):
+    near, far, chip, partner, xrel, mrel = pl
+    cores = T.cores
+    n = [0]
+    send = make_send(g, core, T, topo, n)
+    here = [r for r in range(len(cores)) if core in topo.cores_of(cores[r])]
+    for r in here[:1]:
+        off = topo.engines(core, cores[far[r][0]])
+        on = [e for e in topo.engines(core, cores[r]) if e not in off]
+        if core in xrel[r]:
+            g.wait_ge(T.sem.xa, len(on) * len(here))
+            a, b = QO + A * r, QO + A * r + A * len(here)
+            if core == xrel[r][0]:
+                send("xa", [(T.rx[:].bitcast(dt.uint8), [(cores[q], T.ld0[:, a:b].bitcast(dt.uint8)) for q in far[r]], off)])
+            else:
+                send("xa", [(T.rxs[:], [(cores[q], T.ld0s[:, a:b]) for q in far[r]], off)])
+    for r in here:
+        p = partner[r]
+        h = 128 if r > p else 0
+        off = topo.engines(core, cores[p])
+        on = [e for e in topo.engines(core, cores[r]) if e not in off]
+        if core == mrel[r][0]:
+            g.wait_ge(T.sem.mr, len(on))
+            send("ma", [(T.rm[:].bitcast(dt.uint8), [(cores[p], T.mc0[:, h:h + 128].bitcast(dt.uint8))], off)])
+        if core == mrel[r][1]:
+            g.wait_ge(T.sem.ms, len(on))
+            send("ma", [(T.rms[:], [(cores[p], T.mc0s[:, h:h + 128])], off)])
+    if n[0]:
+        g.wait_ge(T.sem.ls, n[0])
+
+
+def conflicts(q, r, w, wr, rd, acc, strict):
+    d = []
+    for k in r:
+        d += wr.get(k, [])
+        if k[0] == "#":
+            d += [e for e in rd.get(k, []) if e[2] != q]
+    for k in w:
+        d += [e for e in wr.get(k, []) if strict or not (acc and e[2] == q)]
+        d += [e for e in rd.get(k, []) if strict or e[2] != q]
+    return d
+
+
+def note(e, r, w, wr, rd):
+    for k in w:
+        wr[k], rd[k] = [e], []
+    for k in r:
+        rd.setdefault(k, []).append(e)
+
+
+def in_order(ops):
+    n = len(ops)
+    wr, rd, pred = {}, {}, []
+    last = {}
+    for i, o in enumerate(ops):
+        p = {e[0] for e in conflicts(o["q"], o["r"], o["w"], wr, rd, False, True)}
+        p.update(last[s] for s in o["after"])
+        if o["tag"]:
+            last[o["tag"]] = i
+        pred.append(p)
+        note((i, 0, o["q"]), o["r"], o["w"], wr, rd)
+    prio = [o["dur"] for o in ops]
+    for i in range(n - 1, -1, -1):
+        for p in pred[i]:
+            prio[p] = max(prio[p], ops[p]["dur"] + WAKE + prio[i])
+    free, done, out = {}, {}, []
+    succ = [[] for _ in range(n)]
+    wait = [len(p) for p in pred]
+    for i in range(n):
+        for p in pred[i]:
+            succ[p].append(i)
+    ready = {i for i in range(n) if wait[i] == 0}
+    while ready:
+        best = None
+        byq = {}
+        for i in sorted(ready):
+            byq.setdefault(ops[i]["q"], []).append(i)
+        for q, c in byq.items():
+            st = {i: max([free.get(q, 0.0)] + [done[p] + WAKE for p in pred[i]]) for i in c}
+            b = min(c, key=lambda i: (st[i], -prio[i], i))
+            better = [i for i in c if prio[i] > prio[b] and st[i] < st[b] + ops[b]["hold"] - 0.03]
+            if better:
+                b = max(better, key=lambda i: (prio[i], -i))
+            if best is None or (st[b], b) < best:
+                best = (st[b], b)
+        s, i = best
+        ready.discard(i)
+        free[ops[i]["q"]] = s + ops[i]["hold"]
+        done[i] = s + ops[i]["dur"]
+        out.append(ops[i])
+        for j in succ[i]:
+            wait[j] -= 1
+            if wait[j] == 0:
+                ready.add(j)
+    assert len(out) == n
+    return out
+
+
+def rank_program(g, core, T, topo):
+    pl = plan(T, topo)
+    near, far, chip, partner, xrel, mrel = pl
+    cores = T.cores
+    N = len(cores)
+    rank = T.rank_of(core)
+    if rank is None:
+        relay(g, core, T, topo, pl)
+        return
+    op, X, AF = AluOpType, AxisListType.X, ActivationFunctionType
+    V, S, P = g.vector, g.scalar, g.tensor
+    queue = {"V": g.vector, "S": g.scalar, "P": g.tensor, "G": g, "Y": g.sync}
+    ops = []
+    ls = [0]
+    fused = make_send(g, core, T, topo, ls)
+
+    def add(q, r, w, call, sem, inc, dur, hold=None, acc=False, after=(), tag=None):
+        ops.append({"q": q, "r": r.split(), "w": w.split(), "call": call, "sem": sem, "inc": inc, "dur": dur,
+                    "hold": dur if hold is None else hold, "acc": acc, "after": after, "tag": tag})
+
+    def do(q, r, w, call, dur, acc=False):
+        add(q, r, w, call, q, 1, dur, acc=acc)
+
+    def ew(n):
+        return max(64, n) * 0.00083
+
+    def dma(q, sem, r, w, o, i):
+        add(q, r, w, lambda: queue[q].dma_start(o, i), sem, 16, DMA, 0.06)
+
+    def send(sem, r, parts, after=(), tag=None):
+        add("G", r, "", lambda: fused(sem, parts), None, 0, CALL, after=after, tag=tag or sem)
+
+    def arrive(sem, n, w, after=None):
+        add("far " + sem, "", w, None, sem, n, HOP[sem], after=(after or sem,))
+
+    def ts(r, w, out, in0, s1, s2, o0, o1=None, n=8):
+        if o1 is None:
+            do("V", r, w, lambda: V.tensor_scalar(out, in0, s1, s2, o0), ew(n))
+        else:
+            do("V", r, w, lambda: V.tensor_scalar(out, in0, s1, s2, o0, o1), ew(n))
+
+    def tt(r, w, out, in0, in1, o, n=8):
+        do("V", r, w, lambda: V.tensor_tensor(out, in0, in1, o), ew(n))
+
+    def scan(r, w, out, d0, d1, init, o0, o1, n=8):
+        do("V", r, w, lambda: V.tensor_tensor_scan(out, d0, d1, init, o0, o1), ew(n))
+
+    def red(r, w, out, in_, o, n=8):
+        do("V", r, w, lambda: V.tensor_reduce(out, in_, X, o), ew(n))
+
+    def cp(r, w, out, in_, n=8):
+        do("V", r, w, lambda: V.tensor_copy(out, in_), ew(n))
+
+    def gather(r, w, out, win, off, n):
+        do("V", r, w, lambda: V.tensor_copy(out, win.indirect(off)), 0.05 + n * 0.00125)
+
+    def act(r, w, out, in_, f, bias=0.0, scale=1.0, accum=None, n=128):
+        do("S", r, w, lambda: S.activation(out, in_, f, bias=bias, scale=scale, accum_out=accum), ew(n) + 0.02)
+
+    junk = [0]
+
+    def count(r, w, in_, f, bias, scale, accum, n=128):
+        j = junk[0] % 20
+        junk[0] += 1
+        act(r, "%s jk%d" % (w, j), T.jk[:, 256 * j:256 * j + n], in_, f, bias, scale, accum, n)
+
+    def quant(r, w, c, s, in_, n=128):
+        do("V", r, w, lambda: V.quantize_mx(c, s, in_), 0.012 + 0.00088 * n)
+
+    def fill(w, ap, c, n=8):
+        do("V", "", w, lambda: V.memset(ap, c), ew(n))
+
+    def pick(out, outs, win, wins, off, r, rs, w, ws, ro, n):
+        do("V", r + " " + ro, w, lambda: V.tensor_copy(out.bitcast(dt.uint32), win.bitcast(dt.uint32).indirect(off)), 0.05 + n * 0.00125)
+        do("S", rs + " " + ro, ws, lambda: S.activation(outs, wins.indirect(off), AF.Copy), 0.07 + n * 0.00125)
+
+    def bank(k, n=128):
+        return T.ps[:, 512 * k:512 * k + n]
+
+    def mm(k, n, lc, lsc, rc, rsc, r, start=True, stop=True):
+        do("P", r, "#%d" % k, lambda: P.matmul_mx(bank(k, n), lc, lsc, rc, rsc, start, stop), (n + 16) * 0.0008, acc=not start)
+
+    grp = near[rank]
+    mates = [q for q in grp if q != rank]
+    on_mates = [q for q in mates if q in chip[rank]]
+    off_mates = [q for q in mates if q not in chip[rank]]
+    eoff = topo.engines(core, cores[off_mates[0]])
+    eon = [e for e in topo.engines(core, cores[on_mates[0]]) if e not in eoff]
+    hosted = {q: sorted((q, partner[q])) for q in grp}
+    h = grp.index(rank)
+    lo, hi = hosted[rank]
+    own = 0 if rank == lo else 1
+    order = [s for q in grp for s in hosted[q]]
+    weight = [2.0 ** (N - 1 - s) for s in order]
+    foff = len(eoff)
+    from_mates = len(off_mates) * foff + len(on_mates) * len(eon)
+
+    def spread(sem, r, src, dst):
+        send(sem, r, [(src, [(cores[q], dst) for q in off_mates], eoff), (src, [(cores[q], dst) for q in on_mates], eon)])
+
+    def iota(w, ap, pat, n, base=0, mul=0, flag=True):
+        if flag:
+            do("G", "", w, lambda: g.iota(ap, pat, base, mul, allow_small_or_imprecise_dtypes=True), 0.13 + 0.00166 * n)
+        else:
+            do("G", "", w, lambda: g.iota(ap, pat, base, mul), 0.13 + 0.00166 * n)
+        if n > 128:
+            ops[-1]["after"] = ("last",)
+
+    dma("Y", "dx", "", "xt", T.xt[:, 0:64], T.x[:, :])
+    dma("S", "dm", "", "mt", T.mt[:, :], T.me[:, :])
+    dma("Y", "dw", "", "wt", T.wt[:, :], T.w[:, :])
+    fill("xz", T.xt[:, 64:512], 0.0, 448)
+    quant("xt xz", "xq xqs", T.xq[:, 0:128], T.xqs[:, 0:128], T.xt[:, :])
+    mo = 128 * own
+    quant("mt", "mcown0 mcown0s", T.mc0[:, mo:mo + 128], T.mc0s[:, mo:mo + 128], T.mt[:, :])
+    qa = QO + A * rank
+    ra = A * chip[rank].index(rank)
+    xs, xd = T.xq[:, 0:A].bitcast(dt.uint8), T.ld0[:, qa:qa + A].bitcast(dt.uint8)
+    ys, yd = T.xqs[:, 0:A], T.ld0s[:, qa:qa + A]
+    send("xa", "xq", [(xs, [(xrel[rank][0], T.rx[:, ra:ra + A].bitcast(dt.uint8))] + [(cores[q], xd) for q in on_mates], eon)],
+         tag="s0")
+    send("xa", "xqs", [(ys, [(xrel[rank][1], T.rxs[:, ra:ra + A])] + [(cores[q], yd) for q in on_mates], eon)],
+         after=("s0",), tag="s1")
+    send("mr", "mcown0", [(T.mc0[:, mo:mo + 128].bitcast(dt.uint8), [(mrel[rank][0], T.rm[:].bitcast(dt.uint8))], eon)],
+         after=("s1",), tag="s2")
+    send("ms", "mcown0s", [(T.mc0s[:, mo:mo + 128], [(mrel[rank][1], T.rms[:])], eon)], after=("s2",), tag="s3")
+    send("xa", "xq", [(xs, [(cores[q], xd) for q in off_mates], eoff)], after=("s3",), tag="s4")
+    send("xa", "xqs", [(ys, [(cores[q], yd) for q in off_mates], eoff)], after=("s4",), tag="last")
+    arrive("xa", 2 * (from_mates + foff * (len(far[rank]) // len(chip[rank]))), "qfar0 qfar0s", "s1")
+    arrive("ma", 2 * foff, "mcfar0 mcfar0s", "s3")
+    iota("pint0", T.pint[:, 0:1], [[0, 1]], 1, 0, 1, False)
+    iota("b8", T.b8[:, :], [[1, 8]], 8)
+    iota("jf", T.jf[:, :], [[1, 128]], 128)
+    iota("jm", T.jm[:, :], [[0, 8], [1, 16]], 128)
+    iota("jw", T.jw[:, :], [[0, 24], [1, 4]], 96)
+    iota("jt", T.jt[:, :], [[0, 32], [-1, 4], [1, 4]], 512)
+    iota("wina", T.wina[:, :], [[0, 32], [1, 16]], 512)
+    iota("d1", T.d1[:, :], [[0, 2], [16, 16], [0, 16]], 512)
+    iota("d2", T.d2[:, :], [[256, 2], [0, 256]], 512)
+    fill("zz", T.zz[:, :], 0.0, 256)
+    ts("pint0", "p16i", T.pint[:, 1:2], T.pint[:, 0:1], 15, None, op.bitwise_and)
+    ts("pint0", "g16i", T.pint[:, 2:3], T.pint[:, 0:1], 4, None, op.logical_shift_right)
+    cp("pint0", "pf0", T.pf[:, 0:1], T.pint[:, 0:1])
+    ts("p16i", "p4i", T.pint[:, 3:4], T.pint[:, 1:2], 2, None, op.logical_shift_right)
+    cp("p16i", "p16", T.pf[:, 1:2], T.pint[:, 1:2])
+    cp("g16i", "g16", T.pf[:, 2:3], T.pint[:, 2:3])
+    cp("p4i", "p4", T.pf[:, 3:4], T.pint[:, 3:4])
+    cp("p16i", "ox", T.ox[:, 0:1], T.pint[:, 1:2])
+    pick(T.ld0[:, qa:qa + A], T.ld0s[:, qa:qa + A], T.xq[:, 0:128], T.xqs[:, 0:128], T.ox[:, 0:1],
+         "xq", "xqs", "qown0", "qown0s", "ox", 16)
+    pf, p16, g16, p4 = T.pf[:, 0:1], T.pf[:, 1:2], T.pf[:, 2:3], T.pf[:, 3:4]
+    for k in range(4):
+        ts("p16", "rm%d" % k, T.rmk[:, k:k + 1], p16, float(k), None, op.is_equal)
+    ts("p16", "rm4", T.rmk[:, 4:5], p16, 2.0, None, op.is_lt)
+    ts("p16", "rm5", T.rmk[:, 5:6], p16, 3.0, None, op.is_lt)
+    tt("rm2 rm3", "rm6", T.rmk[:, 6:7], T.rmk[:, 2:3], T.rmk[:, 3:4], op.add)
+    for t in range(2):
+        fill("lmz%d" % t, T["lm%d" % t][:, 4 * h:4 * h + 4], 0.0)
+    fill("nlz", T.nl[:, 4 * h:4 * h + 4], 0.0)
+    for i, k in ((1, 0), (2, 1), (3, 4), (4, 6)):
+        act("zz rm%d" % k, "wt%d" % i, T.wtile[:, 512 * i:512 * i + 512], T.zz[:, :], AF.Identity, bias=T.rmk[:, k:k + 1], n=512)
+    for nm, a, b in (("wt5", 2560, 3072), ("wt6", 3072, 3584)):
+        act("zz", nm, T.wtile[:, a:b], T.zz[:, 0:b - a], AF.Copy, n=512)
+    for nm in ("ha", "hf", "hc", "hl", "ht", "hm"):
+        act("zz", nm + "z", T[nm][:, 0:512], T.zz[:, 0:512], AF.Copy, n=512)
+    act("zz", "htz1", T.ht[:, 512:520], T.zz[:, 0:8], AF.Copy, n=8)
+    ts("b8 g16", "dg", T.dg[:, :], T.b8[:, :], g16, None, op.is_equal)
+    ts("jw p4", "m1", T.m1[:, :], T.jw[:, :], p4, None, op.is_equal)
+    ts("jw", "hold", T.hold[:, :], T.jw[:, :], 0.0, None, op.is_gt)
+    ts("jf pf0", "idn", T.idn[:, :], T.jf[:, :], pf, None, op.is_equal, n=128)
+    fill("et", T.et[:, :], 0.0, 1024)
+    for b in range(4):
+        ts("idn et", "et%d" % b, T.et[:, 512 * b + b:512 * b + 512:4], T.idn[:, :], 0.5, None, op.mult)
+    quant("et et0 et1 et2 et3", "ec ecs", T.ec[:, :], T.ecs[:, :], T.et[:, :], 512)
+    ts("jf pf0", "tri", T.tri[:, :], T.jf[:, :], pf, None, op.is_lt, n=128)
+    for k in range(4):
+        ts("p16", "kb%d" % k, T.kb[:, k:k + 1], p16, 16.0 * (k % 2) + 0.5, None, op.add)
+    fill("kb4", T.kb[:, 4:5], E + 0.5)
+    ts("pf0", "old", T.kb[:, 5:6], pf, float(QO), None, op.add)
+    ts("pf0", "nold", T.kb[:, 6:7], pf, -1.0, -float(QO), op.mult, op.add)
+    for e in range(2):
+        ts("pf0", "cp%d" % e, T.cc[:, e:e + 1], pf, 128.0 * e + 1, None, op.add)
+        ts("pf0", "cl%d" % e, T.cc[:, 2 + e:3 + e], pf, 128.0 * e, None, op.add)
+        ts("pf0", "cd%d" % e, T.cc[:, 4 + e:5 + e], pf, -1.0, 320.0 - 128.0 * e, op.mult, op.add)
+    for i, (nm, val) in enumerate((("winc", lambda s: float(s == lo)), ("tc1", lambda s: float(s == hi)),
+                                   ("tc2", lambda s: 256.0 * (N - s)), ("tc3", lambda s: 32.0 * order.index(s)))):
+        fill(nm + "z", T[nm][:, 0:256], 0.0, 128)
+        for s in range(N):
+            if val(s):
+                do("V", nm + "z", nm + "_%d" % s,
+                   lambda nm=nm, s=s, val=val: V.memset(T[nm][:, 2 ** (N - 1 - s):2 ** (N - s)], val(s)), ew(8))
+    keys = lambda nm: " ".join([nm + "z"] + [nm + "_%d" % s for s in range(N)])
+    for i in range(N):
+        fill("vd%d" % i, T.vd[:, i:i + 1], 256.0 * (N - order[i]) + 32.0 * i)
+        fill("wd%d" % i, T.wd[:, i:i + 1], weight[i - 1] / weight[i] if i else 1.0)
+    VD, WD = " ".join("vd%d" % i for i in range(N)), " ".join("wd%d" % i for i in range(N))
+    ts("jt rm5", "wt0", T.wtile[:, 0:512], T.jt[:, :], 0.0, T.rmk[:, 5:6], op.is_equal, op.mult, n=256)
+    ts("jm p16 wt5", "wt5a", T.wtile[:, 2560:3072:4], T.jm[:, :], p16, 16.0, op.is_equal, op.mult)
+    ts("jm p16 wt5", "wt5b", T.wtile[:, 2561:3072:4], T.jm[:, :], p16, None, op.is_equal)
+    ts("zz wt6", "wt6a", T.wtile[:, 3072:3584:4], T.zz[:, 0:128], 16.0, None, op.add)
+    ts("zz wt6", "wt6b", T.wtile[:, 3073:3584:4], T.zz[:, 0:128], 1.0, None, op.add)
+    quant("wt0 wt1 wt2 wt3", "wc wcs", T.wc[:, 0:512], T.wcs[:, 0:512], T.wtile[:, 0:2048], 512)
+    quant("wt4 wt5 wt6 wt5a wt5b wt6a wt6b", "wc4 wcs4", T.wc[:, 512:896], T.wcs[:, 512:896], T.wtile[:, 2048:3584], 384)
+    cp("xt", "hcx", T.hc[:, 512:520], T.xt[:, 0:8])
+    cp("xt hlz", "hlx", T.hl[:, 504:512], T.xt[:, 0:8])
+    cp("xt hmz", "hmx", T.hm[:, 504:512], T.xt[:, 0:8])
+    quant("wt", "wq wqs", T.wq[:, :], T.wqs[:, :], T.wt[:, :])
+    dma("Y", "t0", "d1", "wina", T.wina[1:128:16, :], T.d1[1:128:16, :])
+    dma("Y", "t1", "d2", "wina", T.wina[2:128:16, :], T.d2[2:128:16, :])
+    for k in (1, 2, 3):
+        dma("Y", "t%d" % (k + 1), keys("tc%d" % k) + " " + keys("winc"), "wincr%d" % k,
+            T.winc[k:128:16, :], T["tc%d" % k][k:128:16, :])
+    WINC = keys("winc") + " wincr1 wincr2 wincr3"
+
+    def W(i):
+        return T.wc[:, 128 * i:128 * i + 128], T.wcs[:, 128 * i:128 * i + 128]
+
+    def both(nm):
+        return "%s %ss" % (nm, nm)
+
+    def wrapped(k, z, n, out, w, hk, hcod, hsc, h_, r):
+        quant("%s %sz %sx" % (r, hk, hk), both(hk + "c"), hcod[:, :], hsc[:, :], h_[:, :])
+        mm(k, 128, *W(0), hcod[:, :], hsc[:, :], "wc wcs " + both(hk + "c"))
+        scan("#%d m1" % k, "w1" + hk, T.w1[:, z:z + n], bank(k, n), T.m1[:, 0:n], 0.0, op.add, op.mult, n=n)
+        scan("w1%s hold" % hk, "w2" + hk, T.w2[:, z:z + n], T.hold[:, 0:n], T.w1[:, z:z + n], 0.0, op.mult, op.add, n=n)
+        cp("w2" + hk, w, out, T.w2[:, z + 3:z + n:4])
+
+    def one_round(t):
+        ld, lds = T["ld%d" % t], T["ld%ds" % t]
+        mc, mcs = T["mc%d" % t], T["mc%ds" % t]
+        mp, mps = T["mp%d" % t], T["mp%ds" % t]
+        lm = T["lm%d" % t]
+        q, qs = ld[:, QO:QO + 128], lds[:, QO:QO + 128]
+        Q = "qown%d qown%ds qfar%d qfar%ds" % (t, t, t, t)
+        MEM = "mcown%d mcfar%d" % (t, t)
+        MEMS = "mcown%ds mcfar%ds" % (t, t)
+        mm(0, 256, q, qs, mc[:, 0:256], mcs[:, 0:256], Q + " " + MEM + " " + MEMS)
+        for e in range(2):
+            red("#0 lmz%d" % t, "lmo%d%d" % (t, e), lm[:, 4 * h + 2 * e:4 * h + 2 * e + 1], T.ps[:, 128 * e:128 * e + 128], op.max, n=128)
+        OWN = "lmz%d lmo%d0 lmo%d1" % (t, t, t) + (" lmn1" if t else "")
+        spread("m%d" % t, OWN, lm[:, 4 * h:4 * h + 4], lm[:, 4 * h:4 * h + 4])
+        arrive("m%d" % t, from_mates, "lma%d" % t)
+        for b in range(4):
+            mm(1 + b, 128, T.ec[:, 128 * b:128 * b + 128], T.ecs[:, 128 * b:128 * b + 128], q, qs, "ec ecs " + Q, True, False)
+        scan("#0 zz", "cm", T.cm[:, :], T.ps[:, 0:256], T.zz[:, 0:256], -1e29, op.max, op.add, n=256)
+        a, hi16, low = T.aa[:, t:t + 1], T.aa[:, 2 + t:3 + t], T.lw[:, t:t + 1]
+        count("cm", "ah%d" % t, T.cm[:, 15:256:16], AF.Sign, T.cm[:, 255:256], -1.0, hi16, n=16)
+        count("cm", "a%d" % t, T.cm[:, :], AF.Sign, T.cm[:, 255:256], -1.0, a, n=256)
+        ts("dg haz ah%d" % t, "hah", T.ha[:, 0:32:4], T.dg[:, :], hi16, None, op.mult)
+        ts("ah%d a%d" % (t, t), "low%d" % t, low, hi16, -16.0, a, op.mult, op.add)
+        ts("dg haz low%d" % t, "hal", T.ha[:, 1:32:4], T.dg[:, :], low, None, op.mult)
+        quant("haz hah hal", both("hac"), T.hac[:, :], T.hacs[:, :], T.ha[:, :])
+        mm(7, 128, *W(5), T.hac[:, :], T.hacs[:, :], "wc4 wcs4 " + both("hac"))
+        cp("#7", "oaw", T.oaw[:, :], bank(7, 8))
+        pick(mp[:, :], mps[:, :], mc[:, 0:256], mcs[:, 0:256], T.oaw[:, 0:8], MEM, MEMS, "mp%d" % t, "mp%ds" % t, "oaw", 128)
+        for b in range(4):
+            mm(1 + b, 128, T.ec[:, 128 * b:128 * b + 128], T.ecs[:, 128 * b:128 * b + 128], mp[:, :], mps[:, :],
+               "ec ecs mp%d mp%ds" % (t, t), False, True)
+        for b in range(4):
+            if b % 2 == 0:
+                cp("#%d htz" % (1 + b), "ht%d" % b, T.ht[:, b:512:4], bank(1 + b), n=128)
+            else:
+                act("#%d htz" % (1 + b), "ht%d" % b, T.ht[:, b:512:4], bank(1 + b), AF.Copy)
+        quant("ht0 ht1 ht2 ht3 htz htz1", "cand%d cand%ds" % (t, t), mc[:, 256:386], mcs[:, 256:386], T.ht[:, :], 130)
+        ts("idn hfz ah%d" % t, "hfh", T.hf[:, 0:512:4], T.idn[:, :], hi16, None, op.mult)
+        ts("idn hfz low%d" % t, "hfl", T.hf[:, 1:512:4], T.idn[:, :], low, None, op.mult)
+        quant("hfz hfh hfl", both("hfc"), T.hfc[:, :], T.hfcs[:, :], T.hf[:, :])
+        mm(7, 128, *W(6), T.hfc[:, :], T.hfcs[:, :], "wc4 wcs4 " + both("hfc"))
+        act("#7", "fra", T.fra[:, :], bank(7), AF.Identity, bias=1.0)
+        ts("a%d" % t, "nm0", T.nm[:, 0:1], a, 128.0, 128.0 * (hi - 1 - lo), op.is_ge, op.mult)
+        ts("nm0 a%d" % t, "nm1", T.nm[:, 1:2], a, T.nm[:, 0:1], 128.0 * lo, op.add, op.add)
+        nt, nk = ((T.lm1, "lmn1"), (T.nl, "nlo"))[t]
+        ts("nm1 lmz1 nlz", nk, nt[:, 4 * h + 1:4 * h + 4:2], T.zz[:, 0:2], T.nm[:, 1:2], None, op.add)
+        if t == 1:
+            spread("nn", "nlo nlz", T.nl[:, 4 * h:4 * h + 4], T.nl[:, 4 * h:4 * h + 4])
+            arrive("nn", from_mates, "nla")
+        LM = OWN + " lma%d" % t
+        red(LM, "mx", T.mx[:, :], lm[:, 0:16:2], op.max)
+        ts(LM + " mx", "eq", T.eq[:, :], lm[:, 0:16:2], T.mx[:, 0:1], None, op.is_equal)
+        scan("eq " + WD, "sc", T.sc[:, :], T.wd[:, :], T.eq[:, :], 0.0, op.mult, op.add)
+        ts("dg sc", "oc8", T.oc8[:, :], T.dg[:, :], T.sc[:, 7:8], None, op.mult)
+        gather("oc8 hcz hcx " + WINC, "hcg", T.hc[:, 0:512:4], T.winc[:, :], T.oc8[:, 0:8], 128)
+        quant("hcg hcz hcx", both("hcc"), T.hcc[:, 0:130], T.hccs[:, 0:130], T.hc[:, :], 130)
+        for k, i in ((5, 1), (6, 2), (7, 3), (0, 4)):
+            mm(k, 130, *W(i), T.hcc[:, 0:130], T.hccs[:, 0:130], "wc wcs wc4 wcs4 " + both("hcc"))
+        scan("#5 zz", "clo", T.clo[:, :], bank(5), T.zz[:, 0:128], 0.0, op.add, op.add, n=128)
+        scan("#6 zz", "chi", T.chi[:, :], bank(6), T.zz[:, 0:128], 0.0, op.add, op.add, n=128)
+        for c, src, nm in ((0, T.clo, "clo"), (1, T.clo, "clo"), (2, T.chi, "chi")):
+            count("%s kb%d" % (nm, c), "acc%d" % c, src[:, :], AF.Sign, T.kb[:, c:c + 1], -1.0, T.acc[:, c:c + 1])
+        ts("chi kb3", "le", T.le[:, :], T.chi[:, :], T.kb[:, 3:4], None, op.is_le)
+        red("le", "acv", T.acv[:, :], T.le[:, :], op.add, n=128)
+        cp("acv", "os3", T.oslot[:, 3:4], T.acv[:, :])
+        ts("acc0 acc1 acc2", "os0", T.oslot[:, 0:3], T.acc[:, 0:3], 0.5, 64.0, op.mult, op.add)
+        pick(ld[:, 64 * h:64 * h + 64], lds[:, 64 * h:64 * h + 64], mc[:, 256:386], mcs[:, 256:386], T.oslot[:, 0:4],
+             "cand%d" % t, "cand%ds" % t, "slot%d" % t, "slot%ds" % t, "os0 os3", 64)
+        spread("c%d" % t, "slot%d" % t, ld[:, 64 * h:64 * h + 64].bitcast(dt.uint8), ld[:, 64 * h:64 * h + 64].bitcast(dt.uint8))
+        spread("c%d" % t, "slot%ds" % t, lds[:, 64 * h:64 * h + 64], lds[:, 64 * h:64 * h + 64])
+        arrive("c%d" % t, 2 * from_mates, "land%d land%ds" % (t, t))
+        halves = (0, 1) if t == 0 else (own,)
+        tt("#7 fra", "tg", T.tg[:, :], bank(7), T.fra[:, :], op.mult, n=128)
+        for e in halves:
+            src, nm = ((T.clo, "clo"), (T.chi, "chi"))[e]
+            count("%s kb4" % nm, "ta%d" % e, src[:, :], AF.Sign, T.kb[:, 4:5], -1.0, T.ta[:, e:e + 1])
+            ts("tg cp%d" % e, "ep%d" % e, T.ep[:, 128 * e:128 * e + 128], T.tg[:, :], T.cc[:, e:e + 1], None, op.is_equal)
+            scan("ep%d zz" % e, "co%d" % e, T.co[:, 128 * e:128 * e + 128], T.ep[:, 128 * e:128 * e + 128], T.zz[:, 0:128],
+                 0.0, op.max, op.add)
+            count("co%d" % e, "un%d" % e, T.co[:, 128 * e:128 * e + 128], AF.Identity, 1.0, -2.0, T.un[:, e:e + 1])
+            tt("un%d ta%d" % (e, e), "jg%d" % e, T.jg[:, e:e + 1], T.un[:, e:e + 1], T.ta[:, e:e + 1], op.is_lt)
+            ts("un%d cd%d" % (e, e), "jd%d" % e, T.jd[:, e:e + 1], T.un[:, e:e + 1], 0.5, T.cc[:, 4 + e:5 + e], op.mult, op.add)
+            ts("jd%d jg%d cl%d" % (e, e, e), "l3%d" % e, T.l3[:, e:e + 1], T.jd[:, e:e + 1], T.jg[:, e:e + 1],
+               T.cc[:, 2 + e:3 + e], op.mult, op.add)
+        for i, e in enumerate(halves):
+            ts("dg l3%d" % e, "o3%d" % i, T.o3[:, 8 * i:8 * i + 8], T.dg[:, :], T.l3[:, e:e + 1], None, op.mult)
+        v, an = T.vv[:, t:t + 1], T.an[:, t:t + 1]
+        tt("eq " + VD, "pv", T.pv[:, :], T.eq[:, :], T.vd[:, :], op.mult)
+        red("pv", "v%d" % t, v, T.pv[:, :], op.max)
+        cp("v%d" % t, "bi0", T.bi[:, 0:1], v)
+        ts("bi0", "bi1", T.bi[:, 1:2], T.bi[:, 0:1], 255, None, op.bitwise_and)
+        cp("bi1", "kk1", T.kk[:, 1:2], T.bi[:, 1:2])
+        ts("tri v%d" % t, "triv", T.triv[:, :], T.tri[:, :], v, None, op.mult, n=128)
+        tt("#0 triv", "eqt", T.eqt[:, :], bank(0), T.triv[:, :], op.is_equal, n=128)
+        red("eqt", "kk0", T.kk[:, 0:1], T.eqt[:, :], op.add, n=128)
+        ts("kk0", "an%d" % t, an, T.kk[:, 0:1], float(E), None, op.is_lt)
+        ts("kk0 kk1 nold", "kk2", T.kk[:, 2:3], T.kk[:, 0:1], T.kk[:, 1:2], T.kb[:, 6:7], op.add, op.add)
+        ts("kk2 an%d old" % t, "kk3", T.kk[:, 3:4], T.kk[:, 2:3], an, T.kb[:, 5:6], op.mult, op.add)
+        ts("dg kk3", "o2", T.o2[:, :], T.dg[:, :], T.kk[:, 3:4], None, op.mult)
+        gather("o2 wina hlz", "hl0", T.hl[:, 0:128], T.wina[:, :], T.o2[:, 0:8], 128)
+        ts(VD + " v%d" % t, "oh%d" % t, T.oh[:, 8 * t:8 * t + 8], T.vd[:, :], v, None, op.is_equal)
+        ts("an%d" % t, "ws%d" % t, T.wv[:, t:t + 1], an, 2.0, -1.0, op.mult, op.add)
+        ts("an%d" % t, "wb%d" % t, T.wv[:, 2 + t:3 + t], an, -1.0, None, op.add)
+        ts("oh%d ws%d" % (t, t), "og%d" % t, T.og[:, 8 * t:8 * t + 8], T.oh[:, 8 * t:8 * t + 8], T.wv[:, t:t + 1], None, op.mult)
+        if t == 0:
+            gather("o30 wina hlz", "hl1", T.hl[:, 128:256], T.wina[:, :], T.o3[:, 0:8], 128)
+            do("S", "o31 wina hlz", "hl2",
+               lambda: S.activation(T.hl[:, 256:384], T.wina[:, :].indirect(T.o3[:, 8:16]), AF.Copy), 0.23)
+            wrapped(1, 0, 96, T.ol[:, 0:24], "ol", "hl", T.hlc, T.hlcs, T.hl, "hl0 hl1 hl2")
+            pick(T.mc1[:, 0:256], T.mc1s[:, 0:256], mc[:, 0:386], mcs[:, 0:386], T.ol[:, 8:24],
+                 MEM + " cand0", MEMS + " cand0s", "mcown1 mcfar1", "mcown1s mcfar1s", "ol", 256)
+            pick(T.ld1[:, QO:QO + 128], T.ld1s[:, QO:QO + 128], ld[:, 0:384], lds[:, 0:384], T.ol[:, 0:8],
+                 "slot0 land0 qown0 qfar0", "slot0s land0s qown0s qfar0s", "qown1 qfar1", "qown1s qfar1s", "ol", 128)
+        else:
+            wrapped(1, 0, 32, T.ol[:, 0:8], "ol", "hl", T.hlc, T.hlcs, T.hl, "hl0 hl1 hl2")
+            gather("o30 wina hmz", "hm0", T.hm[:, 0:128], T.wina[:, :], T.o3[:, 0:8], 128)
+            wrapped(2, 96, 32, T.om[:, 0:8], "om", "hm", T.hmc, T.hmcs, T.hm, "hm0")
+            pick(T.fm[:, :], T.fms[:, :], mc[:, 0:386], mcs[:, 0:386], T.om[:, 0:8],
+                 MEM + " cand1", MEMS + " cand1s", "fm", "fms", "om", 128)
+            dma("Y", "u0", "fm", "out0", T.oc[:, :], T.fm[:, :].bitcast(dt.uint8))
+            for k in range(4):
+                dma("Y", "u%d" % (1 + k), "fms", "out%d" % (1 + k), T.osc[4 * k:4 * k + 4, :], T.fms[32 * k:32 * k + 4, :])
+
+    one_round(0)
+    one_round(1)
+    pick(T.qf[:, :], T.qfs[:, :], T.ld1[:, 0:384], T.ld1s[:, 0:384], T.ol[:, 0:8],
+         "slot1 land1 qown1 qfar1", "slot1s land1s qown1s qfar1s", "qf", "qfs", "ol", 128)
+    mm(3, 128, T.wq[:, :], T.wqs[:, :], T.qf[:, :], T.qfs[:, :], "wq wqs qf qfs")
+    act("#3", "ysb", T.ysb[:, :], bank(3), AF.Copy)
+    dma("S", "u7", "ysb", "outy", T.y[:, :], T.ysb[:, :])
+    for t, nt, nk in ((0, T.lm1, "lmn1 lmz1 lma1"), (1, T.nl, "nlo nlz nla")):
+        tt("og%d %s" % (t, nk), "oh%d" % t, T.oh[:, 8 * t:8 * t + 8], T.og[:, 8 * t:8 * t + 8], nt[:, 1:16:2], op.mult)
+        red("oh%d" % t, "wg%d" % t, T.wv[:, 4 + t:5 + t], T.oh[:, 8 * t:8 * t + 8], op.add)
+        tt("wg%d wb%d" % (t, t), "wo%d" % t, T.wo[:, t:t + 1], T.wv[:, 4 + t:5 + t], T.wv[:, 2 + t:3 + t], op.add)
+        dma("Y", "u%d" % (5 + t), "wo%d" % t, "out%d" % (5 + t), T.wi[t:t + 1, :], T.wo[:, t:t + 1])
+
+    cnt, known = {}, {q: {} for q in queue}
+    wr, rd = {}, {}
+    for o in in_order(ops):
+        q = o["q"]
+        if o["call"] is None:
+            cnt[o["sem"]] = o["inc"]
+            note((o["sem"], o["inc"], "far", {}), [], o["w"], wr, rd)
+            continue
+        deps = conflicts(q, o["r"], o["w"], wr, rd, o["acc"], False)
+        want = {}
+        for e in deps:
+            if known[q].get(e[0], 0) < e[1]:
+                want[e[0]] = max(want.get(e[0], 0), e[1])
+        for e in deps:
+            for s, v in e[3].items():
+                if s in want and e[0] != s and want[s] <= v:
+                    del want[s]
+        for s, v in want.items():
+            queue[q].wait_ge(T.sem[s], v)
+            known[q][s] = v
+        for e in deps:
+            for s, v in e[3].items():
+                if known[q].get(s, 0) < v:
+                    known[q][s] = v
+        made = o["call"]()
+        if o["sem"]:
+            made.then_inc(T.sem[o["sem"]], o["inc"])
+            cnt[o["sem"]] = cnt.get(o["sem"], 0) + o["inc"]
+            note((o["sem"], cnt[o["sem"]], q if o["sem"] == q else "dma", dict(known[q])), o["r"], o["w"], wr, rd)
+    for s, n in cnt.items():
+        if known["G"].get(s, 0) < n:
+            g.wait_ge(T.sem[s], n)
+    g.wait_ge(T.sem.ls, ls[0])

@@ -3,35 +3,34 @@ from concourse.mybir import dt, AluOpType, AxisListType, ActivationFunctionType
 
 F8 = "float8_e4m3fn_x4"
 SCRATCH = {"ps": ("psum", [128, 4096], "float32")}
-for _n, _w in (("xq", 128), ("wq", 128), ("rx", 32), ("rm", 128), ("ld0", 384), ("ld1", 384), ("qf", 128), ("mc0", 416),
-               ("mc1", 416), ("fm", 128), ("mp0", 128), ("mp1", 128), ("wc", 896), ("ec", 512), ("hac", 128), ("hfc", 128),
-               ("hcc", 136), ("hlc", 128), ("hmc", 128)):
+for _n, _w in (("xq", 128), ("wq", 128), ("rx", 32), ("rm", 128), ("u0", 640), ("u1", 640), ("qf", 128), ("fm", 128),
+               ("mp0", 128), ("mp1", 128), ("cd0", 160), ("cd1", 160), ("wc", 384), ("ec", 512), ("xc", 128), ("hac", 128),
+               ("hcc", 136), ("hqc", 128), ("hmc", 256)):
     SCRATCH[_n] = ("sbuf", [128, _w], F8)
     SCRATCH[_n + "s"] = ("sbuf", [128, _w], "uint8")
-for _n, _w in (("xt", 512), ("mt", 512), ("wt", 512), ("ha", 512), ("hf", 512), ("hc", 520), ("hl", 512), ("hm", 512), ("ht", 520),
-               ("wtile", 3584), ("et", 2048), ("zz", 512), ("wina", 512), ("d1", 512), ("d2", 512), ("winc", 256), ("tc1", 256),
-               ("tc2", 256), ("tc3", 256), ("tri", 128), ("m1", 96), ("hold", 96), ("jm", 128), ("jt", 512), ("jw", 96),
-               ("idn", 128), ("jk", 5120), ("fra", 128), ("clo", 128), ("chi", 128), ("le", 128), ("eqt", 128), ("tg", 128),
-               ("ep", 256), ("co", 256)):
+for _n, _w in (("xt", 512), ("mt", 512), ("wt", 512), ("ha", 512), ("hc", 520), ("hq", 512), ("hm", 1024), ("ht", 520),
+               ("wtile", 1536), ("et", 2048), ("xtile", 512), ("zz", 512), ("jf", 256), ("jm", 128), ("jh", 128), ("tgt", 128),
+               ("c32", 32), ("r32", 32), ("win1", 16), ("tb", 704), ("ida", 128), ("idb", 128), ("ba", 32), ("bb", 32),
+               ("bc", 64), ("tri", 128), ("idn", 128), ("jk", 5120), ("fra", 144), ("pc", 128), ("le", 136), ("eqt", 128),
+               ("triv", 128), ("ne", 128), ("one", 64)):
     SCRATCH[_n] = ("sbuf", [128, _w], "bfloat16")
-for _n, _w in (("jf", 128), ("b8", 8), ("pf", 4), ("rmk", 8), ("dg", 8), ("kb", 8), ("cc", 8), ("vd", 8), ("wd", 8), ("lm0", 16),
-               ("lm1", 16), ("nl", 16), ("cm", 256), ("aa", 4), ("lw", 2), ("vv", 2), ("an", 2), ("w1", 128), ("w2", 128),
-               ("mx", 1), ("eq", 8), ("sc", 8), ("acc", 4), ("acv", 1), ("pv", 8), ("triv", 128), ("kk", 4),
-               ("ta", 2), ("jg", 2), ("jd", 2), ("l3", 2), ("un", 2), ("nm", 2), ("wv", 8), ("oh", 16), ("og", 16), ("wo", 2),
-               ("ysb", 128)):
+for _n, _w in (("pf", 8), ("rmk", 12), ("dg", 8), ("kb", 8), ("odr", 8), ("lm0", 16), ("lm1", 16), ("nl", 16), ("cm", 256),
+               ("aa", 4), ("lw", 2), ("nm", 2), ("c2", 2), ("mx", 2), ("cx", 16), ("w1", 2), ("acc", 4), ("b8", 8), ("cn", 2),
+               ("uu", 2), ("sm", 128), ("wv", 2), ("oh", 16), ("og", 16), ("wo", 2), ("ysb", 128), ("z8", 8), ("e8", 8),
+               ("npl", 2)):
     SCRATCH[_n] = ("sbuf", [128, _w], "float32")
-for _n, _w in (("ox", 2), ("oaw", 8), ("oc8", 8), ("oslot", 4), ("o2", 8), ("o3", 16), ("ol", 24), ("om", 8)):
+for _n, _w in (("ox", 2), ("oaw", 8), ("oc8", 8), ("oslot", 4), ("oq", 8), ("om", 16), ("lq", 8), ("lmem", 16)):
     SCRATCH[_n] = ("sbuf", [128, _w], "uint16")
-for _n, _w in (("pint", 4), ("bi", 2)):
-    SCRATCH[_n] = ("sbuf", [128, _w], "int32")
-SEMAPHORES = ["V", "S", "P", "G", "ls", "xa", "ma", "mr", "ms", "m0", "m1", "nn", "c0", "c1",
-              "dx", "dm", "dw", "t0", "t1", "t2", "t3", "t4", "u0", "u1", "u2", "u3", "u4", "u5", "u6", "u7"]
+SCRATCH["pint"] = ("sbuf", [128, 4], "int32")
+SEMAPHORES = ["V", "S", "P", "G", "ls", "xa", "ma", "mr", "m0", "m1", "nn", "c0", "c1",
+              "dx", "dm", "dw", "o0", "o1", "o2", "o3", "o4", "o5", "o6", "o7"]
 A = 16
 E = 32
-QO = 256
-WAKE = 0.2
-DMA, CALL = 1.8, 0.5
-HOP = {"xa": 6.0, "ma": 7.0, "m0": 1.6, "m1": 1.6, "nn": 1.6, "c0": 2.4, "c1": 2.4}
+SO, QO = 256, 512
+TM, TI = 256, 320
+WAKE = 0.13
+DMA, CALL = 1.9, 0.35
+HOP = {"xa": 4.5, "ma": 4.3, "m0": 1.3, "m1": 1.3, "nn": 1.5, "c0": 2.0, "c1": 2.0}
 
 
 def plan(T, topo):
@@ -40,13 +39,12 @@ def plan(T, topo):
     near = [[q for q in range(n) if q == r or topo.may_write(cores[r], cores[q])] for r in range(n)]
     far = [[q for q in range(n) if q not in near[r]] for r in range(n)]
     chip = [[q for q in range(n) if cores[q] in topo.cores_of(cores[r])] for r in range(n)]
-    partner = [[q for q in far[r] if topo.host(cores[q]) == topo.host(cores[r]) and topo.die(cores[q]) == topo.die(cores[r])][0]
-               for r in range(n)]
+    order = [(i - 1) % n for i in range(n)]
+    partner = [order[order.index(r) ^ 1] for r in range(n)]
+    assert all(partner[r] in far[r] for r in range(n))
     port = [[c for c in topo.cores_of(cores[r]) if c not in cores and topo.die(c) == topo.die(cores[r])
              and topo.may_write(c, cores[far[r][0]])] for r in range(n)]
-    xrel = [(port[chip[r][0]][0], port[chip[r][1]][0]) for r in range(n)]
-    mrel = [(port[r][1], port[r][0]) for r in range(n)]
-    return near, far, chip, partner, xrel, mrel
+    return near, far, chip, order, partner, port
 
 
 def bits(engines):
@@ -69,32 +67,29 @@ def make_send(g, core, T, topo, count):
 
 
 def relay(g, core, T, topo, pl):
-    near, far, chip, partner, xrel, mrel = pl
+    near, far, chip, order, partner, port = pl
     cores = T.cores
     n = [0]
     send = make_send(g, core, T, topo, n)
-    here = [r for r in range(len(cores)) if core in topo.cores_of(cores[r])]
-    for r in here[:1]:
-        off = topo.engines(core, cores[far[r][0]])
-        on = [e for e in topo.engines(core, cores[r]) if e not in off]
-        if core in xrel[r]:
-            g.wait_ge(T.sem.xa, len(on) * len(here))
-            a, b = QO + A * r, QO + A * r + A * len(here)
-            if core == xrel[r][0]:
-                send("xa", [(T.rx[:].bitcast(dt.uint8), [(cores[q], T.ld0[:, a:b].bitcast(dt.uint8)) for q in far[r]], off)])
-            else:
-                send("xa", [(T.rxs[:], [(cores[q], T.ld0s[:, a:b]) for q in far[r]], off)])
-    for r in here:
+    for r in range(len(cores)):
+        if core not in port[r]:
+            continue
+        here = chip[r]
         p = partner[r]
-        h = 128 if r > p else 0
         off = topo.engines(core, cores[p])
-        on = [e for e in topo.engines(core, cores[r]) if e not in off]
-        if core == mrel[r][0]:
-            g.wait_ge(T.sem.mr, len(on))
-            send("ma", [(T.rm[:].bitcast(dt.uint8), [(cores[p], T.mc0[:, h:h + 128].bitcast(dt.uint8))], off)])
-        if core == mrel[r][1]:
-            g.wait_ge(T.sem.ms, len(on))
-            send("ma", [(T.rms[:], [(cores[p], T.mc0s[:, h:h + 128])], off)])
+        allon = topo.engines(core, cores[r])
+        to = chip[p]
+        a, b = QO + A * here[0], QO + A * here[0] + A * len(here)
+        h = 128 if r > p else 0
+        g.wait_ge(T.sem.xa, len(allon))
+        if core == port[r][0]:
+            send("xa", [(T.rx[:].bitcast(dt.uint8), [(cores[q], T.u0[:, a:b].bitcast(dt.uint8)) for q in to], off)])
+            g.wait_ge(T.sem.mr, len(allon))
+            send("ma", [(T.rms[:], [(cores[p], T.u0s[:, h:h + 128])], off)])
+        else:
+            send("xa", [(T.rxs[:], [(cores[q], T.u0s[:, a:b]) for q in to], off)])
+            g.wait_ge(T.sem.mr, len(allon))
+            send("ma", [(T.rm[:].bitcast(dt.uint8), [(cores[p], T.u0[:, h:h + 128].bitcast(dt.uint8))], off)])
     if n[0]:
         g.wait_ge(T.sem.ls, n[0])
 
@@ -168,7 +163,7 @@ def in_order(ops):
 
 def rank_program(g, core, T, topo):
     pl = plan(T, topo)
-    near, far, chip, partner, xrel, mrel = pl
+    near, far, chip, order, partner, port = pl
     cores = T.cores
     N = len(cores)
     rank = T.rank_of(core)
@@ -190,13 +185,13 @@ def rank_program(g, core, T, topo):
         add(q, r, w, call, q, 1, dur, acc=acc)
 
     def ew(n):
-        return max(64, n) * 0.00083
+        return max(64, n) * 0.001
 
     def dma(q, sem, r, w, o, i):
         add(q, r, w, lambda: queue[q].dma_start(o, i), sem, 16, DMA, 0.06)
 
-    def send(sem, r, parts, after=(), tag=None):
-        add("G", r, "", lambda: fused(sem, parts), None, 0, CALL, after=after, tag=tag or sem)
+    def send(sem, r, parts, after=(), tag=None, dur=CALL):
+        add("G", r, "", lambda: fused(sem, parts), None, 0, dur, after=after, tag=tag or sem)
 
     def arrive(sem, n, w, after=None):
         add("far " + sem, "", w, None, sem, n, HOP[sem], after=(after or sem,))
@@ -219,8 +214,11 @@ def rank_program(g, core, T, topo):
     def cp(r, w, out, in_, n=8):
         do("V", r, w, lambda: V.tensor_copy(out, in_), ew(n))
 
-    def gather(r, w, out, win, off, n):
-        do("V", r, w, lambda: V.tensor_copy(out, win.indirect(off)), 0.05 + n * 0.00125)
+    def gather(q, r, w, out, win, off, n):
+        if q == "V":
+            do("V", r, w, lambda: V.tensor_copy(out, win.indirect(off)), 0.055 + n * 0.0015)
+        else:
+            do("S", r, w, lambda: S.activation(out, win.indirect(off), AF.Copy), 0.07 + n * 0.0015)
 
     def act(r, w, out, in_, f, bias=0.0, scale=1.0, accum=None, n=128):
         do("S", r, w, lambda: S.activation(out, in_, f, bias=bias, scale=scale, accum_out=accum), ew(n) + 0.02)
@@ -233,301 +231,300 @@ def rank_program(g, core, T, topo):
         act(r, "%s jk%d" % (w, j), T.jk[:, 256 * j:256 * j + n], in_, f, bias, scale, accum, n)
 
     def quant(r, w, c, s, in_, n=128):
-        do("V", r, w, lambda: V.quantize_mx(c, s, in_), 0.012 + 0.00088 * n)
+        do("V", r, w, lambda: V.quantize_mx(c, s, in_), 0.015 + 0.00105 * n)
 
     def fill(w, ap, c, n=8):
         do("V", "", w, lambda: V.memset(ap, c), ew(n))
 
     def pick(out, outs, win, wins, off, r, rs, w, ws, ro, n):
-        do("V", r + " " + ro, w, lambda: V.tensor_copy(out.bitcast(dt.uint32), win.bitcast(dt.uint32).indirect(off)), 0.05 + n * 0.00125)
-        do("S", rs + " " + ro, ws, lambda: S.activation(outs, wins.indirect(off), AF.Copy), 0.07 + n * 0.00125)
+        do("V", r + " " + ro, w, lambda: V.tensor_copy(out.bitcast(dt.uint32), win.bitcast(dt.uint32).indirect(off)), 0.055 + n * 0.0015)
+        do("S", rs + " " + ro, ws, lambda: S.activation(outs, wins.indirect(off), AF.Copy), 0.07 + n * 0.0015)
 
     def bank(k, n=128):
         return T.ps[:, 512 * k:512 * k + n]
 
-    def mm(k, n, lc, lsc, rc, rsc, r, start=True, stop=True):
-        do("P", r, "#%d" % k, lambda: P.matmul_mx(bank(k, n), lc, lsc, rc, rsc, start, stop), (n + 16) * 0.0008, acc=not start)
+    def mm(k, n, lc, lsc, rc, rsc, r, start=True, stop=True, after=(), tag=None):
+        add("P", r, "#%d" % k, lambda: P.matmul_mx(bank(k, n), lc, lsc, rc, rsc, start, stop), "P", 1, (n + 16) * 0.0008,
+            acc=not start, after=after, tag=tag)
 
     grp = near[rank]
     mates = [q for q in grp if q != rank]
     on_mates = [q for q in mates if q in chip[rank]]
     off_mates = [q for q in mates if q not in chip[rank]]
     eoff = topo.engines(core, cores[off_mates[0]])
-    eon = [e for e in topo.engines(core, cores[on_mates[0]]) if e not in eoff]
-    hosted = {q: sorted((q, partner[q])) for q in grp}
-    h = grp.index(rank)
-    lo, hi = hosted[rank]
-    own = 0 if rank == lo else 1
-    order = [s for q in grp for s in hosted[q]]
-    weight = [2.0 ** (N - 1 - s) for s in order]
+    eall = topo.engines(core, cores[on_mates[0]])
+    eon = [e for e in eall if e not in eoff]
+    pair = [order.index(s) // 2 for s in range(N)]
+    upper = [int(s > partner[s]) for s in range(N)]
+    h = pair[rank]
+    lo, hi = sorted((rank, partner[rank]))
+    own = upper[rank]
     foff = len(eoff)
     from_mates = len(off_mates) * foff + len(on_mates) * len(eon)
 
-    def spread(sem, r, src, dst):
-        send(sem, r, [(src, [(cores[q], dst) for q in off_mates], eoff), (src, [(cores[q], dst) for q in on_mates], eon)])
+    def spread(sem, r, src, dst, after=(), tag=None):
+        send(sem, r, [(src, [(cores[q], dst(q)) for q in off_mates], eoff), (src, [(cores[q], dst(q)) for q in on_mates], eon)],
+             after, tag)
 
-    def iota(w, ap, pat, n, base=0, mul=0, flag=True):
+    def iota(w, ap, pat, n, base=0, mul=0, flag=True, late=False):
         if flag:
-            do("G", "", w, lambda: g.iota(ap, pat, base, mul, allow_small_or_imprecise_dtypes=True), 0.13 + 0.00166 * n)
+            do("G", "", w, lambda: g.iota(ap, pat, base, mul, allow_small_or_imprecise_dtypes=True), 0.15 + 0.002 * n)
         else:
-            do("G", "", w, lambda: g.iota(ap, pat, base, mul), 0.13 + 0.00166 * n)
-        if n > 128:
+            do("G", "", w, lambda: g.iota(ap, pat, base, mul), 0.15 + 0.002 * n)
+        if late:
             ops[-1]["after"] = ("last",)
 
     dma("Y", "dx", "", "xt", T.xt[:, 0:64], T.x[:, :])
     dma("S", "dm", "", "mt", T.mt[:, :], T.me[:, :])
     dma("Y", "dw", "", "wt", T.wt[:, :], T.w[:, :])
-    fill("xz", T.xt[:, 64:512], 0.0, 448)
+    fill("xz", T.xt[:, 64:512], 0.0, 224)
     quant("xt xz", "xq xqs", T.xq[:, 0:128], T.xqs[:, 0:128], T.xt[:, :])
     mo = 128 * own
-    quant("mt", "mcown0 mcown0s", T.mc0[:, mo:mo + 128], T.mc0s[:, mo:mo + 128], T.mt[:, :])
+    quant("mt", "mem0%d mem0%ds" % (own, own), T.u0[:, mo:mo + 128], T.u0s[:, mo:mo + 128], T.mt[:, :])
     qa = QO + A * rank
     ra = A * chip[rank].index(rank)
-    xs, xd = T.xq[:, 0:A].bitcast(dt.uint8), T.ld0[:, qa:qa + A].bitcast(dt.uint8)
-    ys, yd = T.xqs[:, 0:A], T.ld0s[:, qa:qa + A]
-    send("xa", "xq", [(xs, [(xrel[rank][0], T.rx[:, ra:ra + A].bitcast(dt.uint8))] + [(cores[q], xd) for q in on_mates], eon)],
-         tag="s0")
-    send("xa", "xqs", [(ys, [(xrel[rank][1], T.rxs[:, ra:ra + A])] + [(cores[q], yd) for q in on_mates], eon)],
+    xs, xd = T.xq[:, 0:A].bitcast(dt.uint8), T.u0[:, qa:qa + A].bitcast(dt.uint8)
+    ys, yd = T.xqs[:, 0:A], T.u0s[:, qa:qa + A]
+    sets = (eon, eoff)
+    send("xa", "xqs", [(ys, [(port[q][1], T.rxs[:, ra:ra + A])], sets[i]) for i, q in enumerate(chip[rank])], tag="s0", dur=1.4)
+    send("xa", "xq", [(xs, [(port[q][0], T.rx[:, ra:ra + A].bitcast(dt.uint8))], sets[i]) for i, q in enumerate(chip[rank])],
          after=("s0",), tag="s1")
-    send("mr", "mcown0", [(T.mc0[:, mo:mo + 128].bitcast(dt.uint8), [(mrel[rank][0], T.rm[:].bitcast(dt.uint8))], eon)],
+    send("mr", "mem0%d" % own, [(T.u0[:, mo:mo + 128].bitcast(dt.uint8), [(port[rank][1], T.rm[:].bitcast(dt.uint8))], eall)],
          after=("s1",), tag="s2")
-    send("ms", "mcown0s", [(T.mc0s[:, mo:mo + 128], [(mrel[rank][1], T.rms[:])], eon)], after=("s2",), tag="s3")
-    send("xa", "xq", [(xs, [(cores[q], xd) for q in off_mates], eoff)], after=("s3",), tag="s4")
-    send("xa", "xqs", [(ys, [(cores[q], yd) for q in off_mates], eoff)], after=("s4",), tag="last")
+    send("mr", "mem0%ds" % own, [(T.u0s[:, mo:mo + 128], [(port[rank][0], T.rms[:])], eall)], after=("s2",), tag="s3")
+    spread("xa", "xq", xs, lambda q: xd, after=("s3",), tag="s4")
+    spread("xa", "xqs", ys, lambda q: yd, after=("s4",), tag="last")
     arrive("xa", 2 * (from_mates + foff * (len(far[rank]) // len(chip[rank]))), "qfar0 qfar0s", "s1")
-    arrive("ma", 2 * foff, "mcfar0 mcfar0s", "s3")
+    arrive("ma", 2 * foff, "mem0%d mem0%ds" % (1 - own, 1 - own), "s3")
     iota("pint0", T.pint[:, 0:1], [[0, 1]], 1, 0, 1, False)
-    iota("b8", T.b8[:, :], [[1, 8]], 8)
-    iota("jf", T.jf[:, :], [[1, 128]], 128)
     iota("jm", T.jm[:, :], [[0, 8], [1, 16]], 128)
-    iota("jw", T.jw[:, :], [[0, 24], [1, 4]], 96)
-    iota("jt", T.jt[:, :], [[0, 32], [-1, 4], [1, 4]], 512)
-    iota("wina", T.wina[:, :], [[0, 32], [1, 16]], 512)
-    iota("d1", T.d1[:, :], [[0, 2], [16, 16], [0, 16]], 512)
-    iota("d2", T.d2[:, :], [[256, 2], [0, 256]], 512)
+    iota("jf", T.jf[:, 0:128], [[1, 128]], 128)
+    iota("jf2", T.jf[:, 128:256], [[1, 128]], 128, 128, late=True)
+    iota("jh", T.jh[:, :], [[1, 8], [0, 16]], 128, late=True)
+    iota("c32", T.c32[:, :], [[-1, 4], [0, 8]], 32, 3, late=True)
+    iota("r32", T.r32[:, :], [[0, 4], [-1, 8]], 32, 7, late=True)
     fill("zz", T.zz[:, :], 0.0, 256)
+    fill("z8", T.z8[:, :], 0.0)
+    fill("one", T.one[:, :], 1.0)
     ts("pint0", "p16i", T.pint[:, 1:2], T.pint[:, 0:1], 15, None, op.bitwise_and)
     ts("pint0", "g16i", T.pint[:, 2:3], T.pint[:, 0:1], 4, None, op.logical_shift_right)
-    cp("pint0", "pf0", T.pf[:, 0:1], T.pint[:, 0:1])
-    ts("p16i", "p4i", T.pint[:, 3:4], T.pint[:, 1:2], 2, None, op.logical_shift_right)
-    cp("p16i", "p16", T.pf[:, 1:2], T.pint[:, 1:2])
-    cp("g16i", "g16", T.pf[:, 2:3], T.pint[:, 2:3])
-    cp("p4i", "p4", T.pf[:, 3:4], T.pint[:, 3:4])
+    ts("pint0", "p8i", T.pint[:, 3:4], T.pint[:, 0:1], 7, None, op.bitwise_and)
+    cp("pint0 p16i g16i p8i", "pf", T.pf[:, 0:4], T.pint[:, 0:4])
     cp("p16i", "ox", T.ox[:, 0:1], T.pint[:, 1:2])
-    pick(T.ld0[:, qa:qa + A], T.ld0s[:, qa:qa + A], T.xq[:, 0:128], T.xqs[:, 0:128], T.ox[:, 0:1],
+    pick(T.u0[:, qa:qa + A], T.u0s[:, qa:qa + A], T.xq[:, 0:128], T.xqs[:, 0:128], T.ox[:, 0:1],
          "xq", "xqs", "qown0", "qown0s", "ox", 16)
-    pf, p16, g16, p4 = T.pf[:, 0:1], T.pf[:, 1:2], T.pf[:, 2:3], T.pf[:, 3:4]
-    for k in range(4):
-        ts("p16", "rm%d" % k, T.rmk[:, k:k + 1], p16, float(k), None, op.is_equal)
-    ts("p16", "rm4", T.rmk[:, 4:5], p16, 2.0, None, op.is_lt)
-    ts("p16", "rm5", T.rmk[:, 5:6], p16, 3.0, None, op.is_lt)
-    tt("rm2 rm3", "rm6", T.rmk[:, 6:7], T.rmk[:, 2:3], T.rmk[:, 3:4], op.add)
+    pf, p16, g16, p8 = T.pf[:, 0:1], T.pf[:, 1:2], T.pf[:, 2:3], T.pf[:, 3:4]
+    ts("pf", "pf4", T.pf[:, 4:5], pf, 128.0, None, op.add)
+    ts("pf", "old", T.pf[:, 5:6], pf, float(TI + QO - SO), None, op.add)
+    ts("pf", "p161", T.pf[:, 6:7], p16, 1.0, None, op.add)
+    place = (pf, T.pf[:, 4:5])
+    ts("pf pf4", "npl", T.npl[:, :], T.pf[:, 0:5:4], -512.0, None, op.mult)
+    rm = lambda k: T.rmk[:, k:k + 1]
+    ts("jm pf", "rm", T.rmk[:, 0:3], T.jm[:, 0:3], p16, None, op.is_equal)
+    ts("rm", "rm3", rm(3), rm(0), 4.0, None, op.mult)
+    ts("rm", "rm4", rm(4), rm(1), 8.0, None, op.mult)
+    tt("rm3 rm4", "rm5", rm(5), rm(3), rm(4), op.add)
+    ts("rm", "rm6", rm(6), rm(2), 2.0, None, op.mult)
+    ts("rm rm6", "rm7", rm(7), rm(0), 3.0, rm(6), op.mult, op.add)
+    ts("rm rm7", "rm8", rm(8), rm(1), 15.0, rm(7), op.mult, op.add)
+    ts("rm", "rm9", rm(9), rm(0), 16.0, rm(1), op.mult, op.add)
+    ts("rm rm9", "rm10", rm(10), rm(2), 128.0, rm(9), op.mult, op.add)
     for t in range(2):
         fill("lmz%d" % t, T["lm%d" % t][:, 4 * h:4 * h + 4], 0.0)
     fill("nlz", T.nl[:, 4 * h:4 * h + 4], 0.0)
-    for i, k in ((1, 0), (2, 1), (3, 4), (4, 6)):
-        act("zz rm%d" % k, "wt%d" % i, T.wtile[:, 512 * i:512 * i + 512], T.zz[:, :], AF.Identity, bias=T.rmk[:, k:k + 1], n=512)
-    for nm, a, b in (("wt5", 2560, 3072), ("wt6", 3072, 3584)):
-        act("zz", nm, T.wtile[:, a:b], T.zz[:, 0:b - a], AF.Copy, n=512)
-    for nm in ("ha", "hf", "hc", "hl", "ht", "hm"):
-        act("zz", nm + "z", T[nm][:, 0:512], T.zz[:, 0:512], AF.Copy, n=512)
-    act("zz", "htz1", T.ht[:, 512:520], T.zz[:, 0:8], AF.Copy, n=8)
-    ts("b8 g16", "dg", T.dg[:, :], T.b8[:, :], g16, None, op.is_equal)
-    ts("jw p4", "m1", T.m1[:, :], T.jw[:, :], p4, None, op.is_equal)
-    ts("jw", "hold", T.hold[:, :], T.jw[:, :], 0.0, None, op.is_gt)
-    ts("jf pf0", "idn", T.idn[:, :], T.jf[:, :], pf, None, op.is_equal, n=128)
-    fill("et", T.et[:, :], 0.0, 1024)
+    fill("cxz", T.cx[:, 0:16:8], -1e29)
+    fill("c2", T.c2[:, :], 128.0 * lo + 0.5)
+    fill("fraz", T.fra[:, 128:144], -1.0)
+    fill("lez", T.le[:, 128:129], -128.0)
+    fill("kb4", T.kb[:, 4:5], E - 0.5)
+    fill("kb5", T.kb[:, 5:6], -0.5 / N)
+    fill("kb6", T.kb[:, 6:7], -float(E))
+    fill("e8", T.e8[:, :], float(E))
+    ts("jm", "odr1", T.odr[:, 1:8], T.jm[:, 1:8], 0.0, None, op.add)
+    fill("odr0", T.odr[:, 0:1], float(N))
+    for nm, n in (("ha", 1), ("hc", 1), ("hq", 1), ("hm", 2)):
+        for i in range(n):
+            act("zz", "%sz%d" % (nm, i), T[nm][:, 512 * i:512 * i + 512], T.zz[:, 0:512], AF.Copy, n=512)
+    fill("htz", T.ht[:, 512:520], 0.0)
+    ts("jm pf", "dg", T.dg[:, :], T.jm[:, 0:8], g16, None, op.is_equal)
+    ts("jf pf", "idn", T.idn[:, :], T.jf[:, 0:128], pf, None, op.is_equal)
+    ts("jf pf", "tri", T.tri[:, :], T.jf[:, 0:128], pf, None, op.is_lt)
+    ts("jm p161", "win1", T.win1[:, :], T.jm[:, 0:16], T.pf[:, 6:7], None, op.is_equal)
     for b in range(4):
-        ts("idn et", "et%d" % b, T.et[:, 512 * b + b:512 * b + 512:4], T.idn[:, :], 0.5, None, op.mult)
-    quant("et et0 et1 et2 et3", "ec ecs", T.ec[:, :], T.ecs[:, :], T.et[:, :], 512)
-    ts("jf pf0", "tri", T.tri[:, :], T.jf[:, :], pf, None, op.is_lt, n=128)
-    for k in range(4):
-        ts("p16", "kb%d" % k, T.kb[:, k:k + 1], p16, 16.0 * (k % 2) + 0.5, None, op.add)
-    fill("kb4", T.kb[:, 4:5], E + 0.5)
-    ts("pf0", "old", T.kb[:, 5:6], pf, float(QO), None, op.add)
-    ts("pf0", "nold", T.kb[:, 6:7], pf, -1.0, -float(QO), op.mult, op.add)
-    for e in range(2):
-        ts("pf0", "cp%d" % e, T.cc[:, e:e + 1], pf, 128.0 * e + 1, None, op.add)
-        ts("pf0", "cl%d" % e, T.cc[:, 2 + e:3 + e], pf, 128.0 * e, None, op.add)
-        ts("pf0", "cd%d" % e, T.cc[:, 4 + e:5 + e], pf, -1.0, 320.0 - 128.0 * e, op.mult, op.add)
-    for i, (nm, val) in enumerate((("winc", lambda s: float(s == lo)), ("tc1", lambda s: float(s == hi)),
-                                   ("tc2", lambda s: 256.0 * (N - s)), ("tc3", lambda s: 32.0 * order.index(s)))):
-        fill(nm + "z", T[nm][:, 0:256], 0.0, 128)
-        for s in range(N):
-            if val(s):
-                do("V", nm + "z", nm + "_%d" % s,
-                   lambda nm=nm, s=s, val=val: V.memset(T[nm][:, 2 ** (N - 1 - s):2 ** (N - s)], val(s)), ew(8))
-    keys = lambda nm: " ".join([nm + "z"] + [nm + "_%d" % s for s in range(N)])
-    for i in range(N):
-        fill("vd%d" % i, T.vd[:, i:i + 1], 256.0 * (N - order[i]) + 32.0 * i)
-        fill("wd%d" % i, T.wd[:, i:i + 1], weight[i - 1] / weight[i] if i else 1.0)
-    VD, WD = " ".join("vd%d" % i for i in range(N)), " ".join("wd%d" % i for i in range(N))
-    ts("jt rm5", "wt0", T.wtile[:, 0:512], T.jt[:, :], 0.0, T.rmk[:, 5:6], op.is_equal, op.mult, n=256)
-    ts("jm p16 wt5", "wt5a", T.wtile[:, 2560:3072:4], T.jm[:, :], p16, 16.0, op.is_equal, op.mult)
-    ts("jm p16 wt5", "wt5b", T.wtile[:, 2561:3072:4], T.jm[:, :], p16, None, op.is_equal)
-    ts("zz wt6", "wt6a", T.wtile[:, 3072:3584:4], T.zz[:, 0:128], 16.0, None, op.add)
-    ts("zz wt6", "wt6b", T.wtile[:, 3073:3584:4], T.zz[:, 0:128], 1.0, None, op.add)
-    quant("wt0 wt1 wt2 wt3", "wc wcs", T.wc[:, 0:512], T.wcs[:, 0:512], T.wtile[:, 0:2048], 512)
-    quant("wt4 wt5 wt6 wt5a wt5b wt6a wt6b", "wc4 wcs4", T.wc[:, 512:896], T.wcs[:, 512:896], T.wtile[:, 2048:3584], 384)
+        act("zz", "etz%d" % b, T.et[:, 512 * b:512 * b + 512], T.zz[:, :], AF.Copy, n=512)
+        ts("idn etz%d" % b, "et%d" % b, T.et[:, 512 * b + b:512 * b + 512:4], T.idn[:, :], 0.5, None, op.mult)
+    for b in (0, 2):
+        quant("etz%d etz%d et%d et%d" % (b, b + 1, b, b + 1), "ec%d" % b, T.ec[:, 128 * b:128 * b + 256], T.ecs[:, 128 * b:128 * b + 256],
+              T.et[:, 512 * b:512 * b + 1024], 256)
+    for c in range(4):
+        ts("pf", "kb%d" % c, T.kb[:, c:c + 1], p8, -1.0, E - 0.5 - 8.0 * c, op.mult, op.add)
+    for i in range(3):
+        fill("wz%d" % i, T.wtile[:, 512 * i:512 * i + 512], 0.0, 256)
+    ts("jm pf wz0", "w0a", T.wtile[:, 0:512:4], T.jm[:, :], p16, 16.0, op.is_equal, op.mult)
+    ts("jm pf wz0", "w0b", T.wtile[:, 1:512:4], T.jm[:, :], p16, None, op.is_equal)
+    ts("jm", "tgt", T.tgt[:, :], T.jm[:, :], 8.0, float(hi - lo), op.is_ge, op.mult)
+    ts("tgt pf wz1", "w1a", T.wtile[:, 512:1024:4], T.tgt[:, :], float(lo), p16, op.add, op.is_equal)
+    ts("zz p161 wz2", "w2a", T.wtile[:, 1024:1536:4], T.zz[:, 0:128], T.pf[:, 6:7], None, op.add)
+    quant("wz0 w0a w0b", "wc0", T.wc[:, 0:128], T.wcs[:, 0:128], T.wtile[:, 0:512])
+    quant("wz1 wz2 w1a w2a", "wc1", T.wc[:, 128:384], T.wcs[:, 128:384], T.wtile[:, 512:1536], 256)
+    fill("xtz", T.xtile[:, :], 0.0, 256)
+    ts("dg rm10 xtz", "xta", T.xtile[:, 0:32:4], T.dg[:, :], rm(10), None, op.mult)
+    cp("xt xtz", "xtb", T.xtile[:, 32:40], T.xt[:, 0:8])
+    quant("xtz xta xtb", "xc", T.xc[:, :], T.xcs[:, :], T.xtile[:, :])
     cp("xt", "hcx", T.hc[:, 512:520], T.xt[:, 0:8])
-    cp("xt hlz", "hlx", T.hl[:, 504:512], T.xt[:, 0:8])
-    cp("xt hmz", "hmx", T.hm[:, 504:512], T.xt[:, 0:8])
     quant("wt", "wq wqs", T.wq[:, :], T.wqs[:, :], T.wt[:, :])
-    dma("Y", "t0", "d1", "wina", T.wina[1:128:16, :], T.d1[1:128:16, :])
-    dma("Y", "t1", "d2", "wina", T.wina[2:128:16, :], T.d2[2:128:16, :])
-    for k in (1, 2, 3):
-        dma("Y", "t%d" % (k + 1), keys("tc%d" % k) + " " + keys("winc"), "wincr%d" % k,
-            T.winc[k:128:16, :], T["tc%d" % k][k:128:16, :])
-    WINC = keys("winc") + " wincr1 wincr2 wincr3"
+    act("jh rm", "ida", T.ida[:, :], T.jh[:, :], AF.Identity, scale=rm(0))
+    act("jm rm", "idb", T.idb[:, :], T.jm[:, :], AF.Identity, scale=rm(1))
+    tt("ida idb", "tbi0", T.tb[:, TI:TI + 128], T.ida[:, :], T.idb[:, :], op.add, n=256)
+    act("tbi0 rm", "tbi1", T.tb[:, TI + 128:TI + 256], T.tb[:, TI:TI + 128], AF.Identity, bias=rm(2))
+    act("tbi0 rm6", "tbi2", T.tb[:, TI + 256:TI + 384], T.tb[:, TI:TI + 128], AF.Identity, bias=rm(6))
+    act("tbi0 rm8", "tbm", T.tb[:, TM:TM + 64], T.tb[:, TI:TI + 64], AF.Identity, bias=rm(8), scale=-1.0, n=64)
+    act("c32 rm", "ba", T.ba[:, :], T.c32[:, :], AF.Identity, scale=rm(0), n=32)
+    act("r32 rm", "bb", T.bb[:, :], T.r32[:, :], AF.Identity, scale=rm(1), n=32)
+    tt("ba bb", "bc0", T.bc[:, 0:32], T.ba[:, :], T.bb[:, :], op.add)
+    act("bc0 rm", "bc1", T.bc[:, 32:64], T.bc[:, 0:32], AF.Identity, bias=rm(2), n=32)
+    for s in range(N):
+        d = (pair[s] - h) % len(grp)
+        act("bc0 bc1 rm3 rm4 rm5", "tbq%d" % s, T.tb[:, E * s:E * s + E], T.bc[:, E * (d // 2):E * (d // 2) + E], AF.Identity,
+            bias=(0.0, rm(4), rm(3), rm(5))[2 * (d % 2) + upper[s]], n=32)
+    TBM = "tbm tbi0 tbi1"
+    TBQ = TBM + " tbi2 " + " ".join("tbq%d" % s for s in range(N))
 
     def W(i):
         return T.wc[:, 128 * i:128 * i + 128], T.wcs[:, 128 * i:128 * i + 128]
 
     def both(nm):
-        return "%s %ss" % (nm, nm)
-
-    def wrapped(k, z, n, out, w, hk, hcod, hsc, h_, r):
-        quant("%s %sz %sx" % (r, hk, hk), both(hk + "c"), hcod[:, :], hsc[:, :], h_[:, :])
-        mm(k, 128, *W(0), hcod[:, :], hsc[:, :], "wc wcs " + both(hk + "c"))
-        scan("#%d m1" % k, "w1" + hk, T.w1[:, z:z + n], bank(k, n), T.m1[:, 0:n], 0.0, op.add, op.mult, n=n)
-        scan("w1%s hold" % hk, "w2" + hk, T.w2[:, z:z + n], T.hold[:, 0:n], T.w1[:, z:z + n], 0.0, op.mult, op.add, n=n)
-        cp("w2" + hk, w, out, T.w2[:, z + 3:z + n:4])
+        return " ".join("%s %ss" % (k, k) for k in nm.split())
 
     def one_round(t):
-        ld, lds = T["ld%d" % t], T["ld%ds" % t]
-        mc, mcs = T["mc%d" % t], T["mc%ds" % t]
+        u, us = T["u%d" % t], T["u%ds" % t]
+        cd, cds = T["cd%d" % t], T["cd%ds" % t]
         mp, mps = T["mp%d" % t], T["mp%ds" % t]
         lm = T["lm%d" % t]
-        q, qs = ld[:, QO:QO + 128], lds[:, QO:QO + 128]
-        Q = "qown%d qown%ds qfar%d qfar%ds" % (t, t, t, t)
-        MEM = "mcown%d mcfar%d" % (t, t)
-        MEMS = "mcown%ds mcfar%ds" % (t, t)
-        mm(0, 256, q, qs, mc[:, 0:256], mcs[:, 0:256], Q + " " + MEM + " " + MEMS)
-        for e in range(2):
-            red("#0 lmz%d" % t, "lmo%d%d" % (t, e), lm[:, 4 * h + 2 * e:4 * h + 2 * e + 1], T.ps[:, 128 * e:128 * e + 128], op.max, n=128)
+        q, qs = u[:, QO:QO + 128], us[:, QO:QO + 128]
+        Q = both("qown%d qfar%d" % (t, t))
+        MEM = "mem%d0 mem%d1" % (t, t)
+        MEMS = "mem%d0s mem%d1s" % (t, t)
+        for e in (own, 1 - own):
+            mm(e, 128, q, qs, u[:, 128 * e:128 * e + 128], us[:, 128 * e:128 * e + 128], Q + " " + both("mem%d%d" % (t, e)))
+            c = 2 * order.index((lo, hi)[e])
+            red("#%d lmz%d" % (e, t), "lmo%d%d" % (t, e), lm[:, c:c + 1], bank(e), op.max, n=128)
+        mm(2, 256, q, qs, u[:, 0:256], us[:, 0:256], Q + " " + MEM + " " + MEMS, tag="sc%d" % t)
         OWN = "lmz%d lmo%d0 lmo%d1" % (t, t, t) + (" lmn1" if t else "")
-        spread("m%d" % t, OWN, lm[:, 4 * h:4 * h + 4], lm[:, 4 * h:4 * h + 4])
+        spread("m%d" % t, OWN, lm[:, 4 * h:4 * h + 4], lambda r: lm[:, 4 * h:4 * h + 4])
         arrive("m%d" % t, from_mates, "lma%d" % t)
         for b in range(4):
-            mm(1 + b, 128, T.ec[:, 128 * b:128 * b + 128], T.ecs[:, 128 * b:128 * b + 128], q, qs, "ec ecs " + Q, True, False)
-        scan("#0 zz", "cm", T.cm[:, :], T.ps[:, 0:256], T.zz[:, 0:256], -1e29, op.max, op.add, n=256)
+            mm(3 + b, 128, T.ec[:, 128 * b:128 * b + 128], T.ecs[:, 128 * b:128 * b + 128], q, qs, "ec0 ec2 " + Q, True, False,
+               after=("sc%d" % t,))
+        scan("#2 zz", "cm", T.cm[:, :], bank(2, 256), T.zz[:, 0:256], -1e29, op.max, op.add, n=256)
         a, hi16, low = T.aa[:, t:t + 1], T.aa[:, 2 + t:3 + t], T.lw[:, t:t + 1]
         count("cm", "ah%d" % t, T.cm[:, 15:256:16], AF.Sign, T.cm[:, 255:256], -1.0, hi16, n=16)
         count("cm", "a%d" % t, T.cm[:, :], AF.Sign, T.cm[:, 255:256], -1.0, a, n=256)
-        ts("dg haz ah%d" % t, "hah", T.ha[:, 0:32:4], T.dg[:, :], hi16, None, op.mult)
+        ts("dg haz0 ah%d" % t, "hah", T.ha[:, 0:32:4], T.dg[:, :], hi16, None, op.mult)
         ts("ah%d a%d" % (t, t), "low%d" % t, low, hi16, -16.0, a, op.mult, op.add)
-        ts("dg haz low%d" % t, "hal", T.ha[:, 1:32:4], T.dg[:, :], low, None, op.mult)
-        quant("haz hah hal", both("hac"), T.hac[:, :], T.hacs[:, :], T.ha[:, :])
-        mm(7, 128, *W(5), T.hac[:, :], T.hacs[:, :], "wc4 wcs4 " + both("hac"))
+        ts("dg haz0 low%d" % t, "hal", T.ha[:, 1:32:4], T.dg[:, :], low, None, op.mult)
+        quant("haz0 hah hal", both("hac"), T.hac[:, :], T.hacs[:, :], T.ha[:, :])
+        mm(7, 128, *W(0), T.hac[:, :], T.hacs[:, :], "wc0 " + both("hac"))
         cp("#7", "oaw", T.oaw[:, :], bank(7, 8))
-        pick(mp[:, :], mps[:, :], mc[:, 0:256], mcs[:, 0:256], T.oaw[:, 0:8], MEM, MEMS, "mp%d" % t, "mp%ds" % t, "oaw", 128)
+        pick(mp[:, :], mps[:, :], u[:, 0:256], us[:, 0:256], T.oaw[:, 0:8], MEM, MEMS, "mp%d" % t, "mp%ds" % t, "oaw", 128)
         for b in range(4):
-            mm(1 + b, 128, T.ec[:, 128 * b:128 * b + 128], T.ecs[:, 128 * b:128 * b + 128], mp[:, :], mps[:, :],
-               "ec ecs mp%d mp%ds" % (t, t), False, True)
+            mm(3 + b, 128, T.ec[:, 128 * b:128 * b + 128], T.ecs[:, 128 * b:128 * b + 128], mp[:, :], mps[:, :],
+               "ec0 ec2 mp%d mp%ds" % (t, t), False, True)
         for b in range(4):
             if b % 2 == 0:
-                cp("#%d htz" % (1 + b), "ht%d" % b, T.ht[:, b:512:4], bank(1 + b), n=128)
+                cp("#%d" % (3 + b), "ht%d" % b, T.ht[:, b:512:4], bank(3 + b), n=128)
             else:
-                act("#%d htz" % (1 + b), "ht%d" % b, T.ht[:, b:512:4], bank(1 + b), AF.Copy)
-        quant("ht0 ht1 ht2 ht3 htz htz1", "cand%d cand%ds" % (t, t), mc[:, 256:386], mcs[:, 256:386], T.ht[:, :], 130)
-        ts("idn hfz ah%d" % t, "hfh", T.hf[:, 0:512:4], T.idn[:, :], hi16, None, op.mult)
-        ts("idn hfz low%d" % t, "hfl", T.hf[:, 1:512:4], T.idn[:, :], low, None, op.mult)
-        quant("hfz hfh hfl", both("hfc"), T.hfc[:, :], T.hfcs[:, :], T.hf[:, :])
-        mm(7, 128, *W(6), T.hfc[:, :], T.hfcs[:, :], "wc4 wcs4 " + both("hfc"))
-        act("#7", "fra", T.fra[:, :], bank(7), AF.Identity, bias=1.0)
-        ts("a%d" % t, "nm0", T.nm[:, 0:1], a, 128.0, 128.0 * (hi - 1 - lo), op.is_ge, op.mult)
-        ts("nm0 a%d" % t, "nm1", T.nm[:, 1:2], a, T.nm[:, 0:1], 128.0 * lo, op.add, op.add)
+                act("#%d" % (3 + b), "ht%d" % b, T.ht[:, b:512:4], bank(3 + b), AF.Copy)
+        quant("ht0 ht1 ht2 ht3 htz", "cand%d cand%ds" % (t, t), cd[:, 0:130], cds[:, 0:130], T.ht[:, :], 130)
+        gather("S", "oaw jf jf2", "fra", T.fra[:, 0:128], T.jf[:, :], T.oaw[:, 0:8], 128)
         nt, nk = ((T.lm1, "lmn1"), (T.nl, "nlo"))[t]
-        ts("nm1 lmz1 nlz", nk, nt[:, 4 * h + 1:4 * h + 4:2], T.zz[:, 0:2], T.nm[:, 1:2], None, op.add)
+        if hi - lo > 1:
+            ts("a%d" % t, "nm0", T.nm[:, 0:1], a, 128.0, 128.0 * (hi - 1 - lo), op.is_ge, op.mult)
+            ts("nm0 a%d c2 lmz1 nlz" % t, nk, nt[:, 4 * h + 1:4 * h + 4:2], T.c2[:, :], a, T.nm[:, 0:1], op.add, op.add)
+        else:
+            ts("a%d c2 lmz1 nlz" % t, nk, nt[:, 4 * h + 1:4 * h + 4:2], T.c2[:, :], a, None, op.add)
         if t == 1:
-            spread("nn", "nlo nlz", T.nl[:, 4 * h:4 * h + 4], T.nl[:, 4 * h:4 * h + 4])
+            spread("nn", "nlo nlz", T.nl[:, 4 * h:4 * h + 4], lambda r: T.nl[:, 4 * h:4 * h + 4])
             arrive("nn", from_mates, "nla")
         LM = OWN + " lma%d" % t
-        red(LM, "mx", T.mx[:, :], lm[:, 0:16:2], op.max)
-        ts(LM + " mx", "eq", T.eq[:, :], lm[:, 0:16:2], T.mx[:, 0:1], None, op.is_equal)
-        scan("eq " + WD, "sc", T.sc[:, :], T.wd[:, :], T.eq[:, :], 0.0, op.mult, op.add)
-        ts("dg sc", "oc8", T.oc8[:, :], T.dg[:, :], T.sc[:, 7:8], None, op.mult)
-        gather("oc8 hcz hcx " + WINC, "hcg", T.hc[:, 0:512:4], T.winc[:, :], T.oc8[:, 0:8], 128)
-        quant("hcg hcz hcx", both("hcc"), T.hcc[:, 0:130], T.hccs[:, 0:130], T.hc[:, :], 130)
-        for k, i in ((5, 1), (6, 2), (7, 3), (0, 4)):
-            mm(k, 130, *W(i), T.hcc[:, 0:130], T.hccs[:, 0:130], "wc wcs wc4 wcs4 " + both("hcc"))
-        scan("#5 zz", "clo", T.clo[:, :], bank(5), T.zz[:, 0:128], 0.0, op.add, op.add, n=128)
-        scan("#6 zz", "chi", T.chi[:, :], bank(6), T.zz[:, 0:128], 0.0, op.add, op.add, n=128)
-        for c, src, nm in ((0, T.clo, "clo"), (1, T.clo, "clo"), (2, T.chi, "chi")):
-            count("%s kb%d" % (nm, c), "acc%d" % c, src[:, :], AF.Sign, T.kb[:, c:c + 1], -1.0, T.acc[:, c:c + 1])
-        ts("chi kb3", "le", T.le[:, :], T.chi[:, :], T.kb[:, 3:4], None, op.is_le)
-        red("le", "acv", T.acv[:, :], T.le[:, :], op.add, n=128)
-        cp("acv", "os3", T.oslot[:, 3:4], T.acv[:, :])
-        ts("acc0 acc1 acc2", "os0", T.oslot[:, 0:3], T.acc[:, 0:3], 0.5, 64.0, op.mult, op.add)
-        pick(ld[:, 64 * h:64 * h + 64], lds[:, 64 * h:64 * h + 64], mc[:, 256:386], mcs[:, 256:386], T.oslot[:, 0:4],
-             "cand%d" % t, "cand%ds" % t, "slot%d" % t, "slot%ds" % t, "os0 os3", 64)
-        spread("c%d" % t, "slot%d" % t, ld[:, 64 * h:64 * h + 64].bitcast(dt.uint8), ld[:, 64 * h:64 * h + 64].bitcast(dt.uint8))
-        spread("c%d" % t, "slot%ds" % t, lds[:, 64 * h:64 * h + 64], lds[:, 64 * h:64 * h + 64])
+        cx, w1 = T.cx[:, 8 * t:8 * t + 8], T.w1[:, t:t + 1]
+        scan(LM + " zz cxz", "cx%d" % t, T.cx[:, 8 * t + 1:8 * t + 8], lm[:, 2:16:2], T.zz[:, 0:7], -1e29, op.max, op.add)
+        red(LM, "mx%d" % t, T.mx[:, t:t + 1], lm[:, 0:16:2], op.max)
+        count("cxz cx%d mx%d" % (t, t), "w1%d" % t, cx, AF.Sign, T.mx[:, t:t + 1], -1.0, w1, n=8)
+        ts("dg w1%d" % t, "oc8", T.oc8[:, :], T.dg[:, :], w1, None, op.mult)
+        gather("V", "oc8 hcz0 win1", "hcg", T.hc[:, 0:512:4], T.win1[:, :], T.oc8[:, 0:8], 128)
+        quant("hcg hcz0 hcx", both("hcc"), T.hcc[:, 0:130], T.hccs[:, 0:130], T.hc[:, :], 130)
+        mm(0, 130, *W(1), T.hcc[:, 0:130], T.hccs[:, 0:130], "wc1 " + both("hcc"))
+        mm(1, 130, *W(2), T.hcc[:, 0:130], T.hccs[:, 0:130], "wc1 " + both("hcc"))
+        scan("#0 zz", "pc", T.pc[:, :], bank(0), T.zz[:, 0:128], 0.0, op.add, op.add, n=128)
+        for c in range(3):
+            count("pc kb%d" % c, "acc%d" % c, T.pc[:, :], AF.Sign, T.kb[:, c:c + 1], -1.0, T.acc[:, c:c + 1])
+        ts("pc kb3 lez", "le", T.le[:, 0:128], T.pc[:, :], T.kb[:, 3:4], 2.0, op.is_le, op.mult)
+        red("le lez", "acc3", T.acc[:, 3:4], T.le[:, 0:129], op.add, n=129)
+        ts("acc0 acc1 acc2 acc3", "oslot", T.oslot[:, 0:4], T.acc[:, 0:4], 0.5, 64.0, op.mult, op.add)
+        pick(u[:, SO:SO + 64], us[:, SO:SO + 64], cd[:, 0:130], cds[:, 0:130], T.oslot[:, 0:4],
+             "cand%d" % t, "cand%ds" % t, "slot%d" % t, "slot%ds" % t, "oslot", 64)
+        at = lambda r: SO + 64 * ((h - pair[r]) % len(grp))
+        spread("c%d" % t, "slot%d" % t, u[:, SO:SO + 64].bitcast(dt.uint8), lambda r: u[:, at(r):at(r) + 64].bitcast(dt.uint8),
+               tag="cc%d" % t)
+        spread("c%d" % t, "slot%ds" % t, us[:, SO:SO + 64], lambda r: us[:, at(r):at(r) + 64], after=("cc%d" % t,))
         arrive("c%d" % t, 2 * from_mates, "land%d land%ds" % (t, t))
         halves = (0, 1) if t == 0 else (own,)
-        tt("#7 fra", "tg", T.tg[:, :], bank(7), T.fra[:, :], op.mult, n=128)
-        for e in halves:
-            src, nm = ((T.clo, "clo"), (T.chi, "chi"))[e]
-            count("%s kb4" % nm, "ta%d" % e, src[:, :], AF.Sign, T.kb[:, 4:5], -1.0, T.ta[:, e:e + 1])
-            ts("tg cp%d" % e, "ep%d" % e, T.ep[:, 128 * e:128 * e + 128], T.tg[:, :], T.cc[:, e:e + 1], None, op.is_equal)
-            scan("ep%d zz" % e, "co%d" % e, T.co[:, 128 * e:128 * e + 128], T.ep[:, 128 * e:128 * e + 128], T.zz[:, 0:128],
-                 0.0, op.max, op.add)
-            count("co%d" % e, "un%d" % e, T.co[:, 128 * e:128 * e + 128], AF.Identity, 1.0, -2.0, T.un[:, e:e + 1])
-            tt("un%d ta%d" % (e, e), "jg%d" % e, T.jg[:, e:e + 1], T.un[:, e:e + 1], T.ta[:, e:e + 1], op.is_lt)
-            ts("un%d cd%d" % (e, e), "jd%d" % e, T.jd[:, e:e + 1], T.un[:, e:e + 1], 0.5, T.cc[:, 4 + e:5 + e], op.mult, op.add)
-            ts("jd%d jg%d cl%d" % (e, e, e), "l3%d" % e, T.l3[:, e:e + 1], T.jd[:, e:e + 1], T.jg[:, e:e + 1],
-               T.cc[:, 2 + e:3 + e], op.mult, op.add)
         for i, e in enumerate(halves):
-            ts("dg l3%d" % e, "o3%d" % i, T.o3[:, 8 * i:8 * i + 8], T.dg[:, :], T.l3[:, e:e + 1], None, op.mult)
-        v, an = T.vv[:, t:t + 1], T.an[:, t:t + 1]
-        tt("eq " + VD, "pv", T.pv[:, :], T.eq[:, :], T.vd[:, :], op.mult)
-        red("pv", "v%d" % t, v, T.pv[:, :], op.max)
-        cp("v%d" % t, "bi0", T.bi[:, 0:1], v)
-        ts("bi0", "bi1", T.bi[:, 1:2], T.bi[:, 0:1], 255, None, op.bitwise_and)
-        cp("bi1", "kk1", T.kk[:, 1:2], T.bi[:, 1:2])
-        ts("tri v%d" % t, "triv", T.triv[:, :], T.tri[:, :], v, None, op.mult, n=128)
-        tt("#0 triv", "eqt", T.eqt[:, :], bank(0), T.triv[:, :], op.is_equal, n=128)
-        red("eqt", "kk0", T.kk[:, 0:1], T.eqt[:, :], op.add, n=128)
-        ts("kk0", "an%d" % t, an, T.kk[:, 0:1], float(E), None, op.is_lt)
-        ts("kk0 kk1 nold", "kk2", T.kk[:, 2:3], T.kk[:, 0:1], T.kk[:, 1:2], T.kb[:, 6:7], op.add, op.add)
-        ts("kk2 an%d old" % t, "kk3", T.kk[:, 3:4], T.kk[:, 2:3], an, T.kb[:, 5:6], op.mult, op.add)
-        ts("dg kk3", "o2", T.o2[:, :], T.dg[:, :], T.kk[:, 3:4], None, op.mult)
-        gather("o2 wina hlz", "hl0", T.hl[:, 0:128], T.wina[:, :], T.o2[:, 0:8], 128)
-        ts(VD + " v%d" % t, "oh%d" % t, T.oh[:, 8 * t:8 * t + 8], T.vd[:, :], v, None, op.is_equal)
-        ts("an%d" % t, "ws%d" % t, T.wv[:, t:t + 1], an, 2.0, -1.0, op.mult, op.add)
-        ts("an%d" % t, "wb%d" % t, T.wv[:, 2 + t:3 + t], an, -1.0, None, op.add)
-        ts("oh%d ws%d" % (t, t), "og%d" % t, T.og[:, 8 * t:8 * t + 8], T.oh[:, 8 * t:8 * t + 8], T.wv[:, t:t + 1], None, op.mult)
+            ne, sm = T.ne[:, 64 * i:64 * i + 64], T.sm[:, 64 * i:64 * i + 64]
+            do("S", "fra fraz oslot npl", "ne%d" % i,
+               lambda ne=ne, e=e: S.activation(ne, T.fra[:, 0:144].indirect(T.oslot[:, 0:4]), AF.Abs,
+                                               bias=T.npl[:, e:e + 1], scale=512.0), 0.17)
+            scan("ne%d one pf pf4" % i, "sm%d" % i, sm, T.one[:, :], ne, place[e], op.add, op.min)
+            ts("sm%d z8" % i, "om%d" % i, T.om[:, 8 * i:8 * i + 8], T.z8[:, :], T.sm[:, 64 * i + 63:64 * i + 64], None, op.add)
+            gather("VS"[i], "om%d hmz%d %s" % (i, i, TBM), "hm%d" % i, T.hm[:, 512 * i:512 * i + 512:4], T.tb[:, TM:TI + 256],
+                   T.om[:, 8 * i:8 * i + 8], 128)
+        n = len(halves)
+        quant(" ".join("hm%d hmz%d" % (i, i) for i in range(n)), both("hmc"), T.hmc[:, 0:128 * n], T.hmcs[:, 0:128 * n],
+              T.hm[:, 0:512 * n], 128 * n)
+        for i in range(n):
+            k = (2, 0)[i]
+            mm(k, 128, T.hmc[:, 128 * i:128 * i + 128], T.hmcs[:, 128 * i:128 * i + 128], T.xc[:, :], T.xcs[:, :], "xc " + both("hmc"))
+            cp("#%d" % k, "lmem%d" % i, T.lmem[:, 8 * i:8 * i + 8], bank(k, 8))
+        cn, uu = T.cn[:, t:t + 1], T.uu[:, t:t + 1]
+        ts("tri w1%d" % t, "triv", T.triv[:, :], T.tri[:, :], w1, None, op.mult)
+        act("e8 kb6 w1%d" % t, "b8", T.b8[:, :], T.e8[:, :], AF.Identity, bias=T.kb[:, 6:7], scale=w1, n=8)
+        tt("#1 triv", "eqt", T.eqt[:, :], bank(1), T.triv[:, :], op.is_equal, n=128)
+        red("eqt", "cn%d" % t, cn, T.eqt[:, :], op.add, n=128)
+        ts("cn%d old" % t, "uu%d" % t, uu, cn, float(E), T.pf[:, 5:6], op.is_ge, op.mult)
+        ts("b8 cn%d uu%d" % (t, t), "oq", T.oq[:, :], T.b8[:, :], cn, uu, op.add, op.max)
+        gather("S", "oq hqz0 " + TBQ, "hq", T.hq[:, 0:512:4], T.tb[:, :], T.oq[:, 0:8], 128)
+        quant("hq hqz0", both("hqc"), T.hqc[:, :], T.hqcs[:, :], T.hq[:, :])
+        mm(7, 128, T.hqc[:, :], T.hqcs[:, :], T.xc[:, :], T.xcs[:, :], "xc " + both("hqc"))
+        cp("#7", "lq", T.lq[:, :], bank(7, 8))
+        ts("odr0 odr1 w1%d" % t, "oh%d" % t, T.oh[:, 8 * t:8 * t + 8], T.odr[:, :], w1, None, op.is_equal)
+        act("cn%d kb4" % t, "ws%d" % t, T.wv[:, t:t + 1], cn, AF.Sign, bias=T.kb[:, 4:5], scale=-1.0, n=1)
+        NEW = "slot%d land%d qown%d qfar%d" % (t, t, t, t)
+        NEWS = "slot%ds land%ds qown%ds qfar%ds" % (t, t, t, t)
         if t == 0:
-            gather("o30 wina hlz", "hl1", T.hl[:, 128:256], T.wina[:, :], T.o3[:, 0:8], 128)
-            do("S", "o31 wina hlz", "hl2",
-               lambda: S.activation(T.hl[:, 256:384], T.wina[:, :].indirect(T.o3[:, 8:16]), AF.Copy), 0.23)
-            wrapped(1, 0, 96, T.ol[:, 0:24], "ol", "hl", T.hlc, T.hlcs, T.hl, "hl0 hl1 hl2")
-            pick(T.mc1[:, 0:256], T.mc1s[:, 0:256], mc[:, 0:386], mcs[:, 0:386], T.ol[:, 8:24],
-                 MEM + " cand0", MEMS + " cand0s", "mcown1 mcfar1", "mcown1s mcfar1s", "ol", 256)
-            pick(T.ld1[:, QO:QO + 128], T.ld1s[:, QO:QO + 128], ld[:, 0:384], lds[:, 0:384], T.ol[:, 0:8],
-                 "slot0 land0 qown0 qfar0", "slot0s land0s qown0s qfar0s", "qown1 qfar1", "qown1s qfar1s", "ol", 128)
+            for i in range(2):
+                pick(T.u1[:, 128 * i:128 * i + 128], T.u1s[:, 128 * i:128 * i + 128], u[:, 0:SO + 64], us[:, 0:SO + 64],
+                     T.lmem[:, 8 * i:8 * i + 8], MEM + " slot0", MEMS + " slot0s", "mem1%d" % i, "mem1%ds" % i, "lmem%d" % i, 128)
+            pick(T.u1[:, QO:QO + 128], T.u1s[:, QO:QO + 128], u[:, SO:QO + 128], us[:, SO:QO + 128], T.lq[:, 0:8],
+                 NEW, NEWS, "qown1 qfar1", "qown1s qfar1s", "lq", 128)
         else:
-            wrapped(1, 0, 32, T.ol[:, 0:8], "ol", "hl", T.hlc, T.hlcs, T.hl, "hl0 hl1 hl2")
-            gather("o30 wina hmz", "hm0", T.hm[:, 0:128], T.wina[:, :], T.o3[:, 0:8], 128)
-            wrapped(2, 96, 32, T.om[:, 0:8], "om", "hm", T.hmc, T.hmcs, T.hm, "hm0")
-            pick(T.fm[:, :], T.fms[:, :], mc[:, 0:386], mcs[:, 0:386], T.om[:, 0:8],
-                 MEM + " cand1", MEMS + " cand1s", "fm", "fms", "om", 128)
-            dma("Y", "u0", "fm", "out0", T.oc[:, :], T.fm[:, :].bitcast(dt.uint8))
+            pick(T.fm[:, :], T.fms[:, :], u[:, 0:SO + 64], us[:, 0:SO + 64], T.lmem[:, 0:8],
+                 MEM + " slot1", MEMS + " slot1s", "fm", "fms", "lmem0", 128)
+            dma("Y", "o0", "fm", "out0", T.oc[:, :], T.fm[:, :].bitcast(dt.uint8))
             for k in range(4):
-                dma("Y", "u%d" % (1 + k), "fms", "out%d" % (1 + k), T.osc[4 * k:4 * k + 4, :], T.fms[32 * k:32 * k + 4, :])
+                dma("Y", "o%d" % (1 + k), "fms", "out%d" % (1 + k), T.osc[4 * k:4 * k + 4, :], T.fms[32 * k:32 * k + 4, :])
+            pick(T.qf[:, :], T.qfs[:, :], u[:, SO:QO + 128], us[:, SO:QO + 128], T.lq[:, 0:8], NEW, NEWS, "qf", "qfs", "lq", 128)
 
     one_round(0)
     one_round(1)
-    pick(T.qf[:, :], T.qfs[:, :], T.ld1[:, 0:384], T.ld1s[:, 0:384], T.ol[:, 0:8],
-         "slot1 land1 qown1 qfar1", "slot1s land1s qown1s qfar1s", "qf", "qfs", "ol", 128)
     mm(3, 128, T.wq[:, :], T.wqs[:, :], T.qf[:, :], T.qfs[:, :], "wq wqs qf qfs")
     act("#3", "ysb", T.ysb[:, :], bank(3), AF.Copy)
-    dma("S", "u7", "ysb", "outy", T.y[:, :], T.ysb[:, :])
+    dma("S", "o7", "ysb", "outy", T.y[:, :], T.ysb[:, :])
     for t, nt, nk in ((0, T.lm1, "lmn1 lmz1 lma1"), (1, T.nl, "nlo nlz nla")):
-        tt("og%d %s" % (t, nk), "oh%d" % t, T.oh[:, 8 * t:8 * t + 8], T.og[:, 8 * t:8 * t + 8], nt[:, 1:16:2], op.mult)
-        red("oh%d" % t, "wg%d" % t, T.wv[:, 4 + t:5 + t], T.oh[:, 8 * t:8 * t + 8], op.add)
-        tt("wg%d wb%d" % (t, t), "wo%d" % t, T.wo[:, t:t + 1], T.wv[:, 4 + t:5 + t], T.wv[:, 2 + t:3 + t], op.add)
-        dma("Y", "u%d" % (5 + t), "wo%d" % t, "out%d" % (5 + t), T.wi[t:t + 1, :], T.wo[:, t:t + 1])
+        tt("oh%d %s" % (t, nk), "og%d" % t, T.og[:, 8 * t:8 * t + 8], T.oh[:, 8 * t:8 * t + 8], nt[:, 1:16:2], op.mult)
+        act("og%d ws%d kb5" % (t, t), "wo%d oh%d" % (t, t), T.oh[:, 8 * t:8 * t + 8], T.og[:, 8 * t:8 * t + 8], AF.Identity,
+            T.kb[:, 5:6], T.wv[:, t:t + 1], T.wo[:, t:t + 1], n=8)
+        dma("Y", "o%d" % (5 + t), "wo%d" % t, "out%d" % (5 + t), T.wi[t:t + 1, :], T.wo[:, t:t + 1])
 
     cnt, known = {}, {q: {} for q in queue}
     wr, rd = {}, {}

@@ -8,16 +8,16 @@ for _n, _w in (("xq", 128), ("wq", 128), ("rx", 32), ("rm", 128), ("u0", 640), (
                ("hcc", 136), ("hqc", 128), ("hmc", 256)):
     SCRATCH[_n] = ("sbuf", [128, _w], F8)
     SCRATCH[_n + "s"] = ("sbuf", [128, _w], "uint8")
-for _n, _w in (("xt", 512), ("mt", 512), ("wt", 512), ("ha", 512), ("hc", 520), ("hq", 512), ("hm", 1024), ("ht", 520),
-               ("wtile", 1536), ("et", 2048), ("xtile", 512), ("zz", 512), ("jf", 256), ("jm", 128), ("jh", 128), ("tgt", 128),
-               ("c32", 32), ("r32", 32), ("win1", 16), ("tb", 704), ("ida", 128), ("idb", 128), ("ba", 32), ("bb", 32),
-               ("bc", 64), ("tri", 128), ("idn", 128), ("jk", 5120), ("fra", 144), ("pc", 128), ("le", 136), ("eqt", 128),
-               ("triv", 128), ("ne", 128), ("one", 64)):
+for _n, _w in (("xt", 512), ("mt", 512), ("wt", 512), ("hc", 520), ("hm", 1024), ("ht", 520),
+               ("wtile", 520), ("et", 520), ("xtile", 512), ("zz", 512), ("jf", 256), ("jm", 128), ("tgt", 128),
+               ("c32", 32), ("r32", 32), ("win1", 32), ("tb", 704), ("ida", 128), ("idb", 128), ("ba", 32), ("bb", 32),
+               ("bc", 64), ("tri", 128), ("jk", 5120), ("fra", 144), ("pc", 128), ("le", 136),
+               ("eqt", 128), ("triv", 128), ("ne", 128), ("one", 64)):
     SCRATCH[_n] = ("sbuf", [128, _w], "bfloat16")
-for _n, _w in (("pf", 8), ("rmk", 12), ("dg", 8), ("kb", 8), ("odr", 8), ("lm0", 16), ("lm1", 16), ("nl", 16), ("cm", 256),
-               ("aa", 4), ("lw", 2), ("nm", 2), ("c2", 2), ("mx", 2), ("cx", 16), ("w1", 2), ("acc", 4), ("b8", 8), ("cn", 2),
-               ("uu", 2), ("sm", 128), ("wv", 2), ("oh", 16), ("og", 16), ("wo", 2), ("ysb", 128), ("z8", 8), ("e8", 8),
-               ("npl", 2)):
+for _n, _w in (("pf", 8), ("rmk", 16), ("dg", 8), ("dgm", 8), ("kb", 4), ("odr", 8), ("lm0", 16), ("lm1", 16), ("nl", 16),
+               ("cm", 256), ("aa", 4), ("lw", 2), ("nm", 2), ("c2", 2), ("mx", 4), ("cx", 16), ("w1", 2), ("acc", 4), ("b8", 8),
+               ("cn", 2), ("uu", 2), ("sm", 128), ("wv", 2), ("oh", 16), ("og", 16), ("wo", 2), ("ysb", 128), ("z8", 8),
+               ("e8", 8), ("npl", 2)):
     SCRATCH[_n] = ("sbuf", [128, _w], "float32")
 for _n, _w in (("ox", 2), ("oaw", 8), ("oc8", 8), ("oslot", 4), ("oq", 8), ("om", 16), ("lq", 8), ("lmem", 16)):
     SCRATCH[_n] = ("sbuf", [128, _w], "uint16")
@@ -28,9 +28,11 @@ A = 16
 E = 32
 SO, QO = 256, 512
 TM, TI = 256, 320
-WAKE = 0.13
+WAKE = 0.22
 DMA, CALL = 1.9, 0.35
-HOP = {"xa": 4.5, "ma": 4.3, "m0": 1.3, "m1": 1.3, "nn": 1.5, "c0": 2.0, "c1": 2.0}
+HOP = {"xa": 4.5, "ma": 4.3, "m0": 0.7, "m1": 0.7, "nn": 1.5, "c0": 1.3, "c1": 1.3}
+GIVEN = ("hac cx@ oaw f7@ oc8 mp@ hcg w1@ hcc triv ht0 ht2 pc cand@ le eqt acc3 cn@ oslot slot@",
+         "w0@ mp@s hcg2 fra ht1 ht3 b8 acc0 acc1 acc2 slot@s")
 
 
 def plan(T, topo):
@@ -113,21 +115,32 @@ def note(e, r, w, wr, rd):
         rd.setdefault(k, []).append(e)
 
 
-def in_order(ops):
+def in_order(ops, chains):
     n = len(ops)
     wr, rd, pred = {}, {}, []
-    last = {}
+    last, soft = {}, []
     for i, o in enumerate(ops):
         p = {e[0] for e in conflicts(o["q"], o["r"], o["w"], wr, rd, False, True)}
         p.update(last[s] for s in o["after"])
+        soft.append({last[s] for s in o["after"] if ops[last[s]]["q"] == o["q"]})
         if o["tag"]:
             last[o["tag"]] = i
         pred.append(p)
         note((i, 0, o["q"]), o["r"], o["w"], wr, rd)
+    for chain in chains:
+        for a, b in zip(chain, chain[1:]):
+            if a not in pred[b]:
+                pred[b].add(a)
+                soft[b].add(a)
     prio = [o["dur"] for o in ops]
-    for i in range(n - 1, -1, -1):
-        for p in pred[i]:
-            prio[p] = max(prio[p], ops[p]["dur"] + WAKE + prio[i])
+    moved = True
+    while moved:
+        moved = False
+        for i in range(n - 1, -1, -1):
+            for p in pred[i]:
+                v = ops[p]["dur"] + (0.0 if p in soft[i] else WAKE) + prio[i]
+                if v > prio[p] + 1e-9:
+                    prio[p], moved = v, True
     free, done, out = {}, {}, []
     succ = [[] for _ in range(n)]
     wait = [len(p) for p in pred]
@@ -141,7 +154,7 @@ def in_order(ops):
         for i in sorted(ready):
             byq.setdefault(ops[i]["q"], []).append(i)
         for q, c in byq.items():
-            st = {i: max([free.get(q, 0.0)] + [done[p] + WAKE for p in pred[i]]) for i in c}
+            st = {i: max([free.get(q, 0.0)] + [done[p] + (0.0 if p in soft[i] else WAKE) for p in pred[i]]) for i in c}
             b = min(c, key=lambda i: (st[i], -prio[i], i))
             better = [i for i in c if prio[i] > prio[b] and st[i] < st[b] + ops[b]["hold"] - 0.03]
             if better:
@@ -181,14 +194,14 @@ def rank_program(g, core, T, topo):
         ops.append({"q": q, "r": r.split(), "w": w.split(), "call": call, "sem": sem, "inc": inc, "dur": dur,
                     "hold": dur if hold is None else hold, "acc": acc, "after": after, "tag": tag})
 
-    def do(q, r, w, call, dur, acc=False):
-        add(q, r, w, call, q, 1, dur, acc=acc)
+    def do(q, r, w, call, dur):
+        add(q, r, w, call, q, 1, dur)
 
     def ew(n):
         return max(64, n) * 0.001
 
-    def dma(q, sem, r, w, o, i):
-        add(q, r, w, lambda: queue[q].dma_start(o, i), sem, 16, DMA, 0.06)
+    def dma(q, sem, r, w, o, i, dur=DMA):
+        add(q, r, w, lambda: queue[q].dma_start(o, i), sem, 16, dur, 0.06)
 
     def send(sem, r, parts, after=(), tag=None, dur=CALL):
         add("G", r, "", lambda: fused(sem, parts), None, 0, dur, after=after, tag=tag or sem)
@@ -236,6 +249,9 @@ def rank_program(g, core, T, topo):
     def fill(w, ap, c, n=8):
         do("V", "", w, lambda: V.memset(ap, c), ew(n))
 
+    def put(w, ap, c, n):
+        act("zz", w, ap, T.zz[:, 0:n], AF.Identity, bias=c, n=n)
+
     def pick(out, outs, win, wins, off, r, rs, w, ws, ro, n):
         do("V", r + " " + ro, w, lambda: V.tensor_copy(out.bitcast(dt.uint32), win.bitcast(dt.uint32).indirect(off)), 0.055 + n * 0.0015)
         do("S", rs + " " + ro, ws, lambda: S.activation(outs, wins.indirect(off), AF.Copy), 0.07 + n * 0.0015)
@@ -266,16 +282,14 @@ def rank_program(g, core, T, topo):
         send(sem, r, [(src, [(cores[q], dst(q)) for q in off_mates], eoff), (src, [(cores[q], dst(q)) for q in on_mates], eon)],
              after, tag)
 
-    def iota(w, ap, pat, n, base=0, mul=0, flag=True, late=False):
+    def iota(w, ap, pat, n, base=0, mul=0, flag=True):
         if flag:
             do("G", "", w, lambda: g.iota(ap, pat, base, mul, allow_small_or_imprecise_dtypes=True), 0.15 + 0.002 * n)
         else:
             do("G", "", w, lambda: g.iota(ap, pat, base, mul), 0.15 + 0.002 * n)
-        if late:
-            ops[-1]["after"] = ("last",)
 
-    dma("Y", "dx", "", "xt", T.xt[:, 0:64], T.x[:, :])
-    dma("S", "dm", "", "mt", T.mt[:, :], T.me[:, :])
+    dma("Y", "dx", "", "xt", T.xt[:, 0:64], T.x[:, :], 1.3)
+    dma("Y", "dm", "", "mt", T.mt[:, :], T.me[:, :], 1.6)
     dma("Y", "dw", "", "wt", T.wt[:, :], T.w[:, :])
     fill("xz", T.xt[:, 64:512], 0.0, 224)
     quant("xt xz", "xq xqs", T.xq[:, 0:128], T.xqs[:, 0:128], T.xt[:, :])
@@ -299,13 +313,12 @@ def rank_program(g, core, T, topo):
     iota("pint0", T.pint[:, 0:1], [[0, 1]], 1, 0, 1, False)
     iota("jm", T.jm[:, :], [[0, 8], [1, 16]], 128)
     iota("jf", T.jf[:, 0:128], [[1, 128]], 128)
-    iota("jf2", T.jf[:, 128:256], [[1, 128]], 128, 128, late=True)
-    iota("jh", T.jh[:, :], [[1, 8], [0, 16]], 128, late=True)
-    iota("c32", T.c32[:, :], [[-1, 4], [0, 8]], 32, 3, late=True)
-    iota("r32", T.r32[:, :], [[0, 4], [-1, 8]], 32, 7, late=True)
+    iota("c32", T.c32[:, :], [[-1, 4], [0, 8]], 32, 3)
+    iota("r32", T.r32[:, :], [[0, 4], [-1, 8]], 32, 7)
+    act("jf", "jf2", T.jf[:, 128:256], T.jf[:, 0:128], AF.Identity, bias=128.0)
     fill("zz", T.zz[:, :], 0.0, 256)
     fill("z8", T.z8[:, :], 0.0)
-    fill("one", T.one[:, :], 1.0)
+    put("one", T.one[:, :], 1.0, 64)
     ts("pint0", "p16i", T.pint[:, 1:2], T.pint[:, 0:1], 15, None, op.bitwise_and)
     ts("pint0", "g16i", T.pint[:, 2:3], T.pint[:, 0:1], 4, None, op.logical_shift_right)
     ts("pint0", "p8i", T.pint[:, 3:4], T.pint[:, 0:1], 7, None, op.bitwise_and)
@@ -314,11 +327,11 @@ def rank_program(g, core, T, topo):
     pick(T.u0[:, qa:qa + A], T.u0s[:, qa:qa + A], T.xq[:, 0:128], T.xqs[:, 0:128], T.ox[:, 0:1],
          "xq", "xqs", "qown0", "qown0s", "ox", 16)
     pf, p16, g16, p8 = T.pf[:, 0:1], T.pf[:, 1:2], T.pf[:, 2:3], T.pf[:, 3:4]
-    ts("pf", "pf4", T.pf[:, 4:5], pf, 128.0, None, op.add)
-    ts("pf", "old", T.pf[:, 5:6], pf, float(TI + QO - SO), None, op.add)
+    act("pf", "pf4", T.pf[:, 4:5], pf, AF.Identity, bias=128.0, n=1)
+    act("pf", "old", T.pf[:, 5:6], pf, AF.Identity, bias=float(TI + QO - SO), n=1)
     ts("pf", "p161", T.pf[:, 6:7], p16, 1.0, None, op.add)
     place = (pf, T.pf[:, 4:5])
-    ts("pf pf4", "npl", T.npl[:, :], T.pf[:, 0:5:4], -512.0, None, op.mult)
+    act("pf pf4", "npl", T.npl[:, :], T.pf[:, 0:5:4], AF.Identity, scale=-512.0, n=2)
     rm = lambda k: T.rmk[:, k:k + 1]
     ts("jm pf", "rm", T.rmk[:, 0:3], T.jm[:, 0:3], p16, None, op.is_equal)
     ts("rm", "rm3", rm(3), rm(0), 4.0, None, op.mult)
@@ -330,51 +343,47 @@ def rank_program(g, core, T, topo):
     ts("rm", "rm9", rm(9), rm(0), 16.0, rm(1), op.mult, op.add)
     ts("rm rm9", "rm10", rm(10), rm(2), 128.0, rm(9), op.mult, op.add)
     for t in range(2):
-        fill("lmz%d" % t, T["lm%d" % t][:, 4 * h:4 * h + 4], 0.0)
-    fill("nlz", T.nl[:, 4 * h:4 * h + 4], 0.0)
+        put("lmz%d" % t, T["lm%d" % t][:, 4 * h:4 * h + 4], 0.0, 4)
+    put("nlz", T.nl[:, 4 * h:4 * h + 4], 0.0, 4)
     fill("cxz", T.cx[:, 0:16:8], -1e29)
-    fill("c2", T.c2[:, :], 128.0 * lo + 0.5)
-    fill("fraz", T.fra[:, 128:144], -1.0)
-    fill("lez", T.le[:, 128:129], -128.0)
-    fill("kb4", T.kb[:, 4:5], E - 0.5)
-    fill("kb5", T.kb[:, 5:6], -0.5 / N)
-    fill("kb6", T.kb[:, 6:7], -float(E))
-    fill("e8", T.e8[:, :], float(E))
-    ts("jm", "odr1", T.odr[:, 1:8], T.jm[:, 1:8], 0.0, None, op.add)
-    fill("odr0", T.odr[:, 0:1], float(N))
-    for nm, n in (("ha", 1), ("hc", 1), ("hq", 1), ("hm", 2)):
+    put("c2", T.c2[:, :], 128.0 * lo + 0.5, 2)
+    put("fraz", T.fra[:, 128:144], -1.0, 16)
+    put("lez", T.le[:, 128:129], -128.0, 1)
+    put("e8", T.e8[:, :], float(E), 8)
+    act("jm", "odr1", T.odr[:, 1:8], T.jm[:, 1:8], AF.Copy, n=7)
+    put("odr0", T.odr[:, 0:1], float(N), 1)
+    for nm, n in (("hc", 1), ("hm", 2)):
         for i in range(n):
             act("zz", "%sz%d" % (nm, i), T[nm][:, 512 * i:512 * i + 512], T.zz[:, 0:512], AF.Copy, n=512)
     fill("htz", T.ht[:, 512:520], 0.0)
     ts("jm pf", "dg", T.dg[:, :], T.jm[:, 0:8], g16, None, op.is_equal)
-    ts("jf pf", "idn", T.idn[:, :], T.jf[:, 0:128], pf, None, op.is_equal)
     ts("jf pf", "tri", T.tri[:, :], T.jf[:, 0:128], pf, None, op.is_lt)
-    ts("jm p161", "win1", T.win1[:, :], T.jm[:, 0:16], T.pf[:, 6:7], None, op.is_equal)
+    ts("jf p161", "win1", T.win1[:, :], T.jf[:, 0:32], T.pf[:, 6:7], None, op.is_equal)
+    ts("jm pf", "dgm", T.dgm[:, :], T.jm[:, 0:8], g16, 16.0, op.not_equal, op.mult)
+    fill("etz", T.et[:, :], 0.0, 260)
+    ts("jf pf etz", "et", T.et[:, 3:515:4], T.jf[:, 0:128], pf, 0.5, op.is_equal, op.mult)
     for b in range(4):
-        act("zz", "etz%d" % b, T.et[:, 512 * b:512 * b + 512], T.zz[:, :], AF.Copy, n=512)
-        ts("idn etz%d" % b, "et%d" % b, T.et[:, 512 * b + b:512 * b + 512:4], T.idn[:, :], 0.5, None, op.mult)
-    for b in (0, 2):
-        quant("etz%d etz%d et%d et%d" % (b, b + 1, b, b + 1), "ec%d" % b, T.ec[:, 128 * b:128 * b + 256], T.ecs[:, 128 * b:128 * b + 256],
-              T.et[:, 512 * b:512 * b + 1024], 256)
+        quant("etz et", "ec%d" % b, T.ec[:, 128 * b:128 * b + 128], T.ecs[:, 128 * b:128 * b + 128], T.et[:, 3 - b:515 - b])
     for c in range(4):
-        ts("pf", "kb%d" % c, T.kb[:, c:c + 1], p8, -1.0, E - 0.5 - 8.0 * c, op.mult, op.add)
-    for i in range(3):
-        fill("wz%d" % i, T.wtile[:, 512 * i:512 * i + 512], 0.0, 256)
-    ts("jm pf wz0", "w0a", T.wtile[:, 0:512:4], T.jm[:, :], p16, 16.0, op.is_equal, op.mult)
-    ts("jm pf wz0", "w0b", T.wtile[:, 1:512:4], T.jm[:, :], p16, None, op.is_equal)
+        act("pf", "kb%d" % c, T.kb[:, c:c + 1], p8, AF.Identity, bias=E - 0.5 - 8.0 * c, scale=-1.0, n=1)
+    fill("wz", T.wtile[:, 512:520], 0.0)
+    ts("jm pf", "w0a", T.wtile[:, 0:512:4], T.jm[:, :], p16, 16.0, op.is_equal, op.mult)
+    ts("jm pf", "w0b", T.wtile[:, 1:512:4], T.jm[:, :], p16, None, op.is_equal)
     ts("jm", "tgt", T.tgt[:, :], T.jm[:, :], 8.0, float(hi - lo), op.is_ge, op.mult)
-    ts("tgt pf wz1", "w1a", T.wtile[:, 512:1024:4], T.tgt[:, :], float(lo), p16, op.add, op.is_equal)
-    ts("zz p161 wz2", "w2a", T.wtile[:, 1024:1536:4], T.zz[:, 0:128], T.pf[:, 6:7], None, op.add)
-    quant("wz0 w0a w0b", "wc0", T.wc[:, 0:128], T.wcs[:, 0:128], T.wtile[:, 0:512])
-    quant("wz1 wz2 w1a w2a", "wc1", T.wc[:, 128:384], T.wcs[:, 128:384], T.wtile[:, 512:1536], 256)
+    ts("tgt pf", "w1a", T.wtile[:, 2:512:4], T.tgt[:, :], float(lo), p16, op.add, op.is_equal)
+    ts("zz p161", "w2a", T.wtile[:, 3:512:4], T.zz[:, 0:128], T.pf[:, 6:7], None, op.add)
+    for i, z in enumerate((0, 2, 3)):
+        quant("wz w0a w0b w1a w2a", "wc%d" % i, T.wc[:, 128 * i:128 * i + 128], T.wcs[:, 128 * i:128 * i + 128], T.wtile[:, z:z + 512])
     fill("xtz", T.xtile[:, :], 0.0, 256)
     ts("dg rm10 xtz", "xta", T.xtile[:, 0:32:4], T.dg[:, :], rm(10), None, op.mult)
     cp("xt xtz", "xtb", T.xtile[:, 32:40], T.xt[:, 0:8])
     quant("xtz xta xtb", "xc", T.xc[:, :], T.xcs[:, :], T.xtile[:, :])
     cp("xt", "hcx", T.hc[:, 512:520], T.xt[:, 0:8])
     quant("wt", "wq wqs", T.wq[:, :], T.wqs[:, :], T.wt[:, :])
-    act("jh rm", "ida", T.ida[:, :], T.jh[:, :], AF.Identity, scale=rm(0))
-    act("jm rm", "idb", T.idb[:, :], T.jm[:, :], AF.Identity, scale=rm(1))
+    ts("rm", "rm11", rm(11), rm(0), 0.0625, None, op.mult)
+    ts("rm", "rm12", rm(12), rm(0), -0.0625, rm(1), op.mult, op.add)
+    act("jf rm11", "ida", T.ida[:, :], T.jf[:, 0:128], AF.Identity, scale=rm(11))
+    act("jm rm12", "idb", T.idb[:, :], T.jm[:, :], AF.Identity, scale=rm(12))
     tt("ida idb", "tbi0", T.tb[:, TI:TI + 128], T.ida[:, :], T.idb[:, :], op.add, n=256)
     act("tbi0 rm", "tbi1", T.tb[:, TI + 128:TI + 256], T.tb[:, TI:TI + 128], AF.Identity, bias=rm(2))
     act("tbi0 rm6", "tbi2", T.tb[:, TI + 256:TI + 384], T.tb[:, TI:TI + 128], AF.Identity, bias=rm(6))
@@ -396,7 +405,10 @@ def rank_program(g, core, T, topo):
     def both(nm):
         return " ".join("%s %ss" % (k, k) for k in nm.split())
 
+    chains = []
+
     def one_round(t):
+        first = len(ops)
         u, us = T["u%d" % t], T["u%ds" % t]
         cd, cds = T["cd%d" % t], T["cd%ds" % t]
         mp, mps = T["mp%d" % t], T["mp%ds" % t]
@@ -406,30 +418,34 @@ def rank_program(g, core, T, topo):
         MEM = "mem%d0 mem%d1" % (t, t)
         MEMS = "mem%d0s mem%d1s" % (t, t)
         for e in (own, 1 - own):
-            mm(e, 128, q, qs, u[:, 128 * e:128 * e + 128], us[:, 128 * e:128 * e + 128], Q + " " + both("mem%d%d" % (t, e)))
+            mm(e, 128, q, qs, u[:, 128 * e:128 * e + 128], us[:, 128 * e:128 * e + 128], Q + " " + both("mem%d%d" % (t, e)),
+               tag="sc%d" % t)
             c = 2 * order.index((lo, hi)[e])
             red("#%d lmz%d" % (e, t), "lmo%d%d" % (t, e), lm[:, c:c + 1], bank(e), op.max, n=128)
-        mm(2, 256, q, qs, u[:, 0:256], us[:, 0:256], Q + " " + MEM + " " + MEMS, tag="sc%d" % t)
         OWN = "lmz%d lmo%d0 lmo%d1" % (t, t, t) + (" lmn1" if t else "")
         spread("m%d" % t, OWN, lm[:, 4 * h:4 * h + 4], lambda r: lm[:, 4 * h:4 * h + 4])
         arrive("m%d" % t, from_mates, "lma%d" % t)
         for b in range(4):
-            mm(3 + b, 128, T.ec[:, 128 * b:128 * b + 128], T.ecs[:, 128 * b:128 * b + 128], q, qs, "ec0 ec2 " + Q, True, False,
+            mm(3 + b, 128, T.ec[:, 128 * b:128 * b + 128], T.ecs[:, 128 * b:128 * b + 128], q, qs, "ec%d " % b + Q, True, False,
                after=("sc%d" % t,))
-        scan("#2 zz", "cm", T.cm[:, :], bank(2, 256), T.zz[:, 0:256], -1e29, op.max, op.add, n=256)
+        c = 2 * order.index(lo)
+        scan("#0 zz", "cm0", T.cm[:, 0:128], bank(0), T.zz[:, 0:128], -1e29, op.max, op.add, n=128)
+        scan("#1 zz lmo%d0" % t, "cm", T.cm[:, 128:256], bank(1), T.zz[:, 0:128], lm[:, c:c + 1], op.max, op.add, n=128)
         a, hi16, low = T.aa[:, t:t + 1], T.aa[:, 2 + t:3 + t], T.lw[:, t:t + 1]
-        count("cm", "ah%d" % t, T.cm[:, 15:256:16], AF.Sign, T.cm[:, 255:256], -1.0, hi16, n=16)
-        count("cm", "a%d" % t, T.cm[:, :], AF.Sign, T.cm[:, 255:256], -1.0, a, n=256)
-        ts("dg haz0 ah%d" % t, "hah", T.ha[:, 0:32:4], T.dg[:, :], hi16, None, op.mult)
-        ts("ah%d a%d" % (t, t), "low%d" % t, low, hi16, -16.0, a, op.mult, op.add)
-        ts("dg haz0 low%d" % t, "hal", T.ha[:, 1:32:4], T.dg[:, :], low, None, op.mult)
-        quant("haz0 hah hal", both("hac"), T.hac[:, :], T.hacs[:, :], T.ha[:, :])
+        count("cm cm0", "ah%d" % t, T.cm[:, 15:256:16], AF.Sign, T.cm[:, 255:256], -1.0, hi16, n=16)
+        ops[-1]["tag"] = "ah%d" % t
+        count("cm cm0", "a%d" % t, T.cm[:, :], AF.Sign, T.cm[:, 255:256], -1.0, a, n=256)
+        ops[-1]["after"] = ("ah%d" % t,)
+        ts("z8 hmz0 ah%d" % t, "hm0", T.hm[:, 0:32:4], T.z8[:, :], hi16, None, op.add)
+        ts("ah%d" % t, "low%d" % t, low, hi16, -16.0, None, op.mult)
+        ts("dg hmz0 a%d low%d" % (t, t), "hal", T.hm[:, 1:32:4], T.dg[:, :], a, low, op.mult, op.add)
+        quant("hmz0 hm0 hal", both("hac"), T.hac[:, :], T.hacs[:, :], T.hm[:, 0:512])
         mm(7, 128, *W(0), T.hac[:, :], T.hacs[:, :], "wc0 " + both("hac"))
         cp("#7", "oaw", T.oaw[:, :], bank(7, 8))
         pick(mp[:, :], mps[:, :], u[:, 0:256], us[:, 0:256], T.oaw[:, 0:8], MEM, MEMS, "mp%d" % t, "mp%ds" % t, "oaw", 128)
         for b in range(4):
             mm(3 + b, 128, T.ec[:, 128 * b:128 * b + 128], T.ecs[:, 128 * b:128 * b + 128], mp[:, :], mps[:, :],
-               "ec0 ec2 mp%d mp%ds" % (t, t), False, True)
+               "ec%d mp%d mp%ds" % (b, t, t), False, True)
         for b in range(4):
             if b % 2 == 0:
                 cp("#%d" % (3 + b), "ht%d" % b, T.ht[:, b:512:4], bank(3 + b), n=128)
@@ -449,13 +465,16 @@ def rank_program(g, core, T, topo):
         LM = OWN + " lma%d" % t
         cx, w1 = T.cx[:, 8 * t:8 * t + 8], T.w1[:, t:t + 1]
         scan(LM + " zz cxz", "cx%d" % t, T.cx[:, 8 * t + 1:8 * t + 8], lm[:, 2:16:2], T.zz[:, 0:7], -1e29, op.max, op.add)
-        red(LM, "mx%d" % t, T.mx[:, t:t + 1], lm[:, 0:16:2], op.max)
-        count("cxz cx%d mx%d" % (t, t), "w1%d" % t, cx, AF.Sign, T.mx[:, t:t + 1], -1.0, w1, n=8)
-        ts("dg w1%d" % t, "oc8", T.oc8[:, :], T.dg[:, :], w1, None, op.mult)
-        gather("V", "oc8 hcz0 win1", "hcg", T.hc[:, 0:512:4], T.win1[:, :], T.oc8[:, 0:8], 128)
-        quant("hcg hcz0 hcx", both("hcc"), T.hcc[:, 0:130], T.hccs[:, 0:130], T.hc[:, :], 130)
+        top, w0, f7 = T.cx[:, 8 * t + 7:8 * t + 8], T.mx[:, t:t + 1], T.mx[:, 2 + t:3 + t]
+        count("cxz cx%d" % t, "w0%d" % t, cx, AF.Sign, top, -1.0, w0, n=8)
+        ts(LM + " cx%d" % t, "f7%d" % t, f7, lm[:, 0:1], top, float(N), op.is_gt, op.mult)
+        ts("dgm w0%d f7%d" % (t, t), "oc8", T.oc8[:, :], T.dgm[:, :], w0, f7, op.add, op.max)
+        tt("w0%d f7%d" % (t, t), "w1%d" % t, w1, w0, f7, op.max)
+        gather("V", "oc8 hcz0 win1", "hcg", T.hc[:, 0:256:4], T.win1[:, :], T.oc8[:, 0:4], 64)
+        gather("S", "oc8 hcz0 win1", "hcg2", T.hc[:, 256:512:4], T.win1[:, :], T.oc8[:, 4:8], 64)
+        quant("hcg hcg2 hcz0 hcx", both("hcc"), T.hcc[:, 0:130], T.hccs[:, 0:130], T.hc[:, :], 130)
         mm(0, 130, *W(1), T.hcc[:, 0:130], T.hccs[:, 0:130], "wc1 " + both("hcc"))
-        mm(1, 130, *W(2), T.hcc[:, 0:130], T.hccs[:, 0:130], "wc1 " + both("hcc"))
+        mm(1, 130, *W(2), T.hcc[:, 0:130], T.hccs[:, 0:130], "wc2 " + both("hcc"))
         scan("#0 zz", "pc", T.pc[:, :], bank(0), T.zz[:, 0:128], 0.0, op.add, op.add, n=128)
         for c in range(3):
             count("pc kb%d" % c, "acc%d" % c, T.pc[:, :], AF.Sign, T.kb[:, c:c + 1], -1.0, T.acc[:, c:c + 1])
@@ -472,33 +491,40 @@ def rank_program(g, core, T, topo):
         halves = (0, 1) if t == 0 else (own,)
         for i, e in enumerate(halves):
             ne, sm = T.ne[:, 64 * i:64 * i + 64], T.sm[:, 64 * i:64 * i + 64]
-            do("S", "fra fraz oslot npl", "ne%d" % i,
-               lambda ne=ne, e=e: S.activation(ne, T.fra[:, 0:144].indirect(T.oslot[:, 0:4]), AF.Abs,
-                                               bias=T.npl[:, e:e + 1], scale=512.0), 0.17)
+            won = T.fra[:, 0:144].indirect(T.oslot[:, 0:4])
+            if i:
+                do("S", "fra fraz oslot npl", "ne%d" % i,
+                   lambda ne=ne, e=e, won=won: S.activation(ne, won, AF.Abs, bias=T.npl[:, e:e + 1], scale=512.0), 0.17)
+            else:
+                do("V", "fra fraz oslot pf pf4", "ne%d" % i,
+                   lambda ne=ne, e=e, won=won: V.tensor_scalar(ne, won, place[e], 512.0, op.not_equal, op.mult), 0.15)
             scan("ne%d one pf pf4" % i, "sm%d" % i, sm, T.one[:, :], ne, place[e], op.add, op.min)
             ts("sm%d z8" % i, "om%d" % i, T.om[:, 8 * i:8 * i + 8], T.z8[:, :], T.sm[:, 64 * i + 63:64 * i + 64], None, op.add)
             gather("VS"[i], "om%d hmz%d %s" % (i, i, TBM), "hm%d" % i, T.hm[:, 512 * i:512 * i + 512:4], T.tb[:, TM:TI + 256],
                    T.om[:, 8 * i:8 * i + 8], 128)
-        n = len(halves)
-        quant(" ".join("hm%d hmz%d" % (i, i) for i in range(n)), both("hmc"), T.hmc[:, 0:128 * n], T.hmcs[:, 0:128 * n],
-              T.hm[:, 0:512 * n], 128 * n)
-        for i in range(n):
+        for i in range(len(halves)):
             k = (2, 0)[i]
-            mm(k, 128, T.hmc[:, 128 * i:128 * i + 128], T.hmcs[:, 128 * i:128 * i + 128], T.xc[:, :], T.xcs[:, :], "xc " + both("hmc"))
+            quant("hm%d hmz%d hal" % (i, i), both("hmc%d" % i), T.hmc[:, 128 * i:128 * i + 128], T.hmcs[:, 128 * i:128 * i + 128],
+                  T.hm[:, 512 * i:512 * i + 512])
+            mm(k, 128, T.hmc[:, 128 * i:128 * i + 128], T.hmcs[:, 128 * i:128 * i + 128], T.xc[:, :], T.xcs[:, :],
+               "xc " + both("hmc%d" % i))
             cp("#%d" % k, "lmem%d" % i, T.lmem[:, 8 * i:8 * i + 8], bank(k, 8))
         cn, uu = T.cn[:, t:t + 1], T.uu[:, t:t + 1]
         ts("tri w1%d" % t, "triv", T.triv[:, :], T.tri[:, :], w1, None, op.mult)
-        act("e8 kb6 w1%d" % t, "b8", T.b8[:, :], T.e8[:, :], AF.Identity, bias=T.kb[:, 6:7], scale=w1, n=8)
+        act("e8 w1%d" % t, "b8", T.b8[:, :], T.e8[:, :], AF.Identity, bias=-float(E), scale=w1, n=8)
         tt("#1 triv", "eqt", T.eqt[:, :], bank(1), T.triv[:, :], op.is_equal, n=128)
         red("eqt", "cn%d" % t, cn, T.eqt[:, :], op.add, n=128)
         ts("cn%d old" % t, "uu%d" % t, uu, cn, float(E), T.pf[:, 5:6], op.is_ge, op.mult)
         ts("b8 cn%d uu%d" % (t, t), "oq", T.oq[:, :], T.b8[:, :], cn, uu, op.add, op.max)
-        gather("S", "oq hqz0 " + TBQ, "hq", T.hq[:, 0:512:4], T.tb[:, :], T.oq[:, 0:8], 128)
-        quant("hq hqz0", both("hqc"), T.hqc[:, :], T.hqcs[:, :], T.hq[:, :])
+        gather("S", "oq hcz0 " + TBQ, "hcg hcg2", T.hc[:, 0:512:4], T.tb[:, :], T.oq[:, 0:8], 128)
+        quant("hcg hcg2 hcz0", both("hqc"), T.hqc[:, :], T.hqcs[:, :], T.hc[:, 0:512])
         mm(7, 128, T.hqc[:, :], T.hqcs[:, :], T.xc[:, :], T.xcs[:, :], "xc " + both("hqc"))
         cp("#7", "lq", T.lq[:, :], bank(7, 8))
-        ts("odr0 odr1 w1%d" % t, "oh%d" % t, T.oh[:, 8 * t:8 * t + 8], T.odr[:, :], w1, None, op.is_equal)
-        act("cn%d kb4" % t, "ws%d" % t, T.wv[:, t:t + 1], cn, AF.Sign, bias=T.kb[:, 4:5], scale=-1.0, n=1)
+        ts("odr0 odr1 w1%d slot%d" % (t, t), "oh%d" % t, T.oh[:, 8 * t:8 * t + 8], T.odr[:, :], w1, None, op.is_equal)
+        act("cn%d" % t, "ws%d" % t, T.wv[:, t:t + 1], cn, AF.Sign, bias=E - 0.5, scale=-1.0, n=1)
+        made_by = {o["w"][0]: i for i, o in reversed(list(enumerate(ops))) if i >= first and o["w"]}
+        for names in GIVEN:
+            chains.append([made_by[k.replace("@", str(t))] for k in names.split()])
         NEW = "slot%d land%d qown%d qfar%d" % (t, t, t, t)
         NEWS = "slot%ds land%ds qown%ds qfar%ds" % (t, t, t, t)
         if t == 0:
@@ -510,9 +536,9 @@ def rank_program(g, core, T, topo):
         else:
             pick(T.fm[:, :], T.fms[:, :], u[:, 0:SO + 64], us[:, 0:SO + 64], T.lmem[:, 0:8],
                  MEM + " slot1", MEMS + " slot1s", "fm", "fms", "lmem0", 128)
-            dma("Y", "o0", "fm", "out0", T.oc[:, :], T.fm[:, :].bitcast(dt.uint8))
+            dma("Y", "o0", "fm land1s", "out0", T.oc[:, :], T.fm[:, :].bitcast(dt.uint8))
             for k in range(4):
-                dma("Y", "o%d" % (1 + k), "fms", "out%d" % (1 + k), T.osc[4 * k:4 * k + 4, :], T.fms[32 * k:32 * k + 4, :])
+                dma("Y", "o%d" % (1 + k), "fms land1s", "out%d" % (1 + k), T.osc[4 * k:4 * k + 4, :], T.fms[32 * k:32 * k + 4, :])
             pick(T.qf[:, :], T.qfs[:, :], u[:, SO:QO + 128], us[:, SO:QO + 128], T.lq[:, 0:8], NEW, NEWS, "qf", "qfs", "lq", 128)
 
     one_round(0)
@@ -521,14 +547,14 @@ def rank_program(g, core, T, topo):
     act("#3", "ysb", T.ysb[:, :], bank(3), AF.Copy)
     dma("S", "o7", "ysb", "outy", T.y[:, :], T.ysb[:, :])
     for t, nt, nk in ((0, T.lm1, "lmn1 lmz1 lma1"), (1, T.nl, "nlo nlz nla")):
-        tt("oh%d %s" % (t, nk), "og%d" % t, T.og[:, 8 * t:8 * t + 8], T.oh[:, 8 * t:8 * t + 8], nt[:, 1:16:2], op.mult)
-        act("og%d ws%d kb5" % (t, t), "wo%d oh%d" % (t, t), T.oh[:, 8 * t:8 * t + 8], T.og[:, 8 * t:8 * t + 8], AF.Identity,
-            T.kb[:, 5:6], T.wv[:, t:t + 1], T.wo[:, t:t + 1], n=8)
-        dma("Y", "o%d" % (5 + t), "wo%d" % t, "out%d" % (5 + t), T.wi[t:t + 1, :], T.wo[:, t:t + 1])
+        tt("oh%d slot1 %s" % (t, nk), "og%d" % t, T.og[:, 8 * t:8 * t + 8], T.oh[:, 8 * t:8 * t + 8], nt[:, 1:16:2], op.mult)
+        act("og%d ws%d" % (t, t), "wo%d oh%d" % (t, t), T.oh[:, 8 * t:8 * t + 8], T.og[:, 8 * t:8 * t + 8], AF.Identity,
+            -0.5 / N, T.wv[:, t:t + 1], T.wo[:, t:t + 1], n=8)
+        dma("Y", "o%d" % (5 + t), "wo%d land1s" % t, "out%d" % (5 + t), T.wi[t:t + 1, :], T.wo[:, t:t + 1])
 
     cnt, known = {}, {q: {} for q in queue}
     wr, rd = {}, {}
-    for o in in_order(ops):
+    for o in in_order(ops, chains):
         q = o["q"]
         if o["call"] is None:
             cnt[o["sem"]] = o["inc"]
@@ -555,7 +581,7 @@ def rank_program(g, core, T, topo):
             made.then_inc(T.sem[o["sem"]], o["inc"])
             cnt[o["sem"]] = cnt.get(o["sem"], 0) + o["inc"]
             note((o["sem"], cnt[o["sem"]], q if o["sem"] == q else "dma", dict(known[q])), o["r"], o["w"], wr, rd)
+    g.wait_ge(T.sem.ls, ls[0])
     for s, n in cnt.items():
         if known["G"].get(s, 0) < n:
             g.wait_ge(T.sem[s], n)
-    g.wait_ge(T.sem.ls, ls[0])

@@ -4,35 +4,43 @@ from concourse.mybir import dt, AluOpType, AxisListType, ActivationFunctionType
 F8 = "float8_e4m3fn_x4"
 SCRATCH = {"ps": ("psum", [128, 4096], "float32")}
 for _n, _w in (("xq", 128), ("wq", 128), ("rx", 32), ("rm", 128), ("u0", 640), ("u1", 640), ("qf", 128), ("fm", 128),
-               ("mp0", 128), ("mp1", 128), ("cd0", 160), ("cd1", 160), ("wc", 384), ("ec", 512), ("xc", 128), ("hac", 128),
-               ("hcc", 136), ("hqc", 128), ("hmc", 256)):
+               ("mp0", 128), ("mp1", 128), ("cd0", 160), ("cd1", 160), ("wc", 256), ("ec", 512), ("hac", 128),
+               ("hcc", 136), ("hdc", 144), ("hqc", 128), ("hmc", 128)):
     SCRATCH[_n] = ("sbuf", [128, _w], F8)
-    SCRATCH[_n + "s"] = ("sbuf", [128, _w], "uint8")
-for _n, _w in (("xt", 512), ("mt", 512), ("wt", 512), ("hc", 520), ("hm", 1024), ("ht", 520),
-               ("wtile", 520), ("et", 520), ("xtile", 512), ("zz", 512), ("jf", 256), ("jm", 128), ("tgt", 128),
-               ("c32", 32), ("r32", 32), ("win1", 32), ("tb", 704), ("ida", 128), ("idb", 128), ("ba", 32), ("bb", 32),
-               ("bc", 64), ("tri", 128), ("jk", 5120), ("fra", 144), ("pc", 128), ("le", 136),
-               ("eqt", 128), ("triv", 128), ("ne", 128), ("one", 64)):
+    SCRATCH[_n + "s"] = ("sbuf", [128, max(_w, 128)], "uint8")
+for _n, _w in (("xt", 512), ("mt", 512), ("wt", 512), ("hc", 520), ("hd", 552), ("hm", 512), ("ht", 520),
+               ("wtile", 520), ("et", 520), ("zz", 512), ("jf", 256), ("jm", 128),
+               ("c32", 32), ("r32", 32), ("win1", 32), ("win2", 16), ("tq", 768),
+               ("ba", 32), ("bb", 32), ("bc", 64), ("jk", 5120), ("fra", 144), ("eqt", 128), ("ne", 128), ("one", 128)):
     SCRATCH[_n] = ("sbuf", [128, _w], "bfloat16")
-for _n, _w in (("pf", 8), ("rmk", 16), ("dg", 8), ("dgm", 8), ("kb", 4), ("odr", 8), ("lm0", 16), ("lm1", 16), ("nl", 16),
-               ("cm", 256), ("aa", 4), ("lw", 2), ("nm", 2), ("c2", 2), ("mx", 4), ("cx", 16), ("w1", 2), ("acc", 4), ("b8", 8),
-               ("cn", 2), ("uu", 2), ("sm", 128), ("wv", 2), ("oh", 16), ("og", 16), ("wo", 2), ("ysb", 128), ("z8", 8),
-               ("e8", 8), ("npl", 2)):
+for _n, _w in (("pf", 8), ("rmk", 16), ("dg", 16), ("dgm", 8), ("kb", 4), ("odr", 8), ("lm0", 16), ("lm1", 16), ("nl", 16),
+               ("cm", 256), ("aa", 4), ("nm", 2), ("c2", 2), ("mx", 4), ("cx", 16), ("w1", 2), ("acc", 4), ("b8", 8),
+               ("cn", 2), ("sm0", 64), ("sm1", 64), ("sh0", 64), ("sh1", 64), ("far", 4), ("wv", 2), ("oh", 16), ("og", 16), ("wo", 2), ("ysb", 128), ("z8", 8),
+               ("e8", 8), ("npl", 2), ("off8", 8), ("mrep", 8), ("dv", 8), ("zs", 8),
+               ("hf", 2)):
     SCRATCH[_n] = ("sbuf", [128, _w], "float32")
-for _n, _w in (("ox", 2), ("oaw", 8), ("oc8", 8), ("oslot", 4), ("oq", 8), ("om", 16), ("lq", 8), ("lmem", 16)):
+for _n, _w in (("ox", 2), ("oaw", 8), ("oc8", 8), ("od8", 8), ("oslot", 4), ("oq", 8), ("lq", 8), ("lmem", 16)):
     SCRATCH[_n] = ("sbuf", [128, _w], "uint16")
-SCRATCH["pint"] = ("sbuf", [128, 4], "int32")
+for _n, _w in (("pc", 128), ("jb", 512), ("fs", 512)):
+    SCRATCH[_n] = ("sbuf", [128, _w], "float16")
+SCRATCH["pint"] = ("sbuf", [128, 6], "int32")
+NS = 2
+MID = 2048.0
 SEMAPHORES = ["V", "S", "P", "G", "ls", "xa", "ma", "mr", "m0", "m1", "nn", "c0", "c1",
               "dx", "dm", "dw", "o0", "o1", "o2", "o3", "o4", "o5", "o6", "o7"]
+WORLD = 256
 A = 16
 E = 32
 SO, QO = 256, 512
-TM, TI = 256, 320
+KQ = 24
+STEP, TINY = 2.0 ** -24 * (1 + 2.0 ** -10), 1e-30
 WAKE = 0.22
 DMA, CALL = 1.9, 0.35
 HOP = {"xa": 4.5, "ma": 4.3, "m0": 0.7, "m1": 0.7, "nn": 1.5, "c0": 1.3, "c1": 1.3}
-GIVEN = ("hac cx@ oaw f7@ oc8 mp@ hcg w1@ hcc triv ht0 ht2 pc cand@ le eqt acc3 cn@ oslot slot@",
-         "w0@ mp@s hcg2 fra ht1 ht3 b8 acc0 acc1 acc2 slot@s")
+GIVEN = ("mrep wq pint5 far0 far1 hm0 far2 far3 hal hac zs cx@ oc8 f7@ oaw hcg od8 mp@ hcc w1@ hdc ht0 pc ht2 fs2 fs3 cand@ "
+         "osl2 osl3 osl0 eqt slot@ ne0 cn@ sh1 sm1 sh0 sm0 oq mb1 mb0 hmc hqc lmem lq",
+         "a@ step w0@ hcg2 mp@s hdg fra b8 ht1 ht3 acc0 acc1 ne1 slot@s ma1 ma0")
+LATE = ("pint5 far0 far1 far2 far3", "wq")
 
 
 def plan(T, topo):
@@ -46,7 +54,9 @@ def plan(T, topo):
     assert all(partner[r] in far[r] for r in range(n))
     port = [[c for c in topo.cores_of(cores[r]) if c not in cores and topo.die(c) == topo.die(cores[r])
              and topo.may_write(c, cores[far[r][0]])] for r in range(n)]
-    return near, far, chip, order, partner, port
+    across = [[c for c in range(WORLD) if topo.mates(c, cores[partner[r]]) and topo.die(c) == topo.die(cores[r])
+               and topo.may_write(cores[r], c) and topo.may_write(c, cores[partner[r]])] for r in range(n)]
+    return near, far, chip, order, partner, port, across
 
 
 def bits(engines):
@@ -69,29 +79,34 @@ def make_send(g, core, T, topo, count):
 
 
 def relay(g, core, T, topo, pl):
-    near, far, chip, order, partner, port = pl
+    near, far, chip, order, partner, port, across = pl
     cores = T.cores
     n = [0]
     send = make_send(g, core, T, topo, n)
     for r in range(len(cores)):
+        p = partner[r]
+        h = 128 if r > p else 0
+        if core in across[r]:
+            g.wait_ge(T.sem.mr, len(topo.engines(cores[r], core)))
+            if core == across[r][0]:
+                send("ma", [(T.rms[:], [(cores[p], T.u0s[:, h:h + 128])], topo.engines(core, cores[p]))])
+            else:
+                send("ma", [(T.rm[:, 0:64].bitcast(dt.uint8), [(cores[p], T.u0[:, h:h + 64].bitcast(dt.uint8))],
+                             topo.engines(core, cores[p]))])
         if core not in port[r]:
             continue
         here = chip[r]
-        p = partner[r]
         off = topo.engines(core, cores[p])
         allon = topo.engines(core, cores[r])
         to = chip[p]
         a, b = QO + A * here[0], QO + A * here[0] + A * len(here)
-        h = 128 if r > p else 0
-        g.wait_ge(T.sem.xa, len(allon))
+        g.wait_ge(T.sem.xa, len(allon) // 2)
         if core == port[r][0]:
             send("xa", [(T.rx[:].bitcast(dt.uint8), [(cores[q], T.u0[:, a:b].bitcast(dt.uint8)) for q in to], off)])
-            g.wait_ge(T.sem.mr, len(allon))
-            send("ma", [(T.rms[:], [(cores[p], T.u0s[:, h:h + 128])], off)])
         else:
-            send("xa", [(T.rxs[:], [(cores[q], T.u0s[:, a:b]) for q in to], off)])
-            g.wait_ge(T.sem.mr, len(allon))
-            send("ma", [(T.rm[:].bitcast(dt.uint8), [(cores[p], T.u0[:, h:h + 128].bitcast(dt.uint8))], off)])
+            send("xa", [(T.rxs[:, 3 * A:5 * A], [(cores[q], T.u0s[:, a:b]) for q in to], off)])
+            g.wait_ge(T.sem.mr, len(allon) // 2)
+            send("ma", [(T.rm[:, 0:64].bitcast(dt.uint8), [(cores[p], T.u0[:, h + 64:h + 128].bitcast(dt.uint8))], off)])
     if n[0]:
         g.wait_ge(T.sem.ls, n[0])
 
@@ -176,7 +191,7 @@ def in_order(ops, chains):
 
 def rank_program(g, core, T, topo):
     pl = plan(T, topo)
-    near, far, chip, order, partner, port = pl
+    near, far, chip, order, partner, port, across = pl
     cores = T.cores
     N = len(cores)
     rank = T.rank_of(core)
@@ -288,28 +303,35 @@ def rank_program(g, core, T, topo):
         else:
             do("G", "", w, lambda: g.iota(ap, pat, base, mul), 0.15 + 0.002 * n)
 
-    dma("Y", "dx", "", "xt", T.xt[:, 0:64], T.x[:, :], 1.3)
+    first = chip[rank].index(rank)
+    xo = 3 * A * (1 - first)
+    dma("Y", "dx", "", "xt", T.xt[:, 4 * xo:4 * xo + 64], T.x[:, :], 1.3)
     dma("Y", "dm", "", "mt", T.mt[:, :], T.me[:, :], 1.6)
     dma("Y", "dw", "", "wt", T.wt[:, :], T.w[:, :])
-    fill("xz", T.xt[:, 64:512], 0.0, 224)
-    quant("xt xz", "xq xqs", T.xq[:, 0:128], T.xqs[:, 0:128], T.xt[:, :])
+    fill("xz", T.xt[:, 4 * xo + 64:512], 0.0, 224 - 2 * xo)
+    if xo:
+        fill("xz2", T.xt[:, 0:4 * xo], 0.0, 2 * xo)
+    quant("xt xz xz2", "xq xqs", T.xq[:, 0:128], T.xqs[:, 0:128], T.xt[:, :])
     mo = 128 * own
     quant("mt", "mem0%d mem0%ds" % (own, own), T.u0[:, mo:mo + 128], T.u0s[:, mo:mo + 128], T.mt[:, :])
     qa = QO + A * rank
-    ra = A * chip[rank].index(rank)
-    xs, xd = T.xq[:, 0:A].bitcast(dt.uint8), T.u0[:, qa:qa + A].bitcast(dt.uint8)
-    ys, yd = T.xqs[:, 0:A], T.u0s[:, qa:qa + A]
-    sets = (eon, eoff)
-    send("xa", "xqs", [(ys, [(port[q][1], T.rxs[:, ra:ra + A])], sets[i]) for i, q in enumerate(chip[rank])], tag="s0", dur=1.4)
-    send("xa", "xq", [(xs, [(port[q][0], T.rx[:, ra:ra + A].bitcast(dt.uint8))], sets[i]) for i, q in enumerate(chip[rank])],
-         after=("s0",), tag="s1")
-    send("mr", "mem0%d" % own, [(T.u0[:, mo:mo + 128].bitcast(dt.uint8), [(port[rank][1], T.rm[:].bitcast(dt.uint8))], eall)],
+    ra = A * first
+    xs, xd = T.xq[:, xo:xo + A].bitcast(dt.uint8), T.u0[:, qa:qa + A].bitcast(dt.uint8)
+    ys, yd = T.xqs[:, xo:xo + A], T.u0s[:, qa:qa + A]
+    xb = T.xt[:, 4 * xo:4 * xo + 8]
+    parts = []
+    for q in chip[rank]:
+        parts += [(xs, [(port[q][0], T.rx[:, ra:ra + A].bitcast(dt.uint8))]),
+                  (T.xqs[:, 0:4 * A], [(port[q][1], T.rxs[:, 4 * ra:4 * ra + 4 * A])])]
+    send("xa", "xq xqs", [p + (eall[4 * i:4 * i + 4],) for i, p in enumerate(parts)], tag="s1", dur=1.4)
+    send("mr", "mem0%d" % own, [(T.u0[:, mo + 64 * i:mo + 64 * i + 64].bitcast(dt.uint8),
+                                 [((across, port)[i][rank][1], T.rm[:, 0:64].bitcast(dt.uint8))], (eoff, eon)[i]) for i in range(2)],
          after=("s1",), tag="s2")
-    send("mr", "mem0%ds" % own, [(T.u0s[:, mo:mo + 128], [(port[rank][0], T.rms[:])], eall)], after=("s2",), tag="s3")
+    send("mr", "mem0%ds" % own, [(T.u0s[:, mo:mo + 128], [(across[rank][0], T.rms[:])], eoff)], after=("s2",), tag="s3")
     spread("xa", "xq", xs, lambda q: xd, after=("s3",), tag="s4")
     spread("xa", "xqs", ys, lambda q: yd, after=("s4",), tag="last")
     arrive("xa", 2 * (from_mates + foff * (len(far[rank]) // len(chip[rank]))), "qfar0 qfar0s", "s1")
-    arrive("ma", 2 * foff, "mem0%d mem0%ds" % (1 - own, 1 - own), "s3")
+    arrive("ma", 3 * foff, "mem0%d mem0%ds" % (1 - own, 1 - own), "s3")
     iota("pint0", T.pint[:, 0:1], [[0, 1]], 1, 0, 1, False)
     iota("jm", T.jm[:, :], [[0, 8], [1, 16]], 128)
     iota("jf", T.jf[:, 0:128], [[1, 128]], 128)
@@ -318,18 +340,26 @@ def rank_program(g, core, T, topo):
     act("jf", "jf2", T.jf[:, 128:256], T.jf[:, 0:128], AF.Identity, bias=128.0)
     fill("zz", T.zz[:, :], 0.0, 256)
     fill("z8", T.z8[:, :], 0.0)
-    put("one", T.one[:, :], 1.0, 64)
+    put("one", T.one[:, 0:64], 1.0, 64)
+    put("inc0", T.one[:, 64:128], 0.0, 64)
+    act("zz inc0", "inc", T.one[:, 80:128:32], T.zz[:, 0:2], AF.Identity, bias=2.0, n=2)
+    iota("pint4", T.pint[:, 4:5], [[0, 1]], 1, SO + 79, -1, False)
+    ts("pint4", "pint5", T.pint[:, 5:6], T.pint[:, 4:5], 5, None, op.logical_shift_right)
+    for e in range(2):
+        ts("pint4", "far%d" % e, T.far[:, e:e + 1], T.pint[:, 4:5], -80.0 - 128 * e, None, op.add)
+        ts("pint5", "far%d" % (2 + e), T.far[:, 2 + e:3 + e], T.pint[:, 5:6], 2.0, -4.0 - 8 * e, op.mult, op.add)
     ts("pint0", "p16i", T.pint[:, 1:2], T.pint[:, 0:1], 15, None, op.bitwise_and)
     ts("pint0", "g16i", T.pint[:, 2:3], T.pint[:, 0:1], 4, None, op.logical_shift_right)
     ts("pint0", "p8i", T.pint[:, 3:4], T.pint[:, 0:1], 7, None, op.bitwise_and)
     cp("pint0 p16i g16i p8i", "pf", T.pf[:, 0:4], T.pint[:, 0:4])
-    cp("p16i", "ox", T.ox[:, 0:1], T.pint[:, 1:2])
+    pf, p16, g16, p8 = T.pf[:, 0:1], T.pf[:, 1:2], T.pf[:, 2:3], T.pf[:, 3:4]
+    ts("pf", "ox", T.ox[:, 0:1], p16, float(xo), None, op.add)
     pick(T.u0[:, qa:qa + A], T.u0s[:, qa:qa + A], T.xq[:, 0:128], T.xqs[:, 0:128], T.ox[:, 0:1],
          "xq", "xqs", "qown0", "qown0s", "ox", 16)
-    pf, p16, g16, p8 = T.pf[:, 0:1], T.pf[:, 1:2], T.pf[:, 2:3], T.pf[:, 3:4]
     act("pf", "pf4", T.pf[:, 4:5], pf, AF.Identity, bias=128.0, n=1)
-    act("pf", "old", T.pf[:, 5:6], pf, AF.Identity, bias=float(TI + QO - SO), n=1)
+    act("pf", "old", T.pf[:, 5:6], p16, AF.Identity, bias=float(KQ * E - 16), n=1)
     ts("pf", "p161", T.pf[:, 6:7], p16, 1.0, None, op.add)
+    ts("pf", "side", T.pf[:, 7:8], p16, 8.0, 1.0, op.is_ge, op.add)
     place = (pf, T.pf[:, 4:5])
     act("pf pf4", "npl", T.npl[:, :], T.pf[:, 0:5:4], AF.Identity, scale=-512.0, n=2)
     rm = lambda k: T.rmk[:, k:k + 1]
@@ -338,8 +368,6 @@ def rank_program(g, core, T, topo):
     ts("rm", "rm4", rm(4), rm(1), 8.0, None, op.mult)
     tt("rm3 rm4", "rm5", rm(5), rm(3), rm(4), op.add)
     ts("rm", "rm6", rm(6), rm(2), 2.0, None, op.mult)
-    ts("rm rm6", "rm7", rm(7), rm(0), 3.0, rm(6), op.mult, op.add)
-    ts("rm rm7", "rm8", rm(8), rm(1), 15.0, rm(7), op.mult, op.add)
     ts("rm", "rm9", rm(9), rm(0), 16.0, rm(1), op.mult, op.add)
     ts("rm rm9", "rm10", rm(10), rm(2), 128.0, rm(9), op.mult, op.add)
     for t in range(2):
@@ -348,56 +376,53 @@ def rank_program(g, core, T, topo):
     fill("cxz", T.cx[:, 0:16:8], -1e29)
     put("c2", T.c2[:, :], 128.0 * lo + 0.5, 2)
     put("fraz", T.fra[:, 128:144], -1.0, 16)
-    put("lez", T.le[:, 128:129], -128.0, 1)
-    put("e8", T.e8[:, :], float(E), 8)
+    put("e8", T.e8[:, :], -1.0, 8)
+    put("dv", T.dv[:, :], 0.0, 8)
     act("jm", "odr1", T.odr[:, 1:8], T.jm[:, 1:8], AF.Copy, n=7)
     put("odr0", T.odr[:, 0:1], float(N), 1)
-    for nm, n in (("hc", 1), ("hm", 2)):
-        for i in range(n):
-            act("zz", "%sz%d" % (nm, i), T[nm][:, 512 * i:512 * i + 512], T.zz[:, 0:512], AF.Copy, n=512)
+    for nm in ("hc", "hm"):
+        act("zz", nm + "z0", T[nm][:, 0:512], T.zz[:, 0:512], AF.Copy, n=512)
+    fill("hdz0", T.hd[:, :], 0.0, 276)
     fill("htz", T.ht[:, 512:520], 0.0)
-    ts("jm pf", "dg", T.dg[:, :], T.jm[:, 0:8], g16, None, op.is_equal)
-    ts("jf pf", "tri", T.tri[:, :], T.jf[:, 0:128], pf, None, op.is_lt)
+    ts("jm pf", "dg", T.dg[:, 0:8], T.jm[:, 0:8], g16, None, op.is_equal)
+    ts("jm pf", "dg16", T.dg[:, 8:16], T.jm[:, 0:8], g16, 0.0625, op.is_equal, op.mult)
+    ts("jf pf hdz0", "tri", T.hd[:, 1:512:4], T.jf[:, 0:128], pf, 16.0, op.is_ge, op.mult)
     ts("jf p161", "win1", T.win1[:, :], T.jf[:, 0:32], T.pf[:, 6:7], None, op.is_equal)
+    ts("jf side", "win2", T.win2[:, :], T.jf[:, 0:16], T.pf[:, 7:8], -8.0, op.is_equal, op.mult)
     ts("jm pf", "dgm", T.dgm[:, :], T.jm[:, 0:8], g16, 16.0, op.not_equal, op.mult)
+    ts("jm pf", "off8", T.off8[:, :], T.jm[:, 0:8], g16, -1e29, op.not_equal, op.mult)
     fill("etz", T.et[:, :], 0.0, 260)
     ts("jf pf etz", "et", T.et[:, 3:515:4], T.jf[:, 0:128], pf, 0.5, op.is_equal, op.mult)
     for b in range(4):
         quant("etz et", "ec%d" % b, T.ec[:, 128 * b:128 * b + 128], T.ecs[:, 128 * b:128 * b + 128], T.et[:, 3 - b:515 - b])
     for c in range(4):
-        act("pf", "kb%d" % c, T.kb[:, c:c + 1], p8, AF.Identity, bias=E - 0.5 - 8.0 * c, scale=-1.0, n=1)
+        act("pf", "kb%d" % c, T.kb[:, c:c + 1], p8, AF.Identity, bias=128.0 * (E - (0.5 if c < NS else 0.0) - 8.0 * c) - MID,
+            scale=-128.0, n=1)
+    for c in range(NS, 4):
+        ts("jf kb%d" % c, "jb%d" % c, T.jb[:, 128 * c:128 * c + 128], T.jf[:, 0:128], T.kb[:, c:c + 1], None, op.subtract)
     fill("wz", T.wtile[:, 512:520], 0.0)
     ts("jm pf", "w0a", T.wtile[:, 0:512:4], T.jm[:, :], p16, 16.0, op.is_equal, op.mult)
-    ts("jm pf", "w0b", T.wtile[:, 1:512:4], T.jm[:, :], p16, None, op.is_equal)
-    ts("jm", "tgt", T.tgt[:, :], T.jm[:, :], 8.0, float(hi - lo), op.is_ge, op.mult)
-    ts("tgt pf", "w1a", T.wtile[:, 2:512:4], T.tgt[:, :], float(lo), p16, op.add, op.is_equal)
-    ts("zz p161", "w2a", T.wtile[:, 3:512:4], T.zz[:, 0:128], T.pf[:, 6:7], None, op.add)
-    for i, z in enumerate((0, 2, 3)):
-        quant("wz w0a w0b w1a w2a", "wc%d" % i, T.wc[:, 128 * i:128 * i + 128], T.wcs[:, 128 * i:128 * i + 128], T.wtile[:, z:z + 512])
-    fill("xtz", T.xtile[:, :], 0.0, 256)
-    ts("dg rm10 xtz", "xta", T.xtile[:, 0:32:4], T.dg[:, :], rm(10), None, op.mult)
-    cp("xt xtz", "xtb", T.xtile[:, 32:40], T.xt[:, 0:8])
-    quant("xtz xta xtb", "xc", T.xc[:, :], T.xcs[:, :], T.xtile[:, :])
-    cp("xt", "hcx", T.hc[:, 512:520], T.xt[:, 0:8])
+    ts("jm pf", "w0b", T.wtile[:, 1:512:4], T.jm[:, :], p16, 16.0, op.is_equal, op.mult)
+    ts("zz p161", "w1a", T.wtile[:, 2:512:4], T.zz[:, 0:128], T.pf[:, 6:7], None, op.add)
+    ts("jf pf", "w2a", T.wtile[:, 3:512:4], T.jf[:, 0:128], pf, None, op.is_equal)
+    for i in range(2):
+        quant("wz w0a w0b w1a w2a", "wc%d" % i, T.wc[:, 128 * i:128 * i + 128], T.wcs[:, 128 * i:128 * i + 128],
+              T.wtile[:, 2 * i:2 * i + 512])
+    cp("xt", "hcx", T.hc[:, 512:520], xb)
+    cp("xt hdz0", "hdx", T.hd[:, 512:520], xb)
+    ts("dg rm10 hdz0", "xta", T.hd[:, 520:552:4], T.dg[:, 0:8], rm(10), None, op.mult)
     quant("wt", "wq wqs", T.wq[:, :], T.wqs[:, :], T.wt[:, :])
-    ts("rm", "rm11", rm(11), rm(0), 0.0625, None, op.mult)
-    ts("rm", "rm12", rm(12), rm(0), -0.0625, rm(1), op.mult, op.add)
-    act("jf rm11", "ida", T.ida[:, :], T.jf[:, 0:128], AF.Identity, scale=rm(11))
-    act("jm rm12", "idb", T.idb[:, :], T.jm[:, :], AF.Identity, scale=rm(12))
-    tt("ida idb", "tbi0", T.tb[:, TI:TI + 128], T.ida[:, :], T.idb[:, :], op.add, n=256)
-    act("tbi0 rm", "tbi1", T.tb[:, TI + 128:TI + 256], T.tb[:, TI:TI + 128], AF.Identity, bias=rm(2))
-    act("tbi0 rm6", "tbi2", T.tb[:, TI + 256:TI + 384], T.tb[:, TI:TI + 128], AF.Identity, bias=rm(6))
-    act("tbi0 rm8", "tbm", T.tb[:, TM:TM + 64], T.tb[:, TI:TI + 64], AF.Identity, bias=rm(8), scale=-1.0, n=64)
+    ts("rm rm6 pf", "rm13", rm(13), rm(0), g16, rm(6), op.mult, op.add)
+    act("jm rm rm13 tqz", "tbi2", T.tq[:, KQ * E - 16:KQ * E], T.jm[:, 0:16], AF.Identity, bias=rm(13), scale=rm(1), n=16)
     act("c32 rm", "ba", T.ba[:, :], T.c32[:, :], AF.Identity, scale=rm(0), n=32)
     act("r32 rm", "bb", T.bb[:, :], T.r32[:, :], AF.Identity, scale=rm(1), n=32)
     tt("ba bb", "bc0", T.bc[:, 0:32], T.ba[:, :], T.bb[:, :], op.add)
     act("bc0 rm", "bc1", T.bc[:, 32:64], T.bc[:, 0:32], AF.Identity, bias=rm(2), n=32)
     for s in range(N):
         d = (pair[s] - h) % len(grp)
-        act("bc0 bc1 rm3 rm4 rm5", "tbq%d" % s, T.tb[:, E * s:E * s + E], T.bc[:, E * (d // 2):E * (d // 2) + E], AF.Identity,
+        act("bc0 bc1 rm3 rm4 rm5 tqz", "tbq%d" % s, T.tq[:, s:KQ * E:KQ], T.bc[:, E * (d // 2):E * (d // 2) + E], AF.Identity,
             bias=(0.0, rm(4), rm(3), rm(5))[2 * (d % 2) + upper[s]], n=32)
-    TBM = "tbm tbi0 tbi1"
-    TBQ = TBM + " tbi2 " + " ".join("tbq%d" % s for s in range(N))
+    TBQ = "tqz tbi2 " + " ".join("tbq%d" % s for s in range(N))
 
     def W(i):
         return T.wc[:, 128 * i:128 * i + 128], T.wcs[:, 128 * i:128 * i + 128]
@@ -417,9 +442,9 @@ def rank_program(g, core, T, topo):
         Q = both("qown%d qfar%d" % (t, t))
         MEM = "mem%d0 mem%d1" % (t, t)
         MEMS = "mem%d0s mem%d1s" % (t, t)
-        for e in (own, 1 - own):
+        for i, e in enumerate((0, 1) if t else (own, 1 - own)):
             mm(e, 128, q, qs, u[:, 128 * e:128 * e + 128], us[:, 128 * e:128 * e + 128], Q + " " + both("mem%d%d" % (t, e)),
-               tag="sc%d" % t)
+               after=("sc%d" % t,) if i else (), tag="sc%d" % t)
             c = 2 * order.index((lo, hi)[e])
             red("#%d lmz%d" % (e, t), "lmo%d%d" % (t, e), lm[:, c:c + 1], bank(e), op.max, n=128)
         OWN = "lmz%d lmo%d0 lmo%d1" % (t, t, t) + (" lmn1" if t else "")
@@ -431,21 +456,20 @@ def rank_program(g, core, T, topo):
         c = 2 * order.index(lo)
         scan("#0 zz", "cm0", T.cm[:, 0:128], bank(0), T.zz[:, 0:128], -1e29, op.max, op.add, n=128)
         scan("#1 zz lmo%d0" % t, "cm", T.cm[:, 128:256], bank(1), T.zz[:, 0:128], lm[:, c:c + 1], op.max, op.add, n=128)
-        a, hi16, low = T.aa[:, t:t + 1], T.aa[:, 2 + t:3 + t], T.lw[:, t:t + 1]
+        a, hi16 = T.aa[:, t:t + 1], T.aa[:, 2 + t:3 + t]
         count("cm cm0", "ah%d" % t, T.cm[:, 15:256:16], AF.Sign, T.cm[:, 255:256], -1.0, hi16, n=16)
         ops[-1]["tag"] = "ah%d" % t
         count("cm cm0", "a%d" % t, T.cm[:, :], AF.Sign, T.cm[:, 255:256], -1.0, a, n=256)
         ops[-1]["after"] = ("ah%d" % t,)
         ts("z8 hmz0 ah%d" % t, "hm0", T.hm[:, 0:32:4], T.z8[:, :], hi16, None, op.add)
-        ts("ah%d" % t, "low%d" % t, low, hi16, -16.0, None, op.mult)
-        ts("dg hmz0 a%d low%d" % (t, t), "hal", T.hm[:, 1:32:4], T.dg[:, :], a, low, op.mult, op.add)
-        quant("hmz0 hm0 hal", both("hac"), T.hac[:, :], T.hacs[:, :], T.hm[:, 0:512])
+        ts("dg16 hmz0 a%d ah%d" % (t, t), "hal", T.hm[:, 1:32:4], T.dg[:, 8:16], a, hi16, op.mult, op.subtract)
+        quant("hmz0 hm0 hal hm2 hm3", both("hac"), T.hac[:, :], T.hacs[:, :], T.hm[:, 0:512])
         mm(7, 128, *W(0), T.hac[:, :], T.hacs[:, :], "wc0 " + both("hac"))
         cp("#7", "oaw", T.oaw[:, :], bank(7, 8))
         pick(mp[:, :], mps[:, :], u[:, 0:256], us[:, 0:256], T.oaw[:, 0:8], MEM, MEMS, "mp%d" % t, "mp%ds" % t, "oaw", 128)
         for b in range(4):
             mm(3 + b, 128, T.ec[:, 128 * b:128 * b + 128], T.ecs[:, 128 * b:128 * b + 128], mp[:, :], mps[:, :],
-               "ec%d mp%d mp%ds" % (b, t, t), False, True)
+               "ec%d mp%d mp%ds" % (b, t, t), False, True, ("blend",) if b else (), "blend")
         for b in range(4):
             if b % 2 == 0:
                 cp("#%d" % (3 + b), "ht%d" % b, T.ht[:, b:512:4], bank(3 + b), n=128)
@@ -462,27 +486,48 @@ def rank_program(g, core, T, topo):
         if t == 1:
             spread("nn", "nlo nlz", T.nl[:, 4 * h:4 * h + 4], lambda r: T.nl[:, 4 * h:4 * h + 4])
             arrive("nn", from_mates, "nla")
+        m, half, step = T.cm[:, 255:256], T.hf[:, 0:1], T.hf[:, 1:2]
+        cl, ch = 2 * order.index(lo), 2 * order.index(hi)
+        ts("off8 cm", "mrep", T.mrep[:, :], T.off8[:, :], m, None, op.add)
+        ts("lmo%d0 lmo%d1" % (t, t), "half", half, lm[:, ch:ch + 1], lm[:, cl:cl + 1], 1.0, op.is_gt, op.add)
+        if hi - lo > 1:
+            act("cm", "step", step, m, AF.Abs, bias=TINY, scale=STEP, n=1)
+            ts("half step dv", "dv", T.dv[:, N - 1:N], half, -1.0, step, op.add, op.mult)
+            z0 = 2
+        else:
+            act("cm dv", "step", T.dv[:, lo:lo + 1], m, AF.Abs, bias=TINY, scale=STEP, n=1)
+            ts("step dv", "dv", T.dv[:, 0:1], T.dv[:, lo:lo + 1], -1.0, None, op.mult)
+            z0 = 0
         LM = OWN + " lma%d" % t
+        scan(LM + " step dv", "zs", T.zs[:, z0:N], lm[:, 2 * z0:16:2], T.dv[:, z0:N], -1e29, op.max, op.add)
+        ts("mrep zs half", "oc8", T.oc8[:, :], T.mrep[:, :], T.zs[:, N - 1:N], half, op.is_ge, op.mult)
+        gather("V", "oc8 hcz0 win2", "hcg", T.hc[:, 0:256:4], T.win2[:, :], T.oc8[:, 0:4], 64)
+        gather("S", "oc8 hcz0 win2", "hcg2", T.hc[:, 256:512:4], T.win2[:, :], T.oc8[:, 4:8], 64)
+        quant("hcg hcg2 hcz0 hcx", both("hcc"), T.hcc[:, 0:130], T.hccs[:, 0:130], T.hc[:, :], 130)
+        mm(0, 130, *W(0), T.hcc[:, 0:130], T.hccs[:, 0:130], "wc0 " + both("hcc"))
+        scan("#0 zz", "pc", T.pc[:, :], bank(0), T.zz[:, 0:128], MID, op.add, op.add, n=128)
+        for c in range(NS):
+            count("pc kb%d" % c, "acc%d" % c, T.pc[:, :], AF.Sign, T.kb[:, c:c + 1], 1.0, T.acc[:, c:c + 1])
+        for c in range(NS, 4):
+            fs = T.fs[:, 128 * c:128 * c + 128]
+            scan("pc jb%d" % c, "fs%d" % c, fs, T.jb[:, 128 * c:128 * c + 128], T.pc[:, :], 4096.0, op.min, op.max, n=64)
+            ts("fs%d kb%d" % (c, c), "osl%d" % c, T.oslot[:, c:c + 1], T.fs[:, 128 * c + 127:128 * c + 128],
+               T.kb[:, c:c + 1], 128.0, op.add, op.min)
+        if NS:
+            ts(" ".join("acc%d" % c for c in range(NS)), "osl0", T.oslot[:, 0:NS], T.acc[:, 0:NS], 0.5, 64.0, op.mult, op.add)
+        OS = "osl0 osl1 osl2 osl3"
+        pick(u[:, SO:SO + 64], us[:, SO:SO + 64], cd[:, 0:130], cds[:, 0:130], T.oslot[:, 0:4],
+             "cand%d" % t, "cand%ds" % t, "slot%d" % t, "slot%ds" % t, OS, 64)
         cx, w1 = T.cx[:, 8 * t:8 * t + 8], T.w1[:, t:t + 1]
         scan(LM + " zz cxz", "cx%d" % t, T.cx[:, 8 * t + 1:8 * t + 8], lm[:, 2:16:2], T.zz[:, 0:7], -1e29, op.max, op.add)
         top, w0, f7 = T.cx[:, 8 * t + 7:8 * t + 8], T.mx[:, t:t + 1], T.mx[:, 2 + t:3 + t]
         count("cxz cx%d" % t, "w0%d" % t, cx, AF.Sign, top, -1.0, w0, n=8)
         ts(LM + " cx%d" % t, "f7%d" % t, f7, lm[:, 0:1], top, float(N), op.is_gt, op.mult)
-        ts("dgm w0%d f7%d" % (t, t), "oc8", T.oc8[:, :], T.dgm[:, :], w0, f7, op.add, op.max)
+        ts("dgm w0%d f7%d" % (t, t), "od8", T.od8[:, :], T.dgm[:, :], w0, f7, op.add, op.max)
         tt("w0%d f7%d" % (t, t), "w1%d" % t, w1, w0, f7, op.max)
-        gather("V", "oc8 hcz0 win1", "hcg", T.hc[:, 0:256:4], T.win1[:, :], T.oc8[:, 0:4], 64)
-        gather("S", "oc8 hcz0 win1", "hcg2", T.hc[:, 256:512:4], T.win1[:, :], T.oc8[:, 4:8], 64)
-        quant("hcg hcg2 hcz0 hcx", both("hcc"), T.hcc[:, 0:130], T.hccs[:, 0:130], T.hc[:, :], 130)
-        mm(0, 130, *W(1), T.hcc[:, 0:130], T.hccs[:, 0:130], "wc1 " + both("hcc"))
-        mm(1, 130, *W(2), T.hcc[:, 0:130], T.hccs[:, 0:130], "wc2 " + both("hcc"))
-        scan("#0 zz", "pc", T.pc[:, :], bank(0), T.zz[:, 0:128], 0.0, op.add, op.add, n=128)
-        for c in range(3):
-            count("pc kb%d" % c, "acc%d" % c, T.pc[:, :], AF.Sign, T.kb[:, c:c + 1], -1.0, T.acc[:, c:c + 1])
-        ts("pc kb3 lez", "le", T.le[:, 0:128], T.pc[:, :], T.kb[:, 3:4], 2.0, op.is_le, op.mult)
-        red("le lez", "acc3", T.acc[:, 3:4], T.le[:, 0:129], op.add, n=129)
-        ts("acc0 acc1 acc2 acc3", "oslot", T.oslot[:, 0:4], T.acc[:, 0:4], 0.5, 64.0, op.mult, op.add)
-        pick(u[:, SO:SO + 64], us[:, SO:SO + 64], cd[:, 0:130], cds[:, 0:130], T.oslot[:, 0:4],
-             "cand%d" % t, "cand%ds" % t, "slot%d" % t, "slot%ds" % t, "oslot", 64)
+        gather("S", "od8 hdz0 win1", "hdg", T.hd[:, 0:512:4], T.win1[:, :], T.od8[:, 0:8], 128)
+        quant("hdg hdz0 hdx tri xta", both("hdc"), T.hdc[:, 0:138], T.hdcs[:, 0:138], T.hd[:, :], 138)
+        mm(1, 130, *W(1), T.hdc[:, 0:130], T.hdcs[:, 0:130], "wc1 " + both("hdc"), after=("blend",))
         at = lambda r: SO + 64 * ((h - pair[r]) % len(grp))
         spread("c%d" % t, "slot%d" % t, u[:, SO:SO + 64].bitcast(dt.uint8), lambda r: u[:, at(r):at(r) + 64].bitcast(dt.uint8),
                tag="cc%d" % t)
@@ -490,52 +535,49 @@ def rank_program(g, core, T, topo):
         arrive("c%d" % t, 2 * from_mates, "land%d land%ds" % (t, t))
         halves = (0, 1) if t == 0 else (own,)
         for i, e in enumerate(halves):
-            ne, sm = T.ne[:, 64 * i:64 * i + 64], T.sm[:, 64 * i:64 * i + 64]
+            ne, sm, sh = T.ne[:, 64 * i:64 * i + 64], T["sm%d" % i], T["sh%d" % i]
             won = T.fra[:, 0:144].indirect(T.oslot[:, 0:4])
             if i:
-                do("S", "fra fraz oslot npl", "ne%d" % i,
+                do("S", "fra fraz npl " + OS, "ne%d" % i,
                    lambda ne=ne, e=e, won=won: S.activation(ne, won, AF.Abs, bias=T.npl[:, e:e + 1], scale=512.0), 0.17)
             else:
-                do("V", "fra fraz oslot pf pf4", "ne%d" % i,
+                do("V", "fra fraz pf pf4 " + OS, "ne%d" % i,
                    lambda ne=ne, e=e, won=won: V.tensor_scalar(ne, won, place[e], 512.0, op.not_equal, op.mult), 0.15)
-            scan("ne%d one pf pf4" % i, "sm%d" % i, sm, T.one[:, :], ne, place[e], op.add, op.min)
-            ts("sm%d z8" % i, "om%d" % i, T.om[:, 8 * i:8 * i + 8], T.z8[:, :], T.sm[:, 64 * i + 63:64 * i + 64], None, op.add)
-            gather("VS"[i], "om%d hmz%d %s" % (i, i, TBM), "hm%d" % i, T.hm[:, 512 * i:512 * i + 512:4], T.tb[:, TM:TI + 256],
-                   T.om[:, 8 * i:8 * i + 8], 128)
-        for i in range(len(halves)):
-            k = (2, 0)[i]
-            quant("hm%d hmz%d hal" % (i, i), both("hmc%d" % i), T.hmc[:, 128 * i:128 * i + 128], T.hmcs[:, 128 * i:128 * i + 128],
-                  T.hm[:, 512 * i:512 * i + 512])
-            mm(k, 128, T.hmc[:, 128 * i:128 * i + 128], T.hmcs[:, 128 * i:128 * i + 128], T.xc[:, :], T.xcs[:, :],
-               "xc " + both("hmc%d" % i))
-            cp("#%d" % k, "lmem%d" % i, T.lmem[:, 8 * i:8 * i + 8], bank(k, 8))
-        cn, uu = T.cn[:, t:t + 1], T.uu[:, t:t + 1]
-        ts("tri w1%d" % t, "triv", T.triv[:, :], T.tri[:, :], w1, None, op.mult)
-        act("e8 w1%d" % t, "b8", T.b8[:, :], T.e8[:, :], AF.Identity, bias=-float(E), scale=w1, n=8)
-        tt("#1 triv", "eqt", T.eqt[:, :], bank(1), T.triv[:, :], op.is_equal, n=128)
+            scan("ne%d one far%d" % (i, e), "sm%d" % i, sm[:, :], T.one[:, 0:64], ne, T.far[:, e:e + 1], op.add, op.min)
+            scan("ne%d inc0 inc far%d" % (i, 2 + e), "sh%d" % i, sh[:, :], T.one[:, 64:128], ne, T.far[:, 2 + e:3 + e], op.add, op.min)
+            act("sh%d z8 hmz0" % i, ("ma0 hm0", "ma1 hm2")[i], T.hm[:, 32 * i:32 * i + 32:4], T.z8[:, :], AF.Identity,
+                bias=sh[:, 63:64], n=8)
+            ts("sm%d sh%d dg16 hmz0" % (i, i), ("mb0 hal", "mb1 hm3")[i], T.hm[:, 32 * i + 1:32 * i + 32:4], T.dg[:, 8:16],
+               sm[:, 63:64], sh[:, 63:64], op.mult, op.subtract)
+        quant("hm0 hmz0 hal hm2 hm3", both("hmc"), T.hmc[:, :], T.hmcs[:, :], T.hm[:, :])
+        mm(2, 128, *W(0), T.hmc[:, :], T.hmcs[:, :], "wc0 " + both("hmc"))
+        ts("#2", "lmem", T.lmem[:, :], bank(2, 16), -1.0, SO + 63.0, op.mult, op.add)
+        cn = T.cn[:, t:t + 1]
+        act("e8 w1%d" % t, "b8", T.b8[:, :], T.e8[:, :], AF.Identity, bias=w1, n=8)
+        ts("#1 w1%d" % t, "eqt", T.eqt[:, :], bank(1), w1, float(KQ), op.is_equal, op.mult, n=128)
         red("eqt", "cn%d" % t, cn, T.eqt[:, :], op.add, n=128)
-        ts("cn%d old" % t, "uu%d" % t, uu, cn, float(E), T.pf[:, 5:6], op.is_ge, op.mult)
-        ts("b8 cn%d uu%d" % (t, t), "oq", T.oq[:, :], T.b8[:, :], cn, uu, op.add, op.max)
-        gather("S", "oq hcz0 " + TBQ, "hcg hcg2", T.hc[:, 0:512:4], T.tb[:, :], T.oq[:, 0:8], 128)
+        ts("b8 cn%d old" % t, "oq", T.oq[:, :], T.b8[:, :], cn, T.pf[:, 5:6], op.add, op.min)
+        gather("S", "oq hcz0 " + TBQ, "hcg hcg2", T.hc[:, 0:512:4], T.tq[:, :], T.oq[:, 0:8], 128)
         quant("hcg hcg2 hcz0", both("hqc"), T.hqc[:, :], T.hqcs[:, :], T.hc[:, 0:512])
-        mm(7, 128, T.hqc[:, :], T.hqcs[:, :], T.xc[:, :], T.xcs[:, :], "xc " + both("hqc"))
-        cp("#7", "lq", T.lq[:, :], bank(7, 8))
+        mm(7, 128, T.hqc[:, :], T.hqcs[:, :], T.hdc[:, 10:138], T.hdcs[:, 10:138], both("hdc hqc"))
+        cp("#7", "lq", T.lq[:, :], T.ps[:, 512 * 7 + 120:512 * 7 + 128])
         ts("odr0 odr1 w1%d slot%d" % (t, t), "oh%d" % t, T.oh[:, 8 * t:8 * t + 8], T.odr[:, :], w1, None, op.is_equal)
-        act("cn%d" % t, "ws%d" % t, T.wv[:, t:t + 1], cn, AF.Sign, bias=E - 0.5, scale=-1.0, n=1)
+        act("cn%d" % t, "ws%d" % t, T.wv[:, t:t + 1], cn, AF.Sign, bias=KQ * (E - 0.5), scale=-1.0, n=1)
         made_by = {o["w"][0]: i for i, o in reversed(list(enumerate(ops))) if i >= first and o["w"]}
+        made_by.update({k: i for i, o in enumerate(ops[:first]) for k in o["w"][:1] if k in LATE[t].split()})
         for names in GIVEN:
-            chains.append([made_by[k.replace("@", str(t))] for k in names.split()])
+            names = names.replace("@", str(t)).split()
+            chains.append([made_by[k] for k in names if k in made_by])
         NEW = "slot%d land%d qown%d qfar%d" % (t, t, t, t)
         NEWS = "slot%ds land%ds qown%ds qfar%ds" % (t, t, t, t)
         if t == 0:
-            for i in range(2):
-                pick(T.u1[:, 128 * i:128 * i + 128], T.u1s[:, 128 * i:128 * i + 128], u[:, 0:SO + 64], us[:, 0:SO + 64],
-                     T.lmem[:, 8 * i:8 * i + 8], MEM + " slot0", MEMS + " slot0s", "mem1%d" % i, "mem1%ds" % i, "lmem%d" % i, 128)
+            pick(T.u1[:, 0:SO], T.u1s[:, 0:SO], u[:, 0:SO + 64], us[:, 0:SO + 64], T.lmem[:, :],
+                 MEM + " slot0", MEMS + " slot0s", "mem10 mem11", "mem10s mem11s", "lmem", SO)
             pick(T.u1[:, QO:QO + 128], T.u1s[:, QO:QO + 128], u[:, SO:QO + 128], us[:, SO:QO + 128], T.lq[:, 0:8],
                  NEW, NEWS, "qown1 qfar1", "qown1s qfar1s", "lq", 128)
         else:
             pick(T.fm[:, :], T.fms[:, :], u[:, 0:SO + 64], us[:, 0:SO + 64], T.lmem[:, 0:8],
-                 MEM + " slot1", MEMS + " slot1s", "fm", "fms", "lmem0", 128)
+                 MEM + " slot1", MEMS + " slot1s", "fm", "fms", "lmem", 128)
             dma("Y", "o0", "fm land1s", "out0", T.oc[:, :], T.fm[:, :].bitcast(dt.uint8))
             for k in range(4):
                 dma("Y", "o%d" % (1 + k), "fms land1s", "out%d" % (1 + k), T.osc[4 * k:4 * k + 4, :], T.fms[32 * k:32 * k + 4, :])
@@ -544,7 +586,7 @@ def rank_program(g, core, T, topo):
     one_round(0)
     one_round(1)
     mm(3, 128, T.wq[:, :], T.wqs[:, :], T.qf[:, :], T.qfs[:, :], "wq wqs qf qfs")
-    act("#3", "ysb", T.ysb[:, :], bank(3), AF.Copy)
+    cp("#3", "ysb", T.ysb[:, :], bank(3), n=128)
     dma("S", "o7", "ysb", "outy", T.y[:, :], T.ysb[:, :])
     for t, nt, nk in ((0, T.lm1, "lmn1 lmz1 lma1"), (1, T.nl, "nlo nlz nla")):
         tt("oh%d slot1 %s" % (t, nk), "og%d" % t, T.og[:, 8 * t:8 * t + 8], T.oh[:, 8 * t:8 * t + 8], nt[:, 1:16:2], op.mult)

from concourse.bass import DstId, RemoteDMATransfer
from concourse.mybir import dt, AluOpType, AxisListType, ActivationFunctionType

F8 = "float8_e4m3fn_x4"
SCRATCH = {"ps": ("psum", [128, 4096], "float32")}
for _n, _w in (("xq", 128), ("wq", 128), ("rx", 32), ("rm", 128), ("u0", 640), ("u1", 640), ("qf", 128), ("fm", 128),
               ("mp0", 128), ("mp1", 128), ("cd0", 160), ("cd1", 160), ("wc", 256), ("ec", 512), ("hac", 128),
               ("hcc", 136), ("hdc", 144), ("hqc", 128), ("hmc", 128)):
    SCRATCH[_n] = ("sbuf", [128, _w], F8)
    SCRATCH[_n + "s"] = ("sbuf", [128, max(_w, 128)], "uint8")
for _n, _w in (("xt", 512), ("mt", 512), ("wt", 512), ("hc", 520), ("hd", 552), ("hm", 512), ("ht", 520),
               ("wtile", 520), ("et", 520), ("zz", 512), ("jf", 256), ("jm", 128),
               ("c32", 32), ("r32", 32), ("win1", 32), ("win2", 16), ("tq", 768),
               ("ba", 32), ("bb", 32), ("bc", 64), ("jk", 5120), ("fra", 144), ("eqt", 128), ("ne", 128), ("one", 128)):
    SCRATCH[_n] = ("sbuf", [128, _w], "bfloat16")
for _n, _w in (("pf", 8), ("rmk", 16), ("dg", 16), ("dgm", 8), ("kb", 4), ("odr", 8), ("lm0", 16), ("lm1", 16), ("nl", 16),
               ("cm", 256), ("aa", 4), ("nm", 2), ("c2", 2), ("mx", 4), ("cx", 16), ("w1", 2), ("acc", 4), ("b8", 8),
               ("cn", 2), ("sm0", 64), ("sm1", 64), ("sh0", 64), ("sh1", 64), ("far", 4), ("wv", 2), ("oh", 16), ("og", 16), ("wo", 2), ("ysb", 128), ("z8", 8),
               ("e8", 8), ("npl", 2), ("off8", 8), ("mrep", 8), ("dv", 8), ("zs", 8),
               ("hf", 2)):
    SCRATCH[_n] = ("sbuf", [128, _w], "float32")
for _n, _w in (("ox", 2), ("oaw", 8), ("oc8", 8), ("od8", 8), ("oslot", 4), ("oq", 8), ("lq", 8), ("lmem", 16)):
    SCRATCH[_n] = ("sbuf", [128, _w], "uint16")
for _n, _w in (("pc", 128), ("jb", 512), ("fs", 512)):
    SCRATCH[_n] = ("sbuf", [128, _w], "float16")
SCRATCH["pint"] = ("sbuf", [128, 6], "int32")
NS = 2
MID = 2048.0
SEMAPHORES = ["V", "S", "P", "G", "ls", "xa", "ma", "mr", "m0", "m1", "nn", "c0", "c1",
              "dx", "dm", "dw", "o0", "o1", "o2", "o3", "o4", "o5", "o6", "o7"]
WORLD = 256
A = 16
E = 32
SO, QO = 256, 512
KQ = 24
STEP, TINY = 2.0 ** -24 * (1 + 2.0 ** -10), 1e-30
WAKE = 0.22
DMA, CALL = 1.9, 0.35
HOP = {"xa": 4.5, "ma": 4.3, "m0": 0.7, "m1": 0.7, "nn": 1.5, "c0": 1.3, "c1": 1.3}
GIVEN = ("mrep wq pint5 far0 far1 hm0 far2 far3 hal hac zs cx@ oc8 f7@ oaw hcg od8 mp@ hcc w1@ hdc ht0 pc ht2 fs2 fs3 cand@ "
         "osl2 osl3 osl0 eqt slot@ ne0 cn@ sh1 sm1 sh0 sm0 oq mb1 mb0 hmc hqc lmem lq",
         "a@ step w0@ hcg2 mp@s hdg fra b8 ht1 ht3 acc0 acc1 ne1 slot@s ma1 ma0")
LATE = ("pint5 far0 far1 far2 far3", "wq")


def plan(T, topo):
    cores = T.cores
    n = len(cores)
    near = [[q for q in range(n) if q == r or topo.may_write(cores[r], cores[q])] for r in range(n)]
    far = [[q for q in range(n) if q not in near[r]] for r in range(n)]
    chip = [[q for q in range(n) if cores[q] in topo.cores_of(cores[r])] for r in range(n)]
    order = [(i - 1) % n for i in range(n)]
    partner = [order[order.index(r) ^ 1] for r in range(n)]
    assert all(partner[r] in far[r] for r in range(n))
    port = [[c for c in topo.cores_of(cores[r]) if c not in cores and topo.die(c) == topo.die(cores[r])
             and topo.may_write(c, cores[far[r][0]])] for r in range(n)]
    across = [[c for c in range(WORLD) if topo.mates(c, cores[partner[r]]) and topo.die(c) == topo.die(cores[r])
               and topo.may_write(cores[r], c) and topo.may_write(c, cores[partner[r]])] for r in range(n)]
    return near, far, chip, order, partner, port, across


def bits(engines):
    return sum(1 << e for e in engines)


def make_send(g, core, T, topo, count):
    def send(sem, parts):
        tr = []
        for src, dst, eng in parts:
            ids = []
            for c, _ in dst:
                rid, pid = topo.addr(c, core)
                ids.append(DstId(rid=rid, pnc=pid))
            tr.append(RemoteDMATransfer(dst_ids=ids, dma_engine_mask=bits(eng), remote_sem=T.sem[sem],
                                        srcs=[src], dsts=[d for _, d in dst], alu_op=0))
            count[0] += len(eng)
        g.remote_dma_fused(tr, local_sem=T.sem.ls)
    return send


def relay(g, core, T, topo, pl):
    near, far, chip, order, partner, port, across = pl
    cores = T.cores
    n = [0]
    send = make_send(g, core, T, topo, n)
    for r in range(len(cores)):
        p = partner[r]
        h = 128 if r > p else 0
        if core in across[r]:
            g.wait_ge(T.sem.mr, len(topo.engines(cores[r], core)))
            if core == across[r][0]:
                send("ma", [(T.rms[:], [(cores[p], T.u0s[:, h:h + 128])], topo.engines(core, cores[p]))])
            else:
                send("ma", [(T.rm[:, 0:64].bitcast(dt.uint8), [(cores[p], T.u0[:, h:h + 64].bitcast(dt.uint8))],
                             topo.engines(core, cores[p]))])
        if core not in port[r]:
            continue
        here = chip[r]
        off = topo.engines(core, cores[p])
        allon = topo.engines(core, cores[r])
        to = chip[p]
        a, b = QO + A * here[0], QO + A * here[0] + A * len(here)
        g.wait_ge(T.sem.xa, len(allon) // 2)
        if core == port[r][0]:
            send("xa", [(T.rx[:].bitcast(dt.uint8), [(cores[q], T.u0[:, a:b].bitcast(dt.uint8)) for q in to], off)])
        else:
            send("xa", [(T.rxs[:, 3 * A:5 * A], [(cores[q], T.u0s[:, a:b]) for q in to], off)])
            g.wait_ge(T.sem.mr, len(allon) // 2)
            send("ma", [(T.rm[:, 0:64].bitcast(dt.uint8), [(cores[p], T.u0[:, h + 64:h + 128].bitcast(dt.uint8))], off)])
    if n[0]:
        g.wait_ge(T.sem.ls, n[0])


def conflicts(q, r, w, wr, rd, acc, strict):
    d = []
    for k in r:
        d += wr.get(k, [])
        if k[0] == "#":
            d += [e for e in rd.get(k, []) if e[2] != q]
    for k in w:
        d += [e for e in wr.get(k, []) if strict or not (acc and e[2] == q)]
        d += [e for e in rd.get(k, []) if strict or e[2] != q]
    return d


def note(e, r, w, wr, rd):
    for k in w:
        wr[k], rd[k] = [e], []
    for k in r:
        rd.setdefault(k, []).append(e)


def in_order(ops, chains):
    n = len(ops)
    wr, rd, pred = {}, {}, []
    last, soft = {}, []
    for i, o in enumerate(ops):
        p = {e[0] for e in conflicts(o["q"], o["r"], o["w"], wr, rd, False, True)}
        p.update(last[s] for s in o["after"])
        soft.append({last[s] for s in o["after"] if ops[last[s]]["q"] == o["q"]})
        if o["tag"]:
            last[o["tag"]] = i
        pred.append(p)
        note((i, 0, o["q"]), o["r"], o["w"], wr, rd)
    for chain in chains:
        for a, b in zip(chain, chain[1:]):
            if a not in pred[b]:
                pred[b].add(a)
                soft[b].add(a)
    prio = [o["dur"] for o in ops]
    moved = True
    while moved:
        moved = False
        for i in range(n - 1, -1, -1):
            for p in pred[i]:
                v = ops[p]["dur"] + (0.0 if p in soft[i] else WAKE) + prio[i]
                if v > prio[p] + 1e-9:
                    prio[p], moved = v, True
    free, done, out = {}, {}, []
    succ = [[] for _ in range(n)]
    wait = [len(p) for p in pred]
    for i in range(n):
        for p in pred[i]:
            succ[p].append(i)
    ready = {i for i in range(n) if wait[i] == 0}
    while ready:
        best = None
        byq = {}
        for i in sorted(ready):
            byq.setdefault(ops[i]["q"], []).append(i)
        for q, c in byq.items():
            st = {i: max([free.get(q, 0.0)] + [done[p] + (0.0 if p in soft[i] else WAKE) for p in pred[i]]) for i in c}
            b = min(c, key=lambda i: (st[i], -prio[i], i))
            better = [i for i in c if prio[i] > prio[b] and st[i] < st[b] + ops[b]["hold"] - 0.03]
            if better:
                b = max(better, key=lambda i: (prio[i], -i))
            if best is None or (st[b], b) < best:
                best = (st[b], b)
        s, i = best
        ready.discard(i)
        free[ops[i]["q"]] = s + ops[i]["hold"]
        done[i] = s + ops[i]["dur"]
        out.append(ops[i])
        for j in succ[i]:
            wait[j] -= 1
            if wait[j] == 0:
                ready.add(j)
    assert len(out) == n
    return out


def rank_program(g, core, T, topo):
    pl = plan(T, topo)
    near, far, chip, order, partner, port, across = pl
    cores = T.cores
    N = len(cores)
    rank = T.rank_of(core)
    if rank is None:
        relay(g, core, T, topo, pl)
        return
    op, X, AF = AluOpType, AxisListType.X, ActivationFunctionType
    V, S, P = g.vector, g.scalar, g.tensor
    queue = {"V": g.vector, "S": g.scalar, "P": g.tensor, "G": g, "Y": g.sync}
    ops = []
    ls = [0]
    fused = make_send(g, core, T, topo, ls)

    def add(q, r, w, call, sem, inc, dur, hold=None, acc=False, after=(), tag=None):
        ops.append({"q": q, "r": r.split(), "w": w.split(), "call": call, "sem": sem, "inc": inc, "dur": dur,
                    "hold": dur if hold is None else hold, "acc": acc, "after": after, "tag": tag})

    def do(q, r, w, call, dur):
        add(q, r, w, call, q, 1, dur)

    def ew(n):
        return max(64, n) * 0.001

    def dma(q, sem, r, w, o, i, dur=DMA):
        add(q, r, w, lambda: queue[q].dma_start(o, i), sem, 16, dur, 0.06)

    def send(sem, r, parts, after=(), tag=None, dur=CALL):
        add("G", r, "", lambda: fused(sem, parts), None, 0, dur, after=after, tag=tag or sem)

    def arrive(sem, n, w, after=None):
        add("far " + sem, "", w, None, sem, n, HOP[sem], after=(after or sem,))

    def ts(r, w, out, in0, s1, s2, o0, o1=None, n=8):
        if o1 is None:
            do("V", r, w, lambda: V.tensor_scalar(out, in0, s1, s2, o0), ew(n))
        else:
            do("V", r, w, lambda: V.tensor_scalar(out, in0, s1, s2, o0, o1), ew(n))

    def tt(r, w, out, in0, in1, o, n=8):
        do("V", r, w, lambda: V.tensor_tensor(out, in0, in1, o), ew(n))

    def scan(r, w, out, d0, d1, init, o0, o1, n=8):
        do("V", r, w, lambda: V.tensor_tensor_scan(out, d0, d1, init, o0, o1), ew(n))

    def red(r, w, out, in_, o, n=8):
        do("V", r, w, lambda: V.tensor_reduce(out, in_, X, o), ew(n))

    def cp(r, w, out, in_, n=8):
        do("V", r, w, lambda: V.tensor_copy(out, in_), ew(n))

    def gather(q, r, w, out, win, off, n):
        if q == "V":
            do("V", r, w, lambda: V.tensor_copy(out, win.indirect(off)), 0.055 + n * 0.0015)
        else:
            do("S", r, w, lambda: S.activation(out, win.indirect(off), AF.Copy), 0.07 + n * 0.0015)

    def act(r, w, out, in_, f, bias=0.0, scale=1.0, accum=None, n=128):
        do("S", r, w, lambda: S.activation(out, in_, f, bias=bias, scale=scale, accum_out=accum), ew(n) + 0.02)

    junk = [0]

    def count(r, w, in_, f, bias, scale, accum, n=128):
        j = junk[0] % 20
        junk[0] += 1
        act(r, "%s jk%d" % (w, j), T.jk[:, 256 * j:256 * j + n], in_, f, bias, scale, accum, n)

    def quant(r, w, c, s, in_, n=128):
        do("V", r, w, lambda: V.quantize_mx(c, s, in_), 0.015 + 0.00105 * n)

    def fill(w, ap, c, n=8):
        do("V", "", w, lambda: V.memset(ap, c), ew(n))

    def put(w, ap, c, n):
        act("zz", w, ap, T.zz[:, 0:n], AF.Identity, bias=c, n=n)

    def pick(out, outs, win, wins, off, r, rs, w, ws, ro, n):
        do("V", r + " " + ro, w, lambda: V.tensor_copy(out.bitcast(dt.uint32), win.bitcast(dt.uint32).indirect(off)), 0.055 + n * 0.0015)
        do("S", rs + " " + ro, ws, lambda: S.activation(outs, wins.indirect(off), AF.Copy), 0.07 + n * 0.0015)

    def bank(k, n=128):
        return T.ps[:, 512 * k:512 * k + n]

    def mm(k, n, lc, lsc, rc, rsc, r, start=True, stop=True, after=(), tag=None):
        add("P", r, "#%d" % k, lambda: P.matmul_mx(bank(k, n), lc, lsc, rc, rsc, start, stop), "P", 1, (n + 16) * 0.0008,
            acc=not start, after=after, tag=tag)

    grp = near[rank]
    mates = [q for q in grp if q != rank]
    on_mates = [q for q in mates if q in chip[rank]]
    off_mates = [q for q in mates if q not in chip[rank]]
    eoff = topo.engines(core, cores[off_mates[0]])
    eall = topo.engines(core, cores[on_mates[0]])
    eon = [e for e in eall if e not in eoff]
    pair = [order.index(s) // 2 for s in range(N)]
    upper = [int(s > partner[s]) for s in range(N)]
    h = pair[rank]
    lo, hi = sorted((rank, partner[rank]))
    own = upper[rank]
    foff = len(eoff)
    from_mates = len(off_mates) * foff + len(on_mates) * len(eon)

    def spread(sem, r, src, dst, after=(), tag=None):
        send(sem, r, [(src, [(cores[q], dst(q)) for q in off_mates], eoff), (src, [(cores[q], dst(q)) for q in on_mates], eon)],
             after, tag)

    def iota(w, ap, pat, n, base=0, mul=0, flag=True):
        if flag:
            do("G", "", w, lambda: g.iota(ap, pat, base, mul, allow_small_or_imprecise_dtypes=True), 0.15 + 0.002 * n)
        else:
            do("G", "", w, lambda: g.iota(ap, pat, base, mul), 0.15 + 0.002 * n)

    first = chip[rank].index(rank)
    xo = 3 * A * (1 - first)
    dma("Y", "dx", "", "xt", T.xt[:, 4 * xo:4 * xo + 64], T.x[:, :], 1.3)
    dma("Y", "dm", "", "mt", T.mt[:, :], T.me[:, :], 1.6)
    dma("Y", "dw", "", "wt", T.wt[:, :], T.w[:, :])
    fill("xz", T.xt[:, 4 * xo + 64:512], 0.0, 224 - 2 * xo)
    if xo:
        fill("xz2", T.xt[:, 0:4 * xo], 0.0, 2 * xo)
    quant("xt xz xz2", "xq xqs", T.xq[:, 0:128], T.xqs[:, 0:128], T.xt[:, :])
    mo = 128 * own
    quant("mt", "mem0%d mem0%ds" % (own, own), T.u0[:, mo:mo + 128], T.u0s[:, mo:mo + 128], T.mt[:, :])
    qa = QO + A * rank
    ra = A * first
    xs, xd = T.xq[:, xo:xo + A].bitcast(dt.uint8), T.u0[:, qa:qa + A].bitcast(dt.uint8)
    ys, yd = T.xqs[:, xo:xo + A], T.u0s[:, qa:qa + A]
    xb = T.xt[:, 4 * xo:4 * xo + 8]
    parts = []
    for q in chip[rank]:
        parts += [(xs, [(port[q][0], T.rx[:, ra:ra + A].bitcast(dt.uint8))]),
                  (T.xqs[:, 0:4 * A], [(port[q][1], T.rxs[:, 4 * ra:4 * ra + 4 * A])])]
    send("xa", "xq xqs", [p + (eall[4 * i:4 * i + 4],) for i, p in enumerate(parts)], tag="s1", dur=1.4)
    send("mr", "mem0%d" % own, [(T.u0[:, mo + 64 * i:mo + 64 * i + 64].bitcast(dt.uint8),
                                 [((across, port)[i][rank][1], T.rm[:, 0:64].bitcast(dt.uint8))], (eoff, eon)[i]) for i in range(2)],
         after=("s1",), tag="s2")
    send("mr", "mem0%ds" % own, [(T.u0s[:, mo:mo + 128], [(across[rank][0], T.rms[:])], eoff)], after=("s2",), tag="s3")
    spread("xa", "xq", xs, lambda q: xd, after=("s3",), tag="s4")
    spread("xa", "xqs", ys, lambda q: yd, after=("s4",), tag="last")
    arrive("xa", 2 * (from_mates + foff * (len(far[rank]) // len(chip[rank]))), "qfar0 qfar0s", "s1")
    arrive("ma", 3 * foff, "mem0%d mem0%ds" % (1 - own, 1 - own), "s3")
    iota("pint0", T.pint[:, 0:1], [[0, 1]], 1, 0, 1, False)
    iota("jm", T.jm[:, :], [[0, 8], [1, 16]], 128)
    iota("jf", T.jf[:, 0:128], [[1, 128]], 128)
    iota("c32", T.c32[:, :], [[-1, 4], [0, 8]], 32, 3)
    iota("r32", T.r32[:, :], [[0, 4], [-1, 8]], 32, 7)
    act("jf", "jf2", T.jf[:, 128:256], T.jf[:, 0:128], AF.Identity, bias=128.0)
    fill("zz", T.zz[:, :], 0.0, 256)
    fill("z8", T.z8[:, :], 0.0)
    put("one", T.one[:, 0:64], 1.0, 64)
    put("inc0", T.one[:, 64:128], 0.0, 64)
    act("zz inc0", "inc", T.one[:, 80:128:32], T.zz[:, 0:2], AF.Identity, bias=2.0, n=2)
    iota("pint4", T.pint[:, 4:5], [[0, 1]], 1, SO + 79, -1, False)
    ts("pint4", "pint5", T.pint[:, 5:6], T.pint[:, 4:5], 5, None, op.logical_shift_right)
    for e in range(2):
        ts("pint4", "far%d" % e, T.far[:, e:e + 1], T.pint[:, 4:5], -80.0 - 128 * e, None, op.add)
        ts("pint5", "far%d" % (2 + e), T.far[:, 2 + e:3 + e], T.pint[:, 5:6], 2.0, -4.0 - 8 * e, op.mult, op.add)
    ts("pint0", "p16i", T.pint[:, 1:2], T.pint[:, 0:1], 15, None, op.bitwise_and)
    ts("pint0", "g16i", T.pint[:, 2:3], T.pint[:, 0:1], 4, None, op.logical_shift_right)
    ts("pint0", "p8i", T.pint[:, 3:4], T.pint[:, 0:1], 7, None, op.bitwise_and)
    cp("pint0 p16i g16i p8i", "pf", T.pf[:, 0:4], T.pint[:, 0:4])
    pf, p16, g16, p8 = T.pf[:, 0:1], T.pf[:, 1:2], T.pf[:, 2:3], T.pf[:, 3:4]
    ts("pf", "ox", T.ox[:, 0:1], p16, float(xo), None, op.add)
    pick(T.u0[:, qa:qa + A], T.u0s[:, qa:qa + A], T.xq[:, 0:128], T.xqs[:, 0:128], T.ox[:, 0:1],
         "xq", "xqs", "qown0", "qown0s", "ox", 16)
    act("pf", "pf4", T.pf[:, 4:5], pf, AF.Identity, bias=128.0, n=1)
    act("pf", "old", T.pf[:, 5:6], p16, AF.Identity, bias=float(KQ * E - 16), n=1)
    ts("pf", "p161", T.pf[:, 6:7], p16, 1.0, None, op.add)
    ts("pf", "side", T.pf[:, 7:8], p16, 8.0, 1.0, op.is_ge, op.add)
    place = (pf, T.pf[:, 4:5])
    act("pf pf4", "npl", T.npl[:, :], T.pf[:, 0:5:4], AF.Identity, scale=-512.0, n=2)
    rm = lambda k: T.rmk[:, k:k + 1]
    ts("jm pf", "rm", T.rmk[:, 0:3], T.jm[:, 0:3], p16, None, op.is_equal)
    ts("rm", "rm3", rm(3), rm(0), 4.0, None, op.mult)
    ts("rm", "rm4", rm(4), rm(1), 8.0, None, op.mult)
    tt("rm3 rm4", "rm5", rm(5), rm(3), rm(4), op.add)
    ts("rm", "rm6", rm(6), rm(2), 2.0, None, op.mult)
    ts("rm", "rm9", rm(9), rm(0), 16.0, rm(1), op.mult, op.add)
    ts("rm rm9", "rm10", rm(10), rm(2), 128.0, rm(9), op.mult, op.add)
    for t in range(2):
        put("lmz%d" % t, T["lm%d" % t][:, 4 * h:4 * h + 4], 0.0, 4)
    put("nlz", T.nl[:, 4 * h:4 * h + 4], 0.0, 4)
    fill("cxz", T.cx[:, 0:16:8], -1e29)
    put("c2", T.c2[:, :], 128.0 * lo + 0.5, 2)
    put("fraz", T.fra[:, 128:144], -1.0, 16)
    put("e8", T.e8[:, :], -1.0, 8)
    put("dv", T.dv[:, :], 0.0, 8)
    act("jm", "odr1", T.odr[:, 1:8], T.jm[:, 1:8], AF.Copy, n=7)
    put("odr0", T.odr[:, 0:1], float(N), 1)
    for nm in ("hc", "hm"):
        act("zz", nm + "z0", T[nm][:, 0:512], T.zz[:, 0:512], AF.Copy, n=512)
    fill("hdz0", T.hd[:, :], 0.0, 276)
    fill("htz", T.ht[:, 512:520], 0.0)
    ts("jm pf", "dg", T.dg[:, 0:8], T.jm[:, 0:8], g16, None, op.is_equal)
    ts("jm pf", "dg16", T.dg[:, 8:16], T.jm[:, 0:8], g16, 0.0625, op.is_equal, op.mult)
    ts("jf pf hdz0", "tri", T.hd[:, 1:512:4], T.jf[:, 0:128], pf, 16.0, op.is_ge, op.mult)
    ts("jf p161", "win1", T.win1[:, :], T.jf[:, 0:32], T.pf[:, 6:7], None, op.is_equal)
    ts("jf side", "win2", T.win2[:, :], T.jf[:, 0:16], T.pf[:, 7:8], -8.0, op.is_equal, op.mult)
    ts("jm pf", "dgm", T.dgm[:, :], T.jm[:, 0:8], g16, 16.0, op.not_equal, op.mult)
    ts("jm pf", "off8", T.off8[:, :], T.jm[:, 0:8], g16, -1e29, op.not_equal, op.mult)
    fill("etz", T.et[:, :], 0.0, 260)
    ts("jf pf etz", "et", T.et[:, 3:515:4], T.jf[:, 0:128], pf, 0.5, op.is_equal, op.mult)
    for b in range(4):
        quant("etz et", "ec%d" % b, T.ec[:, 128 * b:128 * b + 128], T.ecs[:, 128 * b:128 * b + 128], T.et[:, 3 - b:515 - b])
    for c in range(4):
        act("pf", "kb%d" % c, T.kb[:, c:c + 1], p8, AF.Identity, bias=128.0 * (E - (0.5 if c < NS else 0.0) - 8.0 * c) - MID,
            scale=-128.0, n=1)
    for c in range(NS, 4):
        ts("jf kb%d" % c, "jb%d" % c, T.jb[:, 128 * c:128 * c + 128], T.jf[:, 0:128], T.kb[:, c:c + 1], None, op.subtract)
    fill("wz", T.wtile[:, 512:520], 0.0)
    ts("jm pf", "w0a", T.wtile[:, 0:512:4], T.jm[:, :], p16, 16.0, op.is_equal, op.mult)
    ts("jm pf", "w0b", T.wtile[:, 1:512:4], T.jm[:, :], p16, 16.0, op.is_equal, op.mult)
    ts("zz p161", "w1a", T.wtile[:, 2:512:4], T.zz[:, 0:128], T.pf[:, 6:7], None, op.add)
    ts("jf pf", "w2a", T.wtile[:, 3:512:4], T.jf[:, 0:128], pf, None, op.is_equal)
    for i in range(2):
        quant("wz w0a w0b w1a w2a", "wc%d" % i, T.wc[:, 128 * i:128 * i + 128], T.wcs[:, 128 * i:128 * i + 128],
              T.wtile[:, 2 * i:2 * i + 512])
    cp("xt", "hcx", T.hc[:, 512:520], xb)
    cp("xt hdz0", "hdx", T.hd[:, 512:520], xb)
    ts("dg rm10 hdz0", "xta", T.hd[:, 520:552:4], T.dg[:, 0:8], rm(10), None, op.mult)
    quant("wt", "wq wqs", T.wq[:, :], T.wqs[:, :], T.wt[:, :])
    ts("rm rm6 pf", "rm13", rm(13), rm(0), g16, rm(6), op.mult, op.add)
    act("jm rm rm13 tqz", "tbi2", T.tq[:, KQ * E - 16:KQ * E], T.jm[:, 0:16], AF.Identity, bias=rm(13), scale=rm(1), n=16)
    act("c32 rm", "ba", T.ba[:, :], T.c32[:, :], AF.Identity, scale=rm(0), n=32)
    act("r32 rm", "bb", T.bb[:, :], T.r32[:, :], AF.Identity, scale=rm(1), n=32)
    tt("ba bb", "bc0", T.bc[:, 0:32], T.ba[:, :], T.bb[:, :], op.add)
    act("bc0 rm", "bc1", T.bc[:, 32:64], T.bc[:, 0:32], AF.Identity, bias=rm(2), n=32)
    for s in range(N):
        d = (pair[s] - h) % len(grp)
        act("bc0 bc1 rm3 rm4 rm5 tqz", "tbq%d" % s, T.tq[:, s:KQ * E:KQ], T.bc[:, E * (d // 2):E * (d // 2) + E], AF.Identity,
            bias=(0.0, rm(4), rm(3), rm(5))[2 * (d % 2) + upper[s]], n=32)
    TBQ = "tqz tbi2 " + " ".join("tbq%d" % s for s in range(N))

    def W(i):
        return T.wc[:, 128 * i:128 * i + 128], T.wcs[:, 128 * i:128 * i + 128]

    def both(nm):
        return " ".join("%s %ss" % (k, k) for k in nm.split())

    chains = []

    def one_round(t):
        first = len(ops)
        u, us = T["u%d" % t], T["u%ds" % t]
        cd, cds = T["cd%d" % t], T["cd%ds" % t]
        mp, mps = T["mp%d" % t], T["mp%ds" % t]
        lm = T["lm%d" % t]
        q, qs = u[:, QO:QO + 128], us[:, QO:QO + 128]
        Q = both("qown%d qfar%d" % (t, t))
        MEM = "mem%d0 mem%d1" % (t, t)
        MEMS = "mem%d0s mem%d1s" % (t, t)
        for i, e in enumerate((0, 1) if t else (own, 1 - own)):
            mm(e, 128, q, qs, u[:, 128 * e:128 * e + 128], us[:, 128 * e:128 * e + 128], Q + " " + both("mem%d%d" % (t, e)),
               after=("sc%d" % t,) if i else (), tag="sc%d" % t)
            c = 2 * order.index((lo, hi)[e])
            red("#%d lmz%d" % (e, t), "lmo%d%d" % (t, e), lm[:, c:c + 1], bank(e), op.max, n=128)
        OWN = "lmz%d lmo%d0 lmo%d1" % (t, t, t) + (" lmn1" if t else "")
        spread("m%d" % t, OWN, lm[:, 4 * h:4 * h + 4], lambda r: lm[:, 4 * h:4 * h + 4])
        arrive("m%d" % t, from_mates, "lma%d" % t)
        for b in range(4):
            mm(3 + b, 128, T.ec[:, 128 * b:128 * b + 128], T.ecs[:, 128 * b:128 * b + 128], q, qs, "ec%d " % b + Q, True, False,
               after=("sc%d" % t,))
        c = 2 * order.index(lo)
        scan("#0 zz", "cm0", T.cm[:, 0:128], bank(0), T.zz[:, 0:128], -1e29, op.max, op.add, n=128)
        scan("#1 zz lmo%d0" % t, "cm", T.cm[:, 128:256], bank(1), T.zz[:, 0:128], lm[:, c:c + 1], op.max, op.add, n=128)
        a, hi16 = T.aa[:, t:t + 1], T.aa[:, 2 + t:3 + t]
        count("cm cm0", "ah%d" % t, T.cm[:, 15:256:16], AF.Sign, T.cm[:, 255:256], -1.0, hi16, n=16)
        ops[-1]["tag"] = "ah%d" % t
        count("cm cm0", "a%d" % t, T.cm[:, :], AF.Sign, T.cm[:, 255:256], -1.0, a, n=256)
        ops[-1]["after"] = ("ah%d" % t,)
        ts("z8 hmz0 ah%d" % t, "hm0", T.hm[:, 0:32:4], T.z8[:, :], hi16, None, op.add)
        ts("dg16 hmz0 a%d ah%d" % (t, t), "hal", T.hm[:, 1:32:4], T.dg[:, 8:16], a, hi16, op.mult, op.subtract)
        quant("hmz0 hm0 hal hm2 hm3", both("hac"), T.hac[:, :], T.hacs[:, :], T.hm[:, 0:512])
        mm(7, 128, *W(0), T.hac[:, :], T.hacs[:, :], "wc0 " + both("hac"))
        cp("#7", "oaw", T.oaw[:, :], bank(7, 8))
        pick(mp[:, :], mps[:, :], u[:, 0:256], us[:, 0:256], T.oaw[:, 0:8], MEM, MEMS, "mp%d" % t, "mp%ds" % t, "oaw", 128)
        for b in range(4):
            mm(3 + b, 128, T.ec[:, 128 * b:128 * b + 128], T.ecs[:, 128 * b:128 * b + 128], mp[:, :], mps[:, :],
               "ec%d mp%d mp%ds" % (b, t, t), False, True, ("blend",) if b else (), "blend")
        for b in range(4):
            if b % 2 == 0:
                cp("#%d" % (3 + b), "ht%d" % b, T.ht[:, b:512:4], bank(3 + b), n=128)
            else:
                act("#%d" % (3 + b), "ht%d" % b, T.ht[:, b:512:4], bank(3 + b), AF.Copy)
        quant("ht0 ht1 ht2 ht3 htz", "cand%d cand%ds" % (t, t), cd[:, 0:130], cds[:, 0:130], T.ht[:, :], 130)
        gather("S", "oaw jf jf2", "fra", T.fra[:, 0:128], T.jf[:, :], T.oaw[:, 0:8], 128)
        nt, nk = ((T.lm1, "lmn1"), (T.nl, "nlo"))[t]
        if hi - lo > 1:
            ts("a%d" % t, "nm0", T.nm[:, 0:1], a, 128.0, 128.0 * (hi - 1 - lo), op.is_ge, op.mult)
            ts("nm0 a%d c2 lmz1 nlz" % t, nk, nt[:, 4 * h + 1:4 * h + 4:2], T.c2[:, :], a, T.nm[:, 0:1], op.add, op.add)
        else:
            ts("a%d c2 lmz1 nlz" % t, nk, nt[:, 4 * h + 1:4 * h + 4:2], T.c2[:, :], a, None, op.add)
        if t == 1:
            spread("nn", "nlo nlz", T.nl[:, 4 * h:4 * h + 4], lambda r: T.nl[:, 4 * h:4 * h + 4])
            arrive("nn", from_mates, "nla")
        m, half, step = T.cm[:, 255:256], T.hf[:, 0:1], T.hf[:, 1:2]
        cl, ch = 2 * order.index(lo), 2 * order.index(hi)
        ts("off8 cm", "mrep", T.mrep[:, :], T.off8[:, :], m, None, op.add)
        ts("lmo%d0 lmo%d1" % (t, t), "half", half, lm[:, ch:ch + 1], lm[:, cl:cl + 1], 1.0, op.is_gt, op.add)
        if hi - lo > 1:
            act("cm", "step", step, m, AF.Abs, bias=TINY, scale=STEP, n=1)
            ts("half step dv", "dv", T.dv[:, N - 1:N], half, -1.0, step, op.add, op.mult)
            z0 = 2
        else:
            act("cm dv", "step", T.dv[:, lo:lo + 1], m, AF.Abs, bias=TINY, scale=STEP, n=1)
            ts("step dv", "dv", T.dv[:, 0:1], T.dv[:, lo:lo + 1], -1.0, None, op.mult)
            z0 = 0
        LM = OWN + " lma%d" % t
        scan(LM + " step dv", "zs", T.zs[:, z0:N], lm[:, 2 * z0:16:2], T.dv[:, z0:N], -1e29, op.max, op.add)
        ts("mrep zs half", "oc8", T.oc8[:, :], T.mrep[:, :], T.zs[:, N - 1:N], half, op.is_ge, op.mult)
        gather("V", "oc8 hcz0 win2", "hcg", T.hc[:, 0:256:4], T.win2[:, :], T.oc8[:, 0:4], 64)
        gather("S", "oc8 hcz0 win2", "hcg2", T.hc[:, 256:512:4], T.win2[:, :], T.oc8[:, 4:8], 64)
        quant("hcg hcg2 hcz0 hcx", both("hcc"), T.hcc[:, 0:130], T.hccs[:, 0:130], T.hc[:, :], 130)
        mm(0, 130, *W(0), T.hcc[:, 0:130], T.hccs[:, 0:130], "wc0 " + both("hcc"))
        scan("#0 zz", "pc", T.pc[:, :], bank(0), T.zz[:, 0:128], MID, op.add, op.add, n=128)
        for c in range(NS):
            count("pc kb%d" % c, "acc%d" % c, T.pc[:, :], AF.Sign, T.kb[:, c:c + 1], 1.0, T.acc[:, c:c + 1])
        for c in range(NS, 4):
            fs = T.fs[:, 128 * c:128 * c + 128]
            scan("pc jb%d" % c, "fs%d" % c, fs, T.jb[:, 128 * c:128 * c + 128], T.pc[:, :], 4096.0, op.min, op.max, n=64)
            ts("fs%d kb%d" % (c, c), "osl%d" % c, T.oslot[:, c:c + 1], T.fs[:, 128 * c + 127:128 * c + 128],
               T.kb[:, c:c + 1], 128.0, op.add, op.min)
        if NS:
            ts(" ".join("acc%d" % c for c in range(NS)), "osl0", T.oslot[:, 0:NS], T.acc[:, 0:NS], 0.5, 64.0, op.mult, op.add)
        OS = "osl0 osl1 osl2 osl3"
        pick(u[:, SO:SO + 64], us[:, SO:SO + 64], cd[:, 0:130], cds[:, 0:130], T.oslot[:, 0:4],
             "cand%d" % t, "cand%ds" % t, "slot%d" % t, "slot%ds" % t, OS, 64)
        cx, w1 = T.cx[:, 8 * t:8 * t + 8], T.w1[:, t:t + 1]
        scan(LM + " zz cxz", "cx%d" % t, T.cx[:, 8 * t + 1:8 * t + 8], lm[:, 2:16:2], T.zz[:, 0:7], -1e29, op.max, op.add)
        top, w0, f7 = T.cx[:, 8 * t + 7:8 * t + 8], T.mx[:, t:t + 1], T.mx[:, 2 + t:3 + t]
        count("cxz cx%d" % t, "w0%d" % t, cx, AF.Sign, top, -1.0, w0, n=8)
        ts(LM + " cx%d" % t, "f7%d" % t, f7, lm[:, 0:1], top, float(N), op.is_gt, op.mult)
        ts("dgm w0%d f7%d" % (t, t), "od8", T.od8[:, :], T.dgm[:, :], w0, f7, op.add, op.max)
        tt("w0%d f7%d" % (t, t), "w1%d" % t, w1, w0, f7, op.max)
        gather("S", "od8 hdz0 win1", "hdg", T.hd[:, 0:512:4], T.win1[:, :], T.od8[:, 0:8], 128)
        quant("hdg hdz0 hdx tri xta", both("hdc"), T.hdc[:, 0:138], T.hdcs[:, 0:138], T.hd[:, :], 138)
        mm(1, 130, *W(1), T.hdc[:, 0:130], T.hdcs[:, 0:130], "wc1 " + both("hdc"), after=("blend",))
        at = lambda r: SO + 64 * ((h - pair[r]) % len(grp))
        spread("c%d" % t, "slot%d" % t, u[:, SO:SO + 64].bitcast(dt.uint8), lambda r: u[:, at(r):at(r) + 64].bitcast(dt.uint8),
               tag="cc%d" % t)
        spread("c%d" % t, "slot%ds" % t, us[:, SO:SO + 64], lambda r: us[:, at(r):at(r) + 64], after=("cc%d" % t,))
        arrive("c%d" % t, 2 * from_mates, "land%d land%ds" % (t, t))
        halves = (0, 1) if t == 0 else (own,)
        for i, e in enumerate(halves):
            ne, sm, sh = T.ne[:, 64 * i:64 * i + 64], T["sm%d" % i], T["sh%d" % i]
            won = T.fra[:, 0:144].indirect(T.oslot[:, 0:4])
            if i:
                do("S", "fra fraz npl " + OS, "ne%d" % i,
                   lambda ne=ne, e=e, won=won: S.activation(ne, won, AF.Abs, bias=T.npl[:, e:e + 1], scale=512.0), 0.17)
            else:
                do("V", "fra fraz pf pf4 " + OS, "ne%d" % i,
                   lambda ne=ne, e=e, won=won: V.tensor_scalar(ne, won, place[e], 512.0, op.not_equal, op.mult), 0.15)
            scan("ne%d one far%d" % (i, e), "sm%d" % i, sm[:, :], T.one[:, 0:64], ne, T.far[:, e:e + 1], op.add, op.min)
            scan("ne%d inc0 inc far%d" % (i, 2 + e), "sh%d" % i, sh[:, :], T.one[:, 64:128], ne, T.far[:, 2 + e:3 + e], op.add, op.min)
            act("sh%d z8 hmz0" % i, ("ma0 hm0", "ma1 hm2")[i], T.hm[:, 32 * i:32 * i + 32:4], T.z8[:, :], AF.Identity,
                bias=sh[:, 63:64], n=8)
            ts("sm%d sh%d dg16 hmz0" % (i, i), ("mb0 hal", "mb1 hm3")[i], T.hm[:, 32 * i + 1:32 * i + 32:4], T.dg[:, 8:16],
               sm[:, 63:64], sh[:, 63:64], op.mult, op.subtract)
        quant("hm0 hmz0 hal hm2 hm3", both("hmc"), T.hmc[:, :], T.hmcs[:, :], T.hm[:, :])
        mm(2, 128, *W(0), T.hmc[:, :], T.hmcs[:, :], "wc0 " + both("hmc"))
        ts("#2", "lmem", T.lmem[:, :], bank(2, 16), -1.0, SO + 63.0, op.mult, op.add)
        cn = T.cn[:, t:t + 1]
        act("e8 w1%d" % t, "b8", T.b8[:, :], T.e8[:, :], AF.Identity, bias=w1, n=8)
        ts("#1 w1%d" % t, "eqt", T.eqt[:, :], bank(1), w1, float(KQ), op.is_equal, op.mult, n=128)
        red("eqt", "cn%d" % t, cn, T.eqt[:, :], op.add, n=128)
        ts("b8 cn%d old" % t, "oq", T.oq[:, :], T.b8[:, :], cn, T.pf[:, 5:6], op.add, op.min)
        gather("S", "oq hcz0 " + TBQ, "hcg hcg2", T.hc[:, 0:512:4], T.tq[:, :], T.oq[:, 0:8], 128)
        quant("hcg hcg2 hcz0", both("hqc"), T.hqc[:, :], T.hqcs[:, :], T.hc[:, 0:512])
        mm(7, 128, T.hqc[:, :], T.hqcs[:, :], T.hdc[:, 10:138], T.hdcs[:, 10:138], both("hdc hqc"))
        cp("#7", "lq", T.lq[:, :], T.ps[:, 512 * 7 + 120:512 * 7 + 128])
        ts("odr0 odr1 w1%d slot%d" % (t, t), "oh%d" % t, T.oh[:, 8 * t:8 * t + 8], T.odr[:, :], w1, None, op.is_equal)
        act("cn%d" % t, "ws%d" % t, T.wv[:, t:t + 1], cn, AF.Sign, bias=KQ * (E - 0.5), scale=-1.0, n=1)
        made_by = {o["w"][0]: i for i, o in reversed(list(enumerate(ops))) if i >= first and o["w"]}
        made_by.update({k: i for i, o in enumerate(ops[:first]) for k in o["w"][:1] if k in LATE[t].split()})
        for names in GIVEN:
            names = names.replace("@", str(t)).split()
            chains.append([made_by[k] for k in names if k in made_by])
        NEW = "slot%d land%d qown%d qfar%d" % (t, t, t, t)
        NEWS = "slot%ds land%ds qown%ds qfar%ds" % (t, t, t, t)
        if t == 0:
            pick(T.u1[:, 0:SO], T.u1s[:, 0:SO], u[:, 0:SO + 64], us[:, 0:SO + 64], T.lmem[:, :],
                 MEM + " slot0", MEMS + " slot0s", "mem10 mem11", "mem10s mem11s", "lmem", SO)
            pick(T.u1[:, QO:QO + 128], T.u1s[:, QO:QO + 128], u[:, SO:QO + 128], us[:, SO:QO + 128], T.lq[:, 0:8],
                 NEW, NEWS, "qown1 qfar1", "qown1s qfar1s", "lq", 128)
        else:
            pick(T.fm[:, :], T.fms[:, :], u[:, 0:SO + 64], us[:, 0:SO + 64], T.lmem[:, 0:8],
                 MEM + " slot1", MEMS + " slot1s", "fm", "fms", "lmem", 128)
            dma("Y", "o0", "fm land1s", "out0", T.oc[:, :], T.fm[:, :].bitcast(dt.uint8))
            for k in range(4):
                dma("Y", "o%d" % (1 + k), "fms land1s", "out%d" % (1 + k), T.osc[4 * k:4 * k + 4, :], T.fms[32 * k:32 * k + 4, :])
            pick(T.qf[:, :], T.qfs[:, :], u[:, SO:QO + 128], us[:, SO:QO + 128], T.lq[:, 0:8], NEW, NEWS, "qf", "qfs", "lq", 128)

    one_round(0)
    one_round(1)
    mm(3, 128, T.wq[:, :], T.wqs[:, :], T.qf[:, :], T.qfs[:, :], "wq wqs qf qfs")
    cp("#3", "ysb", T.ysb[:, :], bank(3), n=128)
    dma("S", "o7", "ysb", "outy", T.y[:, :], T.ysb[:, :])
    for t, nt, nk in ((0, T.lm1, "lmn1 lmz1 lma1"), (1, T.nl, "nlo nlz nla")):
        tt("oh%d slot1 %s" % (t, nk), "og%d" % t, T.og[:, 8 * t:8 * t + 8], T.oh[:, 8 * t:8 * t + 8], nt[:, 1:16:2], op.mult)
        act("og%d ws%d" % (t, t), "wo%d oh%d" % (t, t), T.oh[:, 8 * t:8 * t + 8], T.og[:, 8 * t:8 * t + 8], AF.Identity,
            -0.5 / N, T.wv[:, t:t + 1], T.wo[:, t:t + 1], n=8)
        dma("Y", "o%d" % (5 + t), "wo%d land1s" % t, "out%d" % (5 + t), T.wi[t:t + 1, :], T.wo[:, t:t + 1])

    cnt, known = {}, {q: {} for q in queue}
    wr, rd = {}, {}
    for o in in_order(ops, chains):
        q = o["q"]
        if o["call"] is None:
            cnt[o["sem"]] = o["inc"]
            note((o["sem"], o["inc"], "far", {}), [], o["w"], wr, rd)
            continue
        deps = conflicts(q, o["r"], o["w"], wr, rd, o["acc"], False)
        want = {}
        for e in deps:
            if known[q].get(e[0], 0) < e[1]:
                want[e[0]] = max(want.get(e[0], 0), e[1])
        for e in deps:
            for s, v in e[3].items():
                if s in want and e[0] != s and want[s] <= v:
                    del want[s]
        for s, v in want.items():
            queue[q].wait_ge(T.sem[s], v)
            known[q][s] = v
        for e in deps:
            for s, v in e[3].items():
                if known[q].get(s, 0) < v:
                    known[q][s] = v
        made = o["call"]()
        if o["sem"]:
            made.then_inc(T.sem[o["sem"]], o["inc"])
            cnt[o["sem"]] = cnt.get(o["sem"], 0) + o["inc"]
            note((o["sem"], cnt[o["sem"]], q if o["sem"] == q else "dma", dict(known[q])), o["r"], o["w"], wr, rd)
    g.wait_ge(T.sem.ls, ls[0])
    for s, n in cnt.items():
        if known["G"].get(s, 0) < n:
            g.wait_ge(T.sem[s], n)
